import numpy as np, ml_dtypes
CORES = [9,25,41,57]
N = 4
BF = ml_dtypes.bfloat16
W, TU, RO, Q, S = 8192, 256, 5, 9, 32
HOPS = [1]
BL = TU // len(HOPS)
def pack(x, l, w, k, h):
    return {"field": x.reshape(N, 128, W).astype(np.float32).astype(BF), "tube": np.ascontiguousarray(l.reshape(N, 128, TU)).astype(np.int32),
            "wt": w.reshape(N, 128, 1).astype(np.int32), "kn": k.reshape(N, 128, 1).astype(np.int32), "lim": np.ascontiguousarray(h.reshape(N, 128, RO)).astype(np.int32)}
def parts(rng):
    dark = rng.random((N, 8, 1, W)) < rng.choice(np.array([0.04, 0.08, 0.15]), (N, 8, 1, 1))
    x = np.where(dark, rng.integers(0, 64, (N, 8, 16, W), dtype=np.int16), rng.integers(48, 256, (N, 8, 16, W), dtype=np.int16))
    l = rng.integers(0, W, (N, 8, 16, TU)); w = rng.integers(0, 256, (N, 8, 16)); k = rng.integers(0, 256, (N, 8, 16))
    return x, l, w, k, rng.integers(16, 72, (N, 8, 16, RO))
def setup_inputs(rng):
    return pack(*parts(rng))
def setup_inputs_spread(rng):
    sh = rng.choice(np.array([0, 0, 0, 0, 0, 1, 1, 2, 4, 8], np.int16), (N, 8, 1, W))
    x = rng.integers(0, 256, (N, 8, 16, W), dtype=np.int16) >> sh
    l = rng.integers(0, W, (N, 8, 16, TU)); l[:, 1::2] = np.minimum((W * rng.random((N, 4, 16, TU)) ** 3).astype(np.int64), W - 1)
    w = rng.integers(0, 256, (N, 8, 16)) >> rng.integers(0, 9, (N, 8, 16)); k = rng.integers(0, 256, (N, 8, 16)) >> rng.integers(0, 9, (N, 8, 16))
    h = rng.integers(0, 249, (N, 8, 16, RO)) >> rng.integers(0, 9, (N, 8, 1, RO))
    return pack(x, l, w, k, h)
def ends_of(rng, hi, shape):
    return np.where(rng.random(shape) < 0.14, rng.integers(0, hi + 1, shape), hi * rng.integers(0, 2, shape))
def setup_inputs_ends(rng):
    kind = rng.random((N, 8, 1, W)); top = np.int16(255)
    x = np.where(kind < 0.7, top, np.where(kind < 0.82, np.int16(0), top * rng.integers(0, 2, (N, 8, 16, W), dtype=np.int16)))
    i = np.arange(16)[:, None]
    b = ((np.arange(N)[:, None] + np.arange(8)[None, :]) & 1) * (W - 1)
    l = np.where(i < rng.integers(0, 17, (N, 8, 1, TU)), b[:, :, None, None], (W - 1) * rng.integers(0, 2, (N, 8, 16, TU)))
    free = ((np.arange(TU) * 5) & 15) < 5; l[..., free] = rng.integers(0, W, (N, 8, 16, int(np.count_nonzero(free))))
    w = ends_of(rng, 255, (N, 8, 16)); k = ends_of(rng, 255, (N, 8, 16))
    h = 248 * rng.integers(0, 2, (N, 8, 16, RO)); h[:, 1::2] = 248 * rng.integers(0, 2, (N, 4, 1, RO))
    for q in range(N):
        for g in range(8):
            o = W - 1 - b[q, g]; x[q, g][:, b[q, g]] = 255
            x[q, g][:, o] = 0 if (g & 3) < 2 or q == 1 else 255 * rng.integers(0, 2, 16) if (g & 3) == 2 else 255
    h[0, :, :, 0] = 0; h[0, 0, :, 1] = 248; h[1, :, :, 0] = 248; h[1, 0, :, 1] = 0; l[1, :, 15, :] = (W - 1 - b[1])[:, None]
    h[2, :, :, 0] = 0; h[2, 0, :, 0] = 248; l[2, 0] = b[2, 0]; l[2, 0, 15, :7] = W - 1 - b[2, 0]; h[2, :, :, 1] = 248
    p = N - 1; u = (15 * 65025) & 4095
    for g in range(4, 8):
        x[p, g][:, 0] = 255; x[p, g][:, W - 1] = 255; w[p, g] = 255
        if g == 5: w[p, g] = 0; w[p, g, 0] = 16; w[p, g, 1] = 1; x[p, g, 1, 0] = 15; x[p, g, 1, W - 1] = 15
        if g > 5:
            w[p, g, 0] = 0; k[p, g] = 255 * (np.arange(16) & 1)
            for j in (0, W - 1):
                x[p, g][:, ((u * u >> 4) + j) & (W - 1)] = 0
                x[p, g][:, ((u * u >> 4) + 255 * u + j) & (W - 1)] = 255 if g == 6 else 0
    return pack(x, l, w, k, h)
def setup_inputs_corners(rng):
    x, l, w, k, h = parts(rng); i = np.arange(16)[:, None]; v = np.arange(TU)
    for q in range(N):
        for g in range(8):
            c = (g + q) & 7
            if c == 0: h[q, g] = 0
            if c == 1: h[q, g] = 248; x[q, g] = np.minimum(x[q, g], 247)
            if c == 2:
                s = rng.integers(0, W, TU); s[0] = 0; s[1] = W - 1; l[q, g] = s[None, :]
            if c == 3:
                m = np.where(rng.random(W) < 0.9, Q, Q - 1)[None, :]
                x[q, g] = np.where(i < m, rng.integers(150, 256, (16, W)), rng.integers(0, 90, (16, W))); h[q, g] = 100
            if c == 4: w[q, g] = 0; k[q, g] = 0
            if c == 5:
                m = rng.random(W) < 0.9; x[q, g, 0, m] = 255; x[q, g, 1, m] = 15; w[q, g] = 0; w[q, g, 0] = 16; w[q, g, 1] = 1; k[q, g] = 255 * rng.integers(0, 2, 16)
            if c == 6:
                t = rng.integers(0, 4, (16, TU)); l[q, g] = np.where(t == 0, 0, np.where(t == 1, W - 1, np.where(t == 2, S * v, S * v + S - 1)))
            if c == 7:
                x[q, g][:, 0::2] = rng.integers(200, 256, (16, W // 2)); x[q, g][:, 1::2] = rng.integers(0, 64, (16, W // 2)); h[q, g] = 100
                l[q, g] = 2 * rng.integers(0, W // 2, (16, TU)) + (i == (v % 17)[None, :])
    return pack(x, l, w, k, h)
def setup_inputs_ties(rng):
    x, l, w, k, h = parts(rng)
    pr = 60 + 4 * rng.integers(0, 3, (N, 8, 16, 5)); x = np.take_along_axis(pr, np.broadcast_to(rng.integers(0, 5, (N, 8, 1, W)), (N, 8, 16, W)), 3)
    return pack(x, l, w, k, rng.integers(53, 66, (N, 8, 16, RO)))
def setup_inputs_brink(rng):
    x, l, w, k, h = parts(rng); r0 = int(rng.integers(0, 8)); v = np.arange(TU)
    h[..., 0] = 0; h[..., 1] = 248; h[..., 2:] = rng.integers(246, 249, (N, 8, 1, RO - 2))
    for g in range(8):
        c = (g + r0) & 7; low = rng.permutation(W)[:32]
        for q in range(N):
            if c < 4:
                o = rng.permutation(16); y = np.full((16, W), 254); y[o[:Q]] = 255
                b = np.nonzero(rng.random(W) < 0.1)[0]; y[o[rng.integers(0, Q, len(b))], b] = 254
                x[q, g] = y
            elif c < 6:
                x[q, g] = rng.integers(248, 256, (16, W)); x[q, g][:, low] = rng.integers(7, 9, (16, 32))
            else:
                x[q, g] = rng.integers(243, 256, (16, W)); x[q, g][:, low] = rng.integers(0, 4, (16, 32))
            if c >= 4:
                l[q, g, rng.integers(1, 16, TU), v] = low[rng.integers(0, 32, TU)]; h[q, g] = 0
            if c == 0:
                d = int(rng.integers(0, W)); s = rng.integers(0, W - 1, (16, TU)); l[q, g] = s + (s >= d)
                l[q, g, rng.integers(1, 16, 7), rng.permutation(TU)[:7]] = d
                x[q, g][:, d] = rng.integers(0, 248, 16); h[q, g, :, 0] = 248
    return pack(x, l, w, k, h)
def check_inputs(d):
    bad = []
    for a, lo, hi in (("field", 0, 255), ("tube", 0, W - 1), ("wt", 0, 255), ("kn", 0, 255), ("lim", 0, 248)):
        v = np.asarray(d[a]).astype(np.float64)
        if not (np.min(v) >= lo and np.max(v) <= hi): bad.append("range of " + a)
        elif np.any(v != np.floor(v)): bad.append("whole numbers of " + a)
    return bad
def reference(field, tube, wt, kn, lim):
    x = field.astype(np.float32).astype(np.int32).reshape(N, 8, 16, W)
    l = tube.astype(np.int64).reshape(N, 8, 16, TU)
    w = wt.astype(np.int64).reshape(N, 8, 16, 1); k = kn.astype(np.int64).reshape(N, 8, 16, 1); h = lim.astype(np.int64).reshape(N, 8, 16, RO)
    cut = [0] * N; v = np.arange(TU); j = np.arange(16)[:, None]
    for rnd in range(RO):
        if rnd: l = np.concatenate([np.roll(l[..., b * BL:(b + 1) * BL], HOPS[b], axis=0) for b in range(len(HOPS))], axis=-1)
        nl = np.zeros((N, 8, 16, TU), np.int64); nz = np.zeros((N, 8, 16, TU), np.int64); ncut = [0] * N
        for q in range(N):
            for g in range(8):
                X, L = x[q, g], l[q, g]
                M = np.minimum.accumulate(X[:, L], axis=1)
                holds = (M >= (h[q, g, :, rnd] + (cut[q] & 7))[:, None, None]).astype(np.int64)
                ok = (np.add.reduce(holds, axis=0) >= Q).astype(np.int64)
                m = np.maximum(np.add.reduce(ok, axis=0), 1) - 1
                Z = np.take_along_axis(M, np.broadcast_to(m[None, None, :], (16, 1, TU)), 1)[:, 0].astype(np.int64)
                u = np.add.reduce(w[q, g] * X[:, L[m, v]], axis=0) & 4095
                c = ((u * u >> 4)[None, :] + k[q, g] * u[None, :] + L) & (W - 1)
                s = np.add.reduce(np.abs(X[:, c] - Z[:, None, :]), axis=0)
                best = c[np.argmin(s, axis=0), v]
                back = L[np.clip(m[None, :] + 1 - j, 0, 15), v[None, :]]
                nl[q, g] = np.where(j == 0, best[None, :], np.where(j <= m[None, :], back, c)); nz[q, g] = Z
                y = (Z + X[:, best]) >> 1
                x[q, g][:, S * v + (u & (S - 1))] = y
                ncut[q] += int(np.count_nonzero(m < 15))
        l = nl; cut = ncut
    return {"yl": l.reshape(N, 128, TU).astype(np.float32), "yz": nz.reshape(N, 128, TU).astype(np.float32)}

@@ -1,0 +1,524 @@
+from concourse.mybir import AluOpType, AxisListType, ActivationFunctionType
+
+RO = 5
+CHUNKS = [(0, 128, [(0, 32), (32, 32), (64, 32), (96, 32)]), (128, 128, [(0, 32), (32, 32), (64, 32), (96, 32)])]
+UNIT = 64
+
+BF, F32, I32, U16 = "bfloat16", "float32", "int32", "uint16"
+SCRATCH = {"DL0": ("dram", [8, 16, 128], F32), "DL1": ("dram", [8, 16, 128], F32), "irow": ("sbuf", [1, 128], BF), "grow": ("sbuf", [1, 128], BF), "c64": ("sbuf", [64, 128], BF)}
+for _n, _w, _d in (
+        ("X", 8192, BF), ("TI", 256, I32), ("wi", 1, I32), ("ki", 1, I32), ("li", 8, I32),
+        ("wc", 1, F32), ("kc", 1, F32), ("nl", 8, F32), ("lf", 8, F32), ("k2", 1, F32), ("k3", 1, F32), ("k4", 1, F32), ("sqb", 1, F32),
+        ("pI", 1, I32), ("iI", 1, I32), ("icol", 1, F32), ("i16", 1, F32), ("i32c", 1, F32),
+        ("pthr", 1, F32), ("pthv", 1, F32), ("ige1", 1, F32), ("e15", 1, F32),
+        ("ones", 128, BF), ("BO1", 128, BF), ("BO", 128, BF), ("IB", 128, BF), ("IF", 128, F32),
+        ("pIm", 128, BF), ("nIm", 128, BF), ("BOd", 128, BF), ("OHm", 128, BF), ("BOf", 128, F32), ("BOf256", 128, F32),
+        ("UA", 256, F32), ("UO", 256, F32),
+        ("S15", 128, BF), ("Sel0", 128, F32), ("LQ", 256, F32),
+        ("sel", 2048, BF), ("isel", 2048, BF), ("wsel", 2048, BF), ("sel128", 2048, BF), ("blk32", 8, BF), ("blk16", 8, BF), ("blkn", 8, BF),
+        ("v1i", 8, I32), ("v2i", 16, I32), ("v3i", 16, I32), ("VB", 8, BF), ("VW", 16, BF), ("SOp", 16, I32),
+        ("R01", 1024, BF), ("RB", 1024, BF), ("RK", 128, BF), ("half", 128, BF), ("W", 4096, F32),
+        ("soA", 16, I32), ("soB", 16, I32), ("soC", 16, I32), ("SO", 16, U16),
+        ("er", 1, F32), ("eI", 1, I32), ("eJ", 1, I32), ("nth", 8, F32), ("thv", 8, F32),
+        ("ZS", 4096, BF), ("G", 4096, BF), ("M", 4096, BF), ("H", 4096, BF), ("Zx", 4096, BF), ("D", 4096, BF), ("A", 4096, BF),
+        ("pas", 256, BF), ("OM", 16, U16), ("OW", 16, U16), ("OT", 16, U16), ("XL", 256, BF), ("Z2", 256, F32), ("B4", 256, BF),
+        ("SQ", 256, F32), ("xI", 256, I32), ("cI", 256, I32), ("CU", 256, U16), ("L32", 256, F32), ("OHA", 256, BF), ("sv", 256, BF),
+        ("OC", 256, F32), ("C1", 256, F32), ("R1", 256, F32), ("tt", 256, F32), ("Y2", 256, BF), ("yls", 256, F32), ("yzs", 256, F32)):
+    SCRATCH[_n] = ("sbuf", [128, _w], _d)
+for _c in range(2):
+    SCRATCH["KM%d" % _c] = ("sbuf", [128, 144], F32)
+    SCRATCH["KB%d" % _c] = ("sbuf", [128, 128], F32)
+    SCRATCH["OH%d" % _c] = ("sbuf", [128, 128], BF)
+    for _b in ("pb%d0", "pb%d1", "pb%d2", "pk%d"):
+        SCRATCH[_b % _c] = ("psum", [128, 512], F32)
+for _t in range(RO):
+    SCRATCH["LU%d" % _t] = ("sbuf", [128, 256], U16)
+    if _t < RO - 1:
+        SCRATCH["NU%d" % _t] = ("sbuf", [128, 256], U16)
+
+SEMAPHORES = ["cv", "cs", "ct", "cg", "sent", "ldt", "ldw", "ldk", "ldl", "ldx", "ldy"] + \
+    ["%s%d" % (a, c) for a in ("oz", "ol", "dl", "w") for c in range(len(CHUNKS))] + ["arr%d%d" % (t, c) for t in range(1, RO) for c in range(len(CHUNKS))]
+
+P = {"cyc": 0.92e-3, "ga": 1.56, "pec": 0.5e-3, "wake": 0.18, "hop": 5.0, "wdma": 7.0}
+PLACE = {}
+PRI = {}
+SIDES = "svssssssssvvvsvsvvssssssssvsvsssvvvvsvsvss"
+RANKS = """-1390 632 827 506 664 -870 -414 -646 440 822 -405 -395 632 -47 -2068 636 463 123 405 -1113 -586 100 256 947 447 2980 1247 -506 31 1199 231 -8 -277 803 223 -1047 -101 74 -971 -1330 -737 388 -75 716 327 513 1140 928 -1274 788 -1515 841 -727 402 1381 91 -1261 211 292 -469 -306 1419 -9 201 452 134 -287 -751 -781 1073 487 -452 33 -412 -1111 -1018 446 375 69 -641 1299 -481 173 307 -788 -491 -449 -727 -588 -1520 611 -1265 191 245 171 -939 -359 1543 248 -402 -2744 -408 -2445 -364 -490 -1360 922 -269 -517 -407 1066 108 1707 -343 290 430 -538 1058 635 549 -1249 -767 -333 255 -632 493 -561 -206 -691 652 255 36 914 -1112 -605 549 265 -381 908 -512 -601 599 741 -279 595 -581 728 -170 -897 -717 7 1542 -457 -745 804 -4 288 1004 -108 -55 -385 -319 -508 951 -592 252 -161 -519 1418 1071 1230 244 46 -1237 2 -204"""
+
+
+def side(key):
+    return PLACE.get(key, "s")
+
+
+def build():
+    O, AF = AluOpType, ActivationFunctionType
+    ops = []
+    cyc, pec = P["cyc"], P["pec"]
+
+    def v1(n): return max(64, n) * cyc
+    def vh(n): return max(64, n / 2) * cyc
+    def vg(n): return 0.055 + n * P["ga"] * cyc
+    def sg(n): return 0.07 + n * P["ga"] * cyc
+    tiny = v1(1)
+
+    def add(eng, cost, reads, writes, fn, name="", sem=None, n=1):
+        ops.append({"eng": eng, "cost": cost, "reads": reads, "writes": writes, "fn": fn, "name": name, "sem": sem, "n": n, "id": len(ops)})
+
+    def V(cost, reads, writes, fn, name=""): add("v", cost, reads, writes, fn, name)
+    def S(cost, reads, writes, fn, name=""): add("s", cost, reads, writes, fn, name)
+    def PE(cyc_n, reads, writes, fn, n, name=""): add("t", cyc_n * pec, reads, writes, fn, name, n=n)
+    def r(b, lo=0, hi=100000): return (b, lo, hi)
+
+    def ap(a):
+        if isinstance(a, (int, float)):
+            return lambda T: a
+        if isinstance(a, str):
+            return lambda T: T[a][:]
+        if len(a) == 3:
+            return lambda T: T[a[0]][:, a[1]:a[2]]
+        return lambda T: T[a[0]][:, a[1]:a[2]:a[3]]
+
+    def copy(out, in_): return lambda q, T: [q.tensor_copy(ap(out)(T), ap(in_)(T))]
+    def fill(out, x): return lambda q, T: [q.memset(ap(out)(T), x)]
+    def tt(out, a, b, op): return lambda q, T: [q.tensor_tensor(ap(out)(T), ap(a)(T), ap(b)(T), op)]
+    def scan(out, a, b, o0, o1): return lambda q, T: [q.tensor_tensor_scan(ap(out)(T), ap(a)(T), ap(b)(T), 0.0, o0, o1)]
+    def act(out, in_, f, **kw): return lambda q, T: [q.activation(ap(out)(T), ap(in_)(T), f, **dict((k, ap(x)(T)) for k, x in kw.items()))]
+
+    def ts(out, in0, s1, o1, s2=None, o2=None):
+        if o2 is None:
+            return lambda q, T: [q.tensor_scalar(ap(out)(T), ap(in0)(T), ap(s1)(T), None, o1)]
+        return lambda q, T: [q.tensor_scalar(ap(out)(T), ap(in0)(T), ap(s1)(T), ap(s2)(T), o1, o2)]
+
+    def gcopy(q_v, out, win, off):
+        if q_v:
+            return lambda q, T: [q.tensor_copy(ap(out)(T), ap(win)(T).indirect(ap(off)(T)))]
+        return lambda q, T: [q.activation(ap(out)(T), ap(win)(T).indirect(ap(off)(T)), AF.Copy)]
+
+    def gtt(out, win, off, b, op): return lambda q, T: [q.tensor_tensor(ap(out)(T), ap(win)(T).indirect(ap(off)(T)), ap(b)(T), op)]
+    def mm(out, terms): return lambda q, T: [q.matmul(ap(out)(T), ap(a)(T), ap(b)(T), i == 0, i == len(terms) - 1) for i, (a, b) in enumerate(terms)]
+
+    def either(key, nv, ns, reads, writes, fv, fs, name):
+        if side(key) == "v":
+            V(nv, reads, writes, fv, name)
+        else:
+            S(ns, reads, writes, fs, name)
+
+    def dma(eng, cost, reads, writes, sem, fn, k=1): add(eng, cost, reads, writes, fn, sem, sem=sem, n=k)
+    dma("y", 2.0, [], [r("TI")], "ldt", lambda q, T: [q.dma_start(T.TI[:], T.tube[:])])
+    dma("y", 2.0, [], [r("wi")], "ldw", lambda q, T: [q.dma_start(T.wi[:], T.wt[:])])
+    dma("y", 2.0, [], [r("ki")], "ldk", lambda q, T: [q.dma_start(T.ki[:], T.kn[:])])
+    dma("y", 2.0, [], [r("li")], "ldl", lambda q, T: [q.dma_start(T.li[:, 0:5], T.lim[:])])
+    dma("y", 9.0, [], [r("X", 0, 4096)], "ldx", lambda q, T: [q.dma_start(T.X[:, 0:4096], T.field[:, 0:4096])])
+    dma("s", 9.0, [], [r("X", 4096, 8192)], "ldy", lambda q, T: [q.dma_start(T.X[:, 4096:8192], T.field[:, 4096:8192])])
+    def G(cost, reads, writes, fn): add("g", cost, reads, writes, fn)
+    V(v1(64), [], [r("ones")], fill("ones", 1.0))
+    G(0.4, [], [r("pI")], lambda q, T: [q.iota(T.pI[:], [[0, 1]], 0, 1)])
+    G(0.4, [], [r("v1i")], lambda q, T: [q.iota(T.v1i[:], [[256, 8]], 0, 0)])
+    G(0.4, [], [r("v2i")], lambda q, T: [q.iota(T.v2i[:], [[0, 2], [16, 8]], -128, 0)])
+    G(0.4, [], [r("v3i")], lambda q, T: [q.iota(T.v3i[:], [[512, 16]], 0, 0)])
+    G(0.6, [], [r("irow")], lambda q, T: [q.iota(T.irow[:], [[0, 8], [1, 16]], 0, 0, allow_small_or_imprecise_dtypes=True)])
+    G(0.6, [], [r("grow")], lambda q, T: [q.iota(T.grow[:], [[16384, 8], [0, 16]], 0, 0, allow_small_or_imprecise_dtypes=True)])
+    V(tiny, [r("grow")], [r("grow")], lambda q, T: [q.tensor_scalar(T.grow[:], T.grow[:], 16.0, None, O.mult)])
+    G(0.5, [r("ones")], [r("BO1")], lambda q, T: [q.affine_select(T.BO1[:], T.ones[:], [[-16, 8], [0, 16]], O.is_ge, 0.0, 0, 1)])
+    G(0.5, [r("BO1")], [r("BO")], lambda q, T: [q.affine_select(T.BO[:], T.BO1[:], [[16, 8], [0, 16]], O.is_ge, 0.0, 15, -1)])
+    G(0.5, [r("ones")], [r("IB")], lambda q, T: [q.affine_select(T.IB[:], T.ones[:], [[-1, 128]], O.is_equal, 0.0, 0, 1)])
+    V(v1(256), [r("TI")], [r("LU0")], copy("LU0", "TI"))
+    V(v1(1024), [], [r("RB")], fill("RB", 0.0))
+    V(v1(64), [r("RB")], [r("RB")], fill(("RB", 0, 1024, 16), 256.0))
+    V(tiny, [r("pI")], [r("iI")], ts("iI", "pI", 15, O.bitwise_and))
+    V(tiny, [r("iI")], [r("icol")], copy("icol", "iI"))
+    V(tiny, [r("wi")], [r("wc")], copy("wc", "wi"))
+    V(tiny, [r("ki")], [r("kc")], copy("kc", "ki"))
+    V(tiny, [r("li")], [r("lf")], copy(("lf", 0, 5), ("li", 0, 5)))
+    V(tiny, [r("lf")], [r("nl")], ts(("nl", 0, 5), ("lf", 0, 5), -1.0, O.mult, 0.5, O.add))
+    V(tiny, [r("nl")], [r("nth", 0, 1)], copy(("nth", 0, 1), ("nl", 0, 1)))
+    V(tiny, [r("lf")], [r("thv", 0, 1)], copy(("thv", 0, 1), ("lf", 0, 1)))
+    V(tiny, [r("icol")], [r("ige1")], ts("ige1", "icol", 1.0, O.is_ge))
+    V(tiny, [r("icol")], [r("e15")], ts("e15", "icol", 15.0, O.is_equal))
+    V(tiny, [r("ige1")], [r("pthr")], ts("pthr", "ige1", 102.0, O.mult, -101.0, O.add))
+    V(tiny, [r("ige1")], [r("pthv")], ts("pthv", "ige1", 109.5, O.mult, -101.0, O.add))
+    V(v1(1024), [], [r("sel")], fill("sel", 0.0))
+    for gg in range(8):
+        V(tiny, [r("BO")], [r("sel")], copy(("sel", 16 * gg, 16 * gg + 129 * 15 + 1, 129), ("BO", 16 * gg, 16 * gg + 16)))
+    V(tiny, [r("icol")], [r("i16")], ts("i16", "icol", 16.0, O.mult))
+    V(tiny, [r("i16"), r("v1i")], [r("VB")], ts("VB", "v1i", "i16", O.add))
+    V(v1(128), [r("BO")], [r("BOf")], copy("BOf", "BO"))
+    V(v1(128), [r("BO")], [r("BOf256")], ts("BOf256", "BO", 256.0, O.mult))
+    G(0.5, [r("BO")], [r("BOd")], lambda q, T: [q.affine_select(T.BOd[:], T.BO[:], [[-1, 128]], O.is_equal, 0.0, -1, 1)])
+    V(v1(256), [r("IB"), r("BOd")], [r("OHm")], tt("OHm", "IB", "BOd", O.subtract))
+    V(tiny, [], [r("c64", 0, 1)], lambda q, T: [q.memset(T.c64[0:32, :], -64.0)])
+    V(tiny, [], [r("c64", 1, 2)], lambda q, T: [q.memset(T.c64[32:64, :], 1.0 / 64)])
+    V(v1(128), [r("IB")], [r("IF")], copy("IF", "IB"))
+    V(tiny, [r("kc")], [r("k2")], ts("k2", "kc", -256.0, O.add))
+    V(tiny, [r("k2")], [r("sqb")], ts("sqb", "k2", 2.0, O.mult, 511.875, O.add))
+    V(tiny, [r("k2")], [r("k3")], ts("k3", "k2", "k2", O.mult, -4.0, O.mult))
+    V(tiny, [r("k3")], [r("k4")], ts("k4", "k3", -128.25, O.add))
+    V(v1(2048), [], [r("ZS")], fill("ZS", 0.0))
+    V(v1(512), [], [r("R01")], fill("R01", 1.0))
+    V(v1(64), [r("R01")], [r("R01")], fill(("R01", 0, 1024, 16), 0.0))
+    V(vh(2048), [r("sel")], [r("sel128")], ts("sel128", "sel", 128.0, O.mult))
+    V(tiny, [r("icol"), r("v2i")], [r("VW")], ts("VW", "v2i", "icol", O.add))
+    V(tiny, [r("BO")], [r("blk32")], ts("blk32", ("BO", 0, 128, 16), 32.0, O.mult))
+    V(tiny, [r("BO")], [r("blkn")], ts("blkn", ("BO", 0, 128, 16), -16.0, O.mult))
+    V(v1(64), [], [r("RK")], fill("RK", 0.0))
+    V(tiny, [r("RK")], [r("RK")], fill(("RK", 0, 128, 16), 8388608.0))
+    for c in range(2):
+        V(tiny, [], [r("KM%d" % c, 128, 144)], fill(("KM%d" % c, 128, 144), 8388608.0))
+    V(vh(128), [r("IB"), r("ige1")], [r("pIm")], ts("pIm", "IB", "ige1", O.mult))
+    V(vh(128), [r("pIm")], [r("nIm")], ts("nIm", "pIm", -1.0, O.mult))
+    V(v1(128), [r("sel")], [r("Sel0")], copy("Sel0", ("sel", 0, 128)))
+    V(vh(2048), [r("sel"), r("icol")], [r("isel")], ts("isel", "sel", "icol", O.mult))
+    V(vh(2048), [r("sel"), r("wc")], [r("wsel")], ts("wsel", "sel", "wc", O.mult))
+    V(tiny, [r("icol")], [r("i32c")], ts("i32c", "icol", 32.0, O.mult))
+    V(tiny, [r("v3i"), r("i32c")], [r("SOp")], ts("SOp", "v3i", "i32c", O.add))
+    V(v1(64), [], [r("half")], fill("half", 0.5))
+    V(vh(128), [r("ones"), r("e15")], [r("S15")], ts("S15", "ones", "e15", O.mult))
+    for c in range(2):
+        S(v1(2048), [r("ZS")], [r("W", 2048 * c, 2048 * c + 2048)], act(("W", 2048 * c, 2048 * c + 2048), ("ZS", 2048 * c, 2048 * c + 2048), AF.Copy))
+
+    C35 = 1.5 * 2.0 ** 35
+    C24 = 1.5 * 2.0 ** 24
+    nsel = [("sel", 128 * k, 128 * k + 128) for k in range(16)]
+    for t in range(RO):
+        last = t == RO - 1
+        LU, NU = "LU%d" % t, "NU%d" % t
+        if t:
+            for c, (a0, n, pcs) in enumerate(CHUNKS):
+                add("x", P["hop"], [r("NU%d" % (t - 1), a0, a0 + n)], [r(LU, a0, a0 + n)], None, "arr", sem="arr%d%d" % (t, c))
+        for c, (a0, n, pcs) in enumerate(CHUNKS):
+            a1 = a0 + n
+            V(v1(n), [r(LU, a0, a1)], [r("L32", a0, a1)], copy(("L32", a0, a1), (LU, a0, a1)), "L32 c%d t%d" % (c, t))
+            S(v1(n), [r("L32", a0, a1), r("k4")], [r("LQ", a0, a1)], act(("LQ", a0, a1), ("L32", a0, a1), AF.Identity, bias="k4"), "LQ c%d t%d" % (c, t))
+            dl = "DL%d" % c
+            dma("y", 2.2, [r("L32", a0, a1)], [r(dl)], "dl%d" % c, lambda q, T, dl=dl, a0=a0, a1=a1: [q.dma_start(T[dl][:], T.L32[:, a0:a1])])
+            dma("y", P["wdma"], [r(dl)], [r("W", 16 * a0, 16 * a1)], "w%d" % c,
+                lambda q, T, dl=dl, a0=a0, a1=a1, n=n: [q.dma_start(T.W[j::16, 16 * a0 + n * j:16 * a1], T[dl][:, 1:17 - j, :]) for j in range(1, 16)], 15)
+        for c, (a0, n, pcs) in enumerate(CHUNKS):
+            c0, b0 = 16 * a0, "pb%d0" % (c % 2)
+            for p, (p0, pn) in enumerate(pcs):
+                lo, hi, m = c0 + 16 * p0, c0 + 16 * (p0 + pn), 16 * pn
+                u0, u1 = a0 + p0, a0 + p0 + pn
+                key = "c%d s%d" % (c, p)
+                pt = " %s t%d" % (key, t)
+                either("G " + key, vg(m), sg(m), [r("X"), r(LU, u0, u1)], [r("G", lo, hi)],
+                       gcopy(True, ("G", lo, hi), ("X", 0, 8192), (LU, u0, u1)), gcopy(False, ("G", lo, hi), ("X", 0, 8192), (LU, u0, u1)), "G" + pt)
+                V(vh(m), [r("G", lo, hi), r("RB")], [r("M", lo, hi)], scan(("M", lo, hi), ("RB", 0, m), ("G", lo, hi), O.max, O.min), "M" + pt)
+            for k in range(n // UNIT):
+                lo, hi, m = c0 + 16 * UNIT * k, c0 + 16 * UNIT * (k + 1), 16 * UNIT
+                u0, u1 = a0 + UNIT * k, a0 + UNIT * (k + 1)
+                key = "c%d u%d" % (c, k)
+                ut = " %s t%d" % (key, t)
+                if side("I " + key) == "s":
+                    S(v1(m), [r("M", lo, hi), r("nth", t, t + 1)], [r("H", lo, hi)], act(("H", lo, hi), ("M", lo, hi), AF.Sign, bias=("nth", t, t + 1)), "I" + ut)
+                    th = "pthr"
+                else:
+                    V(vh(m), [r("M", lo, hi), r("thv", t, t + 1)], [r("H", lo, hi)], ts(("H", lo, hi), ("M", lo, hi), ("thv", t, t + 1), O.is_ge), "I" + ut)
+                    th = "pthv"
+                sa = (b0, 256 + UNIT * k, 256 + UNIT * (k + 1))
+                PE(64 * 17, [r("G", lo, hi), r("wsel"), r("ones"), r("c64")], [r(*sa)],
+                   lambda q, T, sa=sa, lo=lo, hi=hi: [q.matmul(ap(sa)(T), T.ones[0:64, :], T.c64[:, 0:UNIT], True, False)] +
+                   [q.matmul(ap(sa)(T), T.wsel[:, 128 * j:128 * j + 128], T.G[:, lo + j:hi:16], False, j == 15) for j in range(16)], 17, "sa" + ut)
+                cn = (b0, UNIT * k, UNIT * (k + 1))
+                PE(64 * 16, [r("H", lo, hi), r("sel")], [r(*cn)], mm(cn, [(nsel[j], ("H", lo + j, hi, 16)) for j in range(16)]), 16, "cnt" + ut)
+                V(v1(UNIT), [r(*cn), r(th)], [r("pas", u0, u1)], ts(("pas", u0, u1), cn, th, O.is_ge), "pass" + ut)
+            sa, ca, cb = (b0, 256, 256 + n), a0, a0 + n
+            V(v1(n), [r(*sa)], [r("B4", ca, cb)], ts(("B4", ca, cb), sa, C35, O.add, -C35, O.add), "B4 c%d t%d" % (c, t))
+            V(v1(n), [r(*sa), r("B4", ca, cb)], [r("UA", ca, cb)], tt(("UA", ca, cb), sa, ("B4", ca, cb), O.subtract), "UA c%d t%d" % (c, t))
+        nwt = ("pk1", 384, 400)
+        PE(64 * 17, [r("pas"), r("sel128"), r("IB"), r("VW")], [r(*nwt)],
+           mm(nwt, [("IB", "VW")] + [(("sel128", 128 * k, 128 * k + 128), ("pas", k, 256, 16)) for k in range(16)]), 17, "nw t%d" % t)
+        V(tiny, [r(*nwt)], [r("OW")], copy("OW", nwt), "OW t%d" % t)
+        for k in range(2):
+            npk = ("pk0", 256 + 128 * k, 384 + 128 * k)
+            PE(256, [r("pas"), r("pIm"), r("nIm"), r("ones")], [r(*npk)], mm(npk, [("pIm", "ones"), ("nIm", ("pas", 128 * k, 128 * k + 128))]), 2, "np t%d" % t)
+        for c, (a0, n, pcs) in enumerate(CHUNKS):
+            a1, c0, c1, h0, h1 = a0 + n, 16 * a0, 16 * (a0 + n), a0 // 16, (a0 + n) // 16
+            b = c % 2
+            b0, b1, pk = "pb%d0" % b, "pb%d1" % b, "pk%d" % b
+            tag = " c%d t%d" % (c, t)
+            R = lambda x, a0=a0, a1=a1: r(x, a0, a1)
+            Q = lambda x, a0=a0, a1=a1: (x, a0, a1)
+            W = lambda x, c0=c0, c1=c1: r(x, c0, c1)
+            nbt = (b0, 128, 128 + n // 16)
+            PE(64 * 17, [R("pas"), r("sel"), r("IB"), r("VB")], [r(*nbt)],
+               mm(nbt, [("IB", ("VB", 0, n // 16))] + [(nsel[k], ("pas", a0 + k, a1, 16)) for k in range(16)]), 17, "nb" + tag)
+            V(tiny, [r(*nbt)], [r("OM", h0, h1)], ts(("OM", h0, h1), nbt, -1.0, O.add), "OM" + tag)
+            if not last:
+                either("XL c%d" % c, vg(n), sg(n), [W("G"), r("OM", h0, h1)], [R("XL")],
+                       gcopy(True, Q("XL"), ("G", c0, c1), ("OM", h0, h1)), gcopy(False, Q("XL"), ("G", c0, c1), ("OM", h0, h1)), "XL" + tag)
+            zs = ("ZS", c0, c1, 16)
+            either("Z c%d" % c, vg(n), sg(n), [W("M"), r("OM", h0, h1)], [W("ZS")],
+                   gcopy(True, zs, ("M", c0, c1), ("OM", h0, h1)), gcopy(False, zs, ("M", c0, c1), ("OM", h0, h1)), "Z" + tag)
+            f_, u_, q_ = (b1, 384, 384 + n), (b1, 0, n), (b1, 256, 256 + n)
+            PE(n, [R("pas"), r("OHm")], [r(*f_)], mm(f_, [("OHm", Q("pas"))]), 1, "oneh" + tag)
+            V(v1(n), [r(*f_), R("UA")], [R("UO")], tt(Q("UO"), f_, Q("UA"), O.mult), "UO" + tag)
+            PE(4 * n, [R("UO"), r("BOf")], [r(*u_)], mm(u_, [("BOf", Q("UO"))]), 1, "u" + tag)
+            S(v1(n), [r(*u_), r("sqb")], [R("SQ")], act(Q("SQ"), u_, AF.Square, bias="sqb", scale=0.25), "SQ" + tag)
+            PE(8 * n, [R("UO"), r("BOf256"), r("IF"), R("LQ")], [r(*q_)], mm(q_, [("IF", Q("LQ")), ("BOf256", Q("UO"))]), 2, "q" + tag)
+            V(v1(n), [r(*q_), R("SQ")], [R("xI")], tt(Q("xI"), q_, Q("SQ"), O.add), "x" + tag)
+            V(v1(n), [R("xI")], [R("cI")], ts(Q("cI"), Q("xI"), 8191, O.bitwise_and), "and" + tag)
+            V(v1(n), [R("cI")], [R("CU")], copy(Q("CU"), Q("cI")), "CU" + tag)
+            first = []
+            for p, (p0, pn) in enumerate(pcs):
+                lo, hi, m = c0 + 16 * p0, c0 + 16 * (p0 + pn), 16 * pn
+                u0, u1 = a0 + p0, a0 + p0 + pn
+                key = "c%d s%d" % (c, p)
+                pt = " %s t%d" % (key, t)
+                D, A, z16, d16, sv = ("D", lo, hi), ("A", lo, hi), ("ZS", lo, hi, 16), ("D", lo, hi, 16), ("sv", u0, u1)
+                if not last:
+                    f = 2.0 if side("C " + key) == "v" else 1.0
+                    either("Z2 " + key, v1(pn), v1(pn), [r("ZS", lo, hi)], [r("Z2", u0, u1)],
+                           ts(("Z2", u0, u1), z16, f, O.mult, -0.5, O.add), act(("Z2", u0, u1), z16, AF.Copy, bias=-0.5, scale=f), "Z2" + pt)
+                V(vh(m), [r("ZS", lo, hi), r("R01")], [r("Zx", lo, hi)], scan(("Zx", lo, hi), ("R01", 0, m), ("ZS", lo, hi), O.mult, O.add), "Zx" + pt)
+                D0 = r("D0", lo, hi)
+                if side("C " + key) == "v":
+                    V(vg(m), [r("X"), r("CU", u0, u1), r("Zx", lo, hi)], [r(*D), D0], gtt(D, ("X", 0, 8192), ("CU", u0, u1), ("Zx", lo, hi), O.subtract), "D" + pt)
+                    first.append((p0, pn, d16, D0))
+                    either("A " + key, vh(m), v1(m), [r(*D), D0], [r(*A)], ts(A, D, 0.0, O.max), act(A, D, AF.Relu), "A" + pt)
+                else:
+                    S(sg(m), [r("X"), r("CU", u0, u1)], [r(*D), D0], gcopy(False, D, ("X", 0, 8192), ("CU", u0, u1)), "D" + pt)
+                    S(v1(pn), [D0], [r(*sv)], act(sv, d16, AF.Copy), "sv" + pt)
+                    first.append((p0, pn, sv, r(*sv)))
+                    V(v1(2 * pn), [r("ZS", lo, hi), r(*sv)], [D0], tt(d16, sv, z16, O.max), "fx" + pt)
+                    V(vh(m), [r(*D), D0, r("Zx", lo, hi)], [r(*A)], scan(A, ("Zx", lo, hi), D, O.min, O.max), "A" + pt)
+                    S(v1(pn), [r(*sv), r(*A)], [D0], act(d16, sv, AF.Copy), "rs" + pt)
+
+            def key0(q, T, c0=c0, c1=c1, n=n, pk=pk, first=first):
+                o = [q.matmul(T[pk][0:n, 0:128], T.ones[0:1, 0:n], T.irow[:], True, False), q.matmul(T[pk][0:n, 0:128], T.ones[0:1, 0:n], T.grow[:], False, False)]
+                o += [q.matmul(T[pk][0:n, i:128:16], T.D[:, c0 + i:c1:16], T.blkn[:], False, False) for i in range(1, 16)]
+                return o + [q.matmul(T[pk][p0:p0 + pn, 0:128:16], ap(x)(T), T.blkn[:], False, False) for (p0, pn, x, _) in first]
+
+            def key1(q, T, c0=c0, c1=c1, n=n, pk=pk):
+                return [q.matmul(T[pk][0:n, i:128:16], T.A[:, c0 + i:c1:16], T.blk32[:], False, i == 15) for i in range(16)]
+            PE(64 * 17 + 256, [W("D"), r("blkn"), r("irow"), r("grow"), r("ones")] + [f[3] for f in first], [r(pk, 0, 128)], key0, 17 + len(first), "key0" + tag)
+            PE(64 * 16, [W("A"), r("blk32"), r(pk, 0, 128)], [r(pk, 0, 128)], key1, 16, "key1" + tag)
+            KM, KB, OH = "KM%d" % b, "KB%d" % b, "OH%d" % b
+
+            def rows(x, lo=0, hi=128, st=1, n=n): return lambda T: T[x][0:n, lo:hi:st] if st > 1 else T[x][0:n, lo:hi]
+            V(v1(128), [r(pk, 0, 128), r("RK")], [r(KM, 0, 128)], lambda q, T, n=n, KM=KM, pk=pk: [q.tensor_tensor_scan(T[KM][0:n, 0:128], T.RK[0:n, :], T[pk][0:n, 0:128], 0.0, O.max, O.min)], "KM" + tag)
+            V(v1(128), [r(KM), r("RK")], [r(KB)], lambda q, T, n=n, KM=KM, KB=KB: [q.tensor_tensor_scan(T[KB][0:n, :], T.RK[0:n, :], T[KM][0:n, 15:143], 0.0, O.max, O.min)], "KB" + tag)
+            V(v1(128), [r(pk, 0, 128), r(KB)], [r(OH)], lambda q, T, n=n, KB=KB, pk=pk, OH=OH: [q.tensor_tensor(T[OH][0:n, :], T[pk][0:n, 0:128], T[KB][0:n, :], O.is_equal)], "OH" + tag)
+            oh = (b0, 384, 384 + n)
+            PE(n, [r(OH), r("IB")], [r(*oh)], lambda q, T, n=n, OH=OH, oh=oh: [q.matmul(ap(oh)(T), T[OH][0:n, :], T.IB[0:n, 0:n], True, True)], 1, "OHA" + tag)
+            if not last:
+                either("OHA c%d" % c, v1(n), v1(n), [r(*oh)], [R("OHA")], copy(Q("OHA"), oh), act(Q("OHA"), oh, AF.Copy), "OHAe" + tag)
+                tot = (b1, 128, 128 + n // 16)
+                PE(64 * 17, [R("OHA"), r("isel"), r("IB"), r("VB")], [r(*tot)],
+                   mm(tot, [("IB", ("VB", 0, n // 16))] + [(("isel", 128 * k, 128 * k + 128), ("OHA", a0 + k, a1, 16)) for k in range(16)]), 17, "to" + tag)
+                V(tiny, [r(*tot)], [r("OT", h0, h1)], copy(("OT", h0, h1), tot), "OT" + tag)
+                V(vg(n), [W("D"), W("D0"), r("OT", h0, h1), R("Z2")], [R("tt")], gtt(Q("tt"), ("D", c0, c1), ("OT", h0, h1), Q("Z2"), O.add), "tt" + tag)
+                V(v1(n), [R("tt")], [R("Y2")], ts(Q("Y2"), Q("tt"), C24, O.add, -C24, O.add), "Y2" + tag)
+            np_, nl_ = ("pk0", 256 + a0, 256 + a1), ("pb%d2" % b, 0, n)
+            V(vg(n), [W("W"), r("OW", h0, h1), R("pas")], [R("R1")], gtt(Q("R1"), ("W", c0, c1), ("OW", h0, h1), Q("pas"), O.mult), "R1" + tag)
+            V(v1(n), [r(*np_), R("cI")], [R("C1")], tt(Q("C1"), np_, Q("cI"), O.mult), "C1" + tag)
+            V(v1(n), [r(*oh), R("cI")], [R("OC")], tt(Q("OC"), oh, Q("cI"), O.mult), "OC" + tag)
+            PE(8 * n, [R("R1"), R("C1"), r("IF")], [r(*nl_)],
+               lambda q, T, x=Q("R1"), y=Q("C1"), o=nl_: [q.matmul(ap(o)(T), T.IF[:], ap(x)(T), True, False), q.matmul(ap(o)(T), T.IF[:], ap(y)(T), False, False)], 2, "nl0" + tag)
+            PE(4 * n, [R("OC"), r("Sel0"), r(*nl_)], [r(*nl_)], lambda q, T, x=Q("OC"), o=nl_: [q.matmul(ap(o)(T), T.Sel0[:], ap(x)(T), False, True)], 1, "nl1" + tag)
+            if not last:
+                V(v1(n), [r(*nl_)], [R(NU)], copy(Q(NU), nl_), "NU" + tag)
+                add("g", 0.5, [R(NU)], [], ("send", t, c), "send" + tag, sem="sent")
+            else:
+                S(v1(n), [r(*nl_)], [R("yls")], act(Q("yls"), nl_, AF.Copy), "yls" + tag)
+                dma("y", 2.0, [R("yls")], [], "ol%d" % c, lambda q, T, x=Q("yl"), y=Q("yls"): [q.dma_start(ap(x)(T), ap(y)(T))])
+                S(v1(n), [W("ZS")], [R("yzs")], act(Q("yzs"), zs, AF.Copy), "yzs" + tag)
+                dma("y", 2.0, [R("yzs")], [], "oz%d" % c, lambda q, T, x=Q("yz"), y=Q("yzs"): [q.dma_start(ap(x)(T), ap(y)(T))])
+        if not last:
+            tag = " t%d" % t
+            sb = ("pb11", 144, 160)
+            PE(64 * 16, [r("XL"), r("wsel")], [r(*sb)], mm(sb, [(("wsel", 128 * k, 128 * k + 128), ("XL", k, 256, 16)) for k in range(16)]), 16, "sb" + tag)
+            V(tiny, [r(*sb)], [r("soA")], copy("soA", sb), "soA" + tag)
+            V(tiny, [r("soA")], [r("soB")], ts("soB", "soA", 31, O.bitwise_and), "soB" + tag)
+            V(tiny, [r("soB"), r("SOp")], [r("soC")], tt("soC", "soB", "SOp", O.add), "soC" + tag)
+            V(tiny, [r("soC")], [r("SO")], copy("SO", "soC"), "SO" + tag)
+            eb = ("pb11", 192, 256)
+            PE(64 * 4, [r("pas"), r("S15")], [r(*eb)], mm(eb, [("S15", ("pas", 64 * k, 64 * k + 64)) for k in range(4)]), 4, "E" + tag)
+            V(tiny, [r(*eb)], [r("er")], lambda q, T: [q.tensor_reduce(T.er[:], T.pb11[:, 192:256], AxisListType.X, O.add, negate=True)], "er" + tag)
+            V(tiny, [r("er")], [r("eI")], copy("eI", "er"), "eI" + tag)
+            V(tiny, [r("eI")], [r("eJ")], ts("eJ", "eI", 7, O.bitwise_and), "eJ" + tag)
+            n1 = (t + 1, t + 2)
+            who = [side("I c%d u%d" % (c, k)) for c, (a0, n, pcs) in enumerate(CHUNKS) for k in range(n // UNIT)]
+            if "s" in who:
+                V(tiny, [r("eJ"), r("nl")], [r("nth", *n1)], tt(("nth",) + n1, ("nl",) + n1, "eJ", O.subtract), "nth" + tag)
+            if "v" in who:
+                V(tiny, [r("eJ"), r("lf")], [r("thv", *n1)], tt(("thv",) + n1, ("lf",) + n1, "eJ", O.add), "thv" + tag)
+            for c, (a0, n, pcs) in enumerate(CHUNKS):
+                h0, h1 = a0 // 16, (a0 + n) // 16
+                V(0.055 + 3.5 * n * cyc, [r("Y2", a0, a0 + n), r("half"), r("SO")], [r("X")],
+                  lambda q, T, y=("Y2", a0, a0 + n), h=("half", 0, n), o=("SO", h0, h1): [q.tensor_tensor(T.X[:, 0:8192].indirect(ap(o)(T)), ap(y)(T), ap(h)(T), O.mult)], "scat c%d" % c + tag)
+    return ops
+
+
+def deps_of(ops):
+    acc = {}
+    for o in ops:
+        d = set()
+        for (b, lo, hi) in o["reads"]:
+            for (p, l2, h2, w) in acc.get(b, []):
+                if w and l2 < hi and lo < h2:
+                    d.add((p, "raw"))
+        for (b, lo, hi) in o["writes"]:
+            for (p, l2, h2, w) in acc.get(b, []):
+                if l2 < hi and lo < h2:
+                    d.add((p, "waw" if w else "war"))
+        for (b, lo, hi) in o["writes"]:
+            acc[b] = [a for a in acc.get(b, []) if not (lo <= a[1] and a[2] <= hi)] + [(o["id"], lo, hi, True)]
+        for (b, lo, hi) in o["reads"]:
+            acc.setdefault(b, []).append((o["id"], lo, hi, False))
+        o["deps"] = sorted((p, k) for (p, k) in d if p != o["id"])
+        o["banks"] = sorted(set(b for (b, lo, hi) in o["reads"] + o["writes"] if b.startswith("pb") or b.startswith("pk")))
+    return ops
+
+
+def schedule(ops):
+    n = len(ops)
+    wake = P["wake"]
+    succ = [[] for _ in range(n)]
+    left = [0] * n
+    for o in ops:
+        ps = set(p for (p, k) in o["deps"])
+        left[o["id"]] = len(ps)
+        for p in ps:
+            succ[p].append(o["id"])
+    prio = [0.0] * n
+    for o in reversed(ops):
+        prio[o["id"]] = o["cost"] + max([prio[s] + wake for s in succ[o["id"]]], default=0.0) + PRI.get(o["name"].rsplit(" t", 1)[0], 0.0)
+    fin = [0.0] * n
+    start = [0.0] * n
+    avail = [0.0] * n
+    free = {"x": 0.0}
+    bank = {}
+    ready = [o["id"] for o in ops if left[o["id"]] == 0]
+    order = []
+    while ready:
+        cand = []
+        first = 1e9
+        for i in ready:
+            o = ops[i]
+            e = o["eng"]
+            st = max(avail[i], free.get(e, 0.0))
+            for b in o["banks"]:
+                for e2, f2 in bank.get(b, {}).items():
+                    if e2 != e and f2 + wake > st:
+                        st = f2 + wake
+            cand.append((st, -prio[i], i))
+            if st < first:
+                first = st
+        pr, st, i = min((p, s, j) for (s, p, j) in cand if s <= first + 0.03)
+        o = ops[i]
+        e = o["eng"]
+        start[i] = st
+        fin[i] = st + o["cost"]
+        if o["sem"] and e in ("y", "s"):
+            free[e] = st + 0.06 * o["n"]
+        elif e != "x":
+            free[e] = fin[i]
+        for b in o["banks"]:
+            bank.setdefault(b, {})[e] = fin[i]
+        order.append(i)
+        ready.remove(i)
+        for s in succ[i]:
+            left[s] -= 1
+            if left[s] == 0:
+                ready.append(s)
+                a = 0.0
+                for (p, k) in ops[s]["deps"]:
+                    if not (k == "war" and ops[p]["eng"] == ops[s]["eng"]):
+                        a = max(a, fin[p] + wake)
+                avail[s] = a
+    return order, start, fin
+
+
+def free_steps():
+    out = []
+    for c, (a0, n, pcs) in enumerate(CHUNKS):
+        for p in range(len(pcs)):
+            out += ["%s c%d s%d" % (x, c, p) for x in ("G", "C", "A", "Z2")]
+        out += ["I c%d u%d" % (c, k) for k in range(n // UNIT)] + ["%s c%d" % (x, c) for x in ("Z", "XL", "OHA")]
+    return out
+
+
+def step_names():
+    keep, names = dict(PLACE), set()
+    for e in "sv":
+        for k in free_steps():
+            PLACE[k] = e
+        names |= set(o["name"].rsplit(" t", 1)[0] for o in build() if " t" in o["name"])
+    PLACE.clear()
+    PLACE.update(keep)
+    return sorted(names)
+
+
+PLACE.update(zip(free_steps(), SIDES))
+PRI.update((k, int(x) / 10) for k, x in zip(step_names(), RANKS.split()))
+
+
+def rank_program(g, core, T, topo):
+    rank = T.rank_of(core)
+    if rank is None:
+        return
+    cores = T.cores
+    dst = cores[(rank + 1) % len(cores)]
+    rid, pid, _ = topo.addr(dst)
+    mask = topo.mask(core, dst)
+    ne = len(topo.engines(core, dst))
+    ni = len(topo.engines(cores[(rank - 1) % len(cores)], core))
+    ops = deps_of(build())
+    order = schedule(ops)[0]
+    queues = {"v": g.vector, "s": g.scalar, "t": g.tensor, "g": g, "y": g.sync}
+    csem = {"v": "cv", "s": "cs", "t": "ct", "g": "cg"}
+    total = {}
+    token = {}
+    after = {}
+    know = {e: {} for e in queues}
+    lastbank = {}
+    for i in order:
+        o = ops[i]
+        e = o["eng"]
+        if e == "x":
+            token[i] = (o["sem"], ni)
+            total[o["sem"]] = ni
+            after[i] = {}
+            continue
+        q = queues[e]
+        need = {}
+        ds = [p for (p, k) in o["deps"] if not (k == "war" and ops[p]["eng"] == e and token[p][0] == csem.get(e))]
+        if e == "t":
+            ds = [p for p in ds if ops[p]["eng"] != "t"]
+        for b in o["banks"]:
+            for e2, p in lastbank.get(b, {}).items():
+                if e2 != e:
+                    ds.append(p)
+        inherit = []
+        for p in ds:
+            s, v = token[p]
+            if know[e].get(s, 0) < v:
+                need[s] = max(need.get(s, 0), v)
+                inherit.append(p)
+        for s in sorted(need):
+            if any(after[p].get(s, 0) >= need[s] and token[p][0] != s for p in inherit):
+                continue
+            q.wait_ge(T.sem[s], int(need[s]))
+        for p in inherit:
+            s, v = token[p]
+            for s2, v2 in list(after[p].items()) + [(s, v)]:
+                if know[e].get(s2, 0) < v2:
+                    know[e][s2] = v2
+        after[i] = dict(know[e])
+        if isinstance(o["fn"], tuple):
+            _, t, c = o["fn"]
+            a0, n, _ = CHUNKS[c]
+            g.remote_dma(T["LU%d" % (t + 1)][:, a0:a0 + n], T["NU%d" % t][:, a0:a0 + n], T.sem["arr%d%d" % (t + 1, c)], T.sem["sent"], pid, rid, mask)
+            total["sent"] = total.get("sent", 0) + ne
+            token[i] = ("sent", total["sent"])
+        else:
+            ins = o["fn"](q, T)
+            s, k = (o["sem"], 16) if o["sem"] else (csem[e], 1)
+            for x in ins:
+                x.then_inc(T.sem[s], k)
+            total[s] = total.get(s, 0) + k * len(ins)
+            token[i] = (s, total[s])
+        for b in o["banks"]:
+            lastbank.setdefault(b, {})[e] = i
+    for s in sorted(total):
+        g.wait_ge(T.sem[s], int(total[s]))

@@ -1,73 +1,93 @@
 from concourse.mybir import AluOpType, AxisListType, ActivationFunctionType
 
 RO = 5
-CHUNKS = [(0, 128, [(0, 32), (32, 32), (64, 32), (96, 32)]), (128, 128, [(0, 32), (32, 32), (64, 32), (96, 32)])]
+NC, NT = 2, 128
 UNIT = 64
+GP = [[32, 32, 32, 32], [32, 32, 32, 32]]
+DP = [[32, 32, 32, 32], [32, 32, 32, 32]]
+HP = [[1, 1], [1, 1]]
+HU = [64, 64]
+AU, KG = [64, 0], 4
+KP = [[128], [96, 32]]
+DB = [["pa0", "pb0"], ["pa1", "pb1", "pa0", "pb1"]]
+SB = "pc1"
 
-BF, F32, I32, U16 = "bfloat16", "float32", "int32", "uint16"
-SCRATCH = {"DL0": ("dram", [8, 16, 128], F32), "DL1": ("dram", [8, 16, 128], F32), "irow": ("sbuf", [1, 128], BF), "grow": ("sbuf", [1, 128], BF), "c64": ("sbuf", [64, 128], BF)}
+BF, F32, I32, U16, F16 = "bfloat16", "float32", "int32", "uint16", "float16"
+SCRATCH = {"irow": ("sbuf", [1, 128], BF), "grow": ("sbuf", [1, 128], BF), "mh": ("sbuf", [1, 128], BF)}
 for _n, _w, _d in (
-        ("X", 8192, BF), ("TI", 256, I32), ("wi", 1, I32), ("ki", 1, I32), ("li", 8, I32),
-        ("wc", 1, F32), ("kc", 1, F32), ("nl", 8, F32), ("lf", 8, F32), ("k2", 1, F32), ("k3", 1, F32), ("k4", 1, F32), ("sqb", 1, F32),
-        ("pI", 1, I32), ("iI", 1, I32), ("icol", 1, F32), ("i16", 1, F32), ("i32c", 1, F32),
-        ("pthr", 1, F32), ("pthv", 1, F32), ("ige1", 1, F32), ("e15", 1, F32),
-        ("ones", 128, BF), ("BO1", 128, BF), ("BO", 128, BF), ("IB", 128, BF), ("IF", 128, F32),
-        ("pIm", 128, BF), ("nIm", 128, BF), ("BOd", 128, BF), ("OHm", 128, BF), ("BOf", 128, F32), ("BOf256", 128, F32),
-        ("UA", 256, F32), ("UO", 256, F32),
-        ("S15", 128, BF), ("Sel0", 128, F32), ("LQ", 256, F32),
-        ("sel", 2048, BF), ("isel", 2048, BF), ("wsel", 2048, BF), ("sel128", 2048, BF), ("blk32", 8, BF), ("blk16", 8, BF), ("blkn", 8, BF),
-        ("v1i", 8, I32), ("v2i", 16, I32), ("v3i", 16, I32), ("VB", 8, BF), ("VW", 16, BF), ("SOp", 16, I32),
-        ("R01", 1024, BF), ("RB", 1024, BF), ("RK", 128, BF), ("half", 128, BF), ("W", 4096, F32),
-        ("soA", 16, I32), ("soB", 16, I32), ("soC", 16, I32), ("SO", 16, U16),
-        ("er", 1, F32), ("eI", 1, I32), ("eJ", 1, I32), ("nth", 8, F32), ("thv", 8, F32),
-        ("ZS", 4096, BF), ("G", 4096, BF), ("M", 4096, BF), ("H", 4096, BF), ("Zx", 4096, BF), ("D", 4096, BF), ("A", 4096, BF),
-        ("pas", 256, BF), ("OM", 16, U16), ("OW", 16, U16), ("OT", 16, U16), ("XL", 256, BF), ("Z2", 256, F32), ("B4", 256, BF),
-        ("SQ", 256, F32), ("xI", 256, I32), ("cI", 256, I32), ("CU", 256, U16), ("L32", 256, F32), ("OHA", 256, BF), ("sv", 256, BF),
-        ("OC", 256, F32), ("C1", 256, F32), ("R1", 256, F32), ("tt", 256, F32), ("Y2", 256, BF), ("yls", 256, F32), ("yzs", 256, F32)):
+        ("X", 8192, BF), ("TI", 256, I32), ("pri", 8, I32), ("prm", 8, F32), ("wq", 1, F32), ("sqb", 1, F32), ("k3", 1, F32), ("k4", 1, F32),
+        ("pI", 1, I32), ("iI", 1, I32), ("icol", 1, F32), ("pth", 1, F32), ("ige1", 1, F32), ("e15", 1, F32),
+        ("ones", 128, BF), ("BO1", 128, BF), ("BO", 128, BF), ("BOh", 128, F16), ("IB", 128, BF), ("IF", 128, F32),
+        ("pIm", 128, BF), ("nIm", 128, F16), ("BOd", 128, BF), ("OHm", 128, F16), ("S15", 128, F16), ("Sel0", 128, F32),
+        ("sel", 2048, BF), ("wsel", 2048, BF), ("selh", 2048, F16), ("Rep", 2048, BF), ("blk16", 8, BF), ("blk32", 8, BF), ("blkn", 8, BF),
+        ("vbi", 16, I32), ("VB", 8, BF), ("VW", 32, F32), ("VS", 16, BF),
+        ("RB", 1024, BF), ("RK", 128, BF), ("half", 128, BF), ("W", 4096, F32),
+        ("er", 1, F32), ("eI", 1, I32), ("eJ", 1, I32), ("thv", 8, F32),
+        ("G", 4096, BF), ("M", 4096, BF), ("H", 4096, BF), ("D", 4096, BF), ("A", 4096, BF),
+        ("PU", 512, F16), ("OM", 16, U16), ("nw", 32, F32), ("OW", 32, U16), ("OT", 16, U16), ("SO", 16, U16), ("k2", 32, I32), ("rr", 32, BF),
+        ("KQ", 256, I32), ("UA", 256, F16), ("LQ", 256, F32), ("Zb", 256, BF), ("ZT", 256, BF), ("XB", 256, BF),
+        ("xI", 256, I32), ("cI", 256, I32), ("CU", 256, U16), ("L32", 256, F32), ("OHA", 256, BF),
+        ("OC", 256, F32), ("C1", 256, F32), ("RC", 256, F32), ("Y2", 256, BF), ("Z2", 256, F32), ("tt", 256, F32), ("yls", 256, F32), ("yzs", 256, F32)):
     SCRATCH[_n] = ("sbuf", [128, _w], _d)
-for _c in range(2):
+for _c in range(NC):
+    SCRATCH["DL%d" % _c] = ("dram", [8, 16, 128], F32)
     SCRATCH["KM%d" % _c] = ("sbuf", [128, 144], F32)
     SCRATCH["KB%d" % _c] = ("sbuf", [128, 128], F32)
     SCRATCH["OH%d" % _c] = ("sbuf", [128, 128], BF)
-    for _b in ("pb%d0", "pb%d1", "pb%d2", "pk%d"):
+    for _b in ("pa%d", "pb%d", "pc%d", "pk%d"):
         SCRATCH[_b % _c] = ("psum", [128, 512], F32)
 for _t in range(RO):
     SCRATCH["LU%d" % _t] = ("sbuf", [128, 256], U16)
     if _t < RO - 1:
         SCRATCH["NU%d" % _t] = ("sbuf", [128, 256], U16)
+BANKS = [_n for _n in SCRATCH if SCRATCH[_n][0] == "psum"]
 
-SEMAPHORES = ["cv", "cs", "ct", "cg", "sent", "ldt", "ldw", "ldk", "ldl", "ldx", "ldy"] + \
-    ["%s%d" % (a, c) for a in ("oz", "ol", "dl", "w") for c in range(len(CHUNKS))] + ["arr%d%d" % (t, c) for t in range(1, RO) for c in range(len(CHUNKS))]
+SEMAPHORES = ["cv", "cs", "ct", "cg", "sent", "ldp", "ldt", "ldx", "ldy"] + \
+    ["%s%d" % (a, c) for a in ("oz", "ol", "dl", "w") for c in range(NC)] + ["arr%d%d" % (t, c) for t in range(1, RO) for c in range(NC)]
 
-P = {"cyc": 0.92e-3, "ga": 1.56, "pec": 0.5e-3, "wake": 0.18, "hop": 5.0, "wdma": 7.0}
-PLACE = {}
-PRI = {}
-SIDES = "svssssssssvvvsvsvvssssssssvsvsssvvvvsvsvss"
-RANKS = """-1390 632 827 506 664 -870 -414 -646 440 822 -405 -395 632 -47 -2068 636 463 123 405 -1113 -586 100 256 947 447 2980 1247 -506 31 1199 231 -8 -277 803 223 -1047 -101 74 -971 -1330 -737 388 -75 716 327 513 1140 928 -1274 788 -1515 841 -727 402 1381 91 -1261 211 292 -469 -306 1419 -9 201 452 134 -287 -751 -781 1073 487 -452 33 -412 -1111 -1018 446 375 69 -641 1299 -481 173 307 -788 -491 -449 -727 -588 -1520 611 -1265 191 245 171 -939 -359 1543 248 -402 -2744 -408 -2445 -364 -490 -1360 922 -269 -517 -407 1066 108 1707 -343 290 430 -538 1058 635 549 -1249 -767 -333 255 -632 493 -561 -206 -691 652 255 36 914 -1112 -605 549 265 -381 908 -512 -601 599 741 -279 595 -581 728 -170 -897 -717 7 1542 -457 -745 804 -4 288 1004 -108 -55 -385 -319 -508 951 -592 252 -161 -519 1418 1071 1230 244 46 -1237 2 -204"""
+P = {"cyc": 0.87e-3, "ga": 1.56, "sc": 3.8, "pec": 0.45e-3, "wake": 0.18, "hop": 3.5, "wdma": 6.0, "ldx": 8.0}
+ON_V = {"A3b", "RCa", "Gp1a", "Gp3a", "ttb", "Dp3b", "ZTb"}
+PERIOD = 20
+CYCLE = """
+Gp0a Gp1a L32a Gp2a sau0a Mp0a dla Mp1a Hp0u0a keycb Hp1u0a KQu0a Mp2a Gp1b cntu0a Gp3a Gp0b Hp0u1a passu0a UAu0a wa Mp3a onehu0a Gp2b sau1a Mp1b UOu0a Hp1u1a uu0a sau0b Mp0b LQa KQu1a SQu0a Hp1u0b Gp3b cntu1a Hp0u0b KQu0b xu0a L32b cntu0b andu0a passu1a LQb dlb UAu1a CUu0a Mp2b onehu1a sau1b Dp0a UOu1a Mp3b Hp0u1b uu1a npa nba UAu0b SQu1a KQu1b Dp1a passu0b Hp1u1b onehu0b xu1a OMa cntu1b UOu0b andu1a Za CUu1a C1a wb uu0b passu1b Zpa SQu0b UAu1b Dp2a Au0i4a onehu1b Eb npb UOu1b xu0b Au0i0a Dp3a nbb andu0b Au0i12a uu1b OMb SQu1b CUu0b Au1i0a Zb Dp1b xu1b Au1i8a Zpb kla andu1b ZTb key0a nwb Dp0b CUu1b Au1i4a dz1b dx1b Au0i8a dz2b yzsa Dp2b Au1i12a dz0b oza key4a Dp3b dx0b key8a A1b key12a dx2b k2b A0b OWb KMa kl3b RCa dz3b A2b KBa rrb dx3b OHa sob Z2b nl0a yzsb A3b oha key0b ozb erb OCa SOb key1b C1b OHAa eIb nl1a RCb eJb toa KMb ylsa NUa thvb KBb ola -arra senda nl0b OTa OHb tta ohb OCb ypa OHAb nl1b Y2a ylsb tob NUb olb scata sendb -arrb -keyca OTb ttb Y2b scatb
+"""
 
 
-def side(key):
-    return PLACE.get(key, "s")
+def extra(eng, sem, n, sides, cost=0.0):
+    if sem or eng not in "vs":
+        return 0.0
+    if P.get("pm") and any(x[0] in BANKS for x in sides):
+        return max(0.0, n * P["pm"] * P["cyc"] - cost)
+    return n * (P.get("ov", 0.0) + (P.get("op", 0.0) if any(x[0] in BANKS for x in sides) else 0.0))
+
+
+def send_sides(fn, T):
+    _, t, c = fn
+    return T["LU%d" % (t + 1)][:, NT * c:NT * c + NT], T["NU%d" % t][:, NT * c:NT * c + NT]
 
 
 def build():
     O, AF = AluOpType, ActivationFunctionType
     ops = []
     cyc, pec = P["cyc"], P["pec"]
+    n = NT
 
-    def v1(n): return max(64, n) * cyc
-    def vh(n): return max(64, n / 2) * cyc
-    def vg(n): return 0.055 + n * P["ga"] * cyc
-    def sg(n): return 0.07 + n * P["ga"] * cyc
+    def v1(m): return max(64, m) * cyc
+    def vh(m): return max(64, m / 2) * cyc
+    def vg(m): return 0.055 + m * P["ga"] * cyc
+    def sg(m): return 0.07 + m * P["ga"] * cyc
     tiny = v1(1)
 
-    def add(eng, cost, reads, writes, fn, name="", sem=None, n=1):
-        ops.append({"eng": eng, "cost": cost, "reads": reads, "writes": writes, "fn": fn, "name": name, "sem": sem, "n": n, "id": len(ops)})
+    def rng(x): return (x, 0, 100000) if isinstance(x, str) else x[:3]
 
-    def V(cost, reads, writes, fn, name=""): add("v", cost, reads, writes, fn, name)
-    def S(cost, reads, writes, fn, name=""): add("s", cost, reads, writes, fn, name)
-    def PE(cyc_n, reads, writes, fn, n, name=""): add("t", cyc_n * pec, reads, writes, fn, name, n=n)
-    def r(b, lo=0, hi=100000): return (b, lo, hi)
+    def add(eng, cost, reads, writes, fn, step=None, sem=None, k=1):
+        reads, writes = [rng(x) for x in reads], [rng(x) for x in writes]
+        ops.append({"eng": eng, "cost": cost + extra(eng, sem, k, reads + writes, cost), "reads": reads, "writes": writes, "fn": fn, "step": step, "sem": sem, "n": k, "id": len(ops)})
+
+    def V(cost, reads, writes, fn, step=None): add("v", cost, reads, writes, fn, step)
+    def S(cost, reads, writes, fn, step=None): add("s", cost, reads, writes, fn, step)
+    def G(cost, reads, writes, fn): add("g", cost, reads, writes, fn)
+    def dma(eng, cost, reads, writes, sem, fn, k=1, step=None): add(eng, cost, reads, writes, fn, step, sem=sem, k=k)
 
     def ap(a):
         if isinstance(a, (int, float)):
@@ -76,276 +96,269 @@ def build():
             return lambda T: T[a][:]
         if len(a) == 3:
             return lambda T: T[a[0]][:, a[1]:a[2]]
-        return lambda T: T[a[0]][:, a[1]:a[2]:a[3]]
+        if len(a) == 4:
+            return lambda T: T[a[0]][:, a[1]:a[2]:a[3]]
+        return lambda T: T[a[0]][a[4]:a[5], a[1]:a[2]:a[3]]
 
-    def copy(out, in_): return lambda q, T: [q.tensor_copy(ap(out)(T), ap(in_)(T))]
-    def fill(out, x): return lambda q, T: [q.memset(ap(out)(T), x)]
-    def tt(out, a, b, op): return lambda q, T: [q.tensor_tensor(ap(out)(T), ap(a)(T), ap(b)(T), op)]
-    def scan(out, a, b, o0, o1): return lambda q, T: [q.tensor_tensor_scan(ap(out)(T), ap(a)(T), ap(b)(T), 0.0, o0, o1)]
-    def act(out, in_, f, **kw): return lambda q, T: [q.activation(ap(out)(T), ap(in_)(T), f, **dict((k, ap(x)(T)) for k, x in kw.items()))]
+    def names(*xs): return [x for x in xs if not isinstance(x, (int, float)) and x is not None]
+    def wid(a): return SCRATCH[a][1][1] if isinstance(a, str) else len(range(*a[1:4]))
+    def two(*xs): return all(SCRATCH[rng(x)[0]][2] in (BF, F16, U16) for x in xs)
+    def cost1(out, in_): return vh(wid(out)) if two(out, in_) else v1(wid(out))
 
-    def ts(out, in0, s1, o1, s2=None, o2=None):
-        if o2 is None:
-            return lambda q, T: [q.tensor_scalar(ap(out)(T), ap(in0)(T), ap(s1)(T), None, o1)]
-        return lambda q, T: [q.tensor_scalar(ap(out)(T), ap(in0)(T), ap(s1)(T), ap(s2)(T), o1, o2)]
+    def copy(out, in_, step=None): V(cost1(out, in_), [in_], [out], lambda q, T: [q.tensor_copy(ap(out)(T), ap(in_)(T))], step)
+    def fill(out, x): V(cost1(out, out), [], [out], lambda q, T: [q.memset(ap(out)(T), x)])
 
-    def gcopy(q_v, out, win, off):
-        if q_v:
-            return lambda q, T: [q.tensor_copy(ap(out)(T), ap(win)(T).indirect(ap(off)(T)))]
-        return lambda q, T: [q.activation(ap(out)(T), ap(win)(T).indirect(ap(off)(T)), AF.Copy)]
+    def tt(out, a, b, op, step=None):
+        f = 1 if rng(a)[0] in BANKS or rng(b)[0] in BANKS else 2
+        V(v1(f * wid(out)), [a, b], [out], lambda q, T: [q.tensor_tensor(ap(out)(T), ap(a)(T), ap(b)(T), op)], step)
 
-    def gtt(out, win, off, b, op): return lambda q, T: [q.tensor_tensor(ap(out)(T), ap(win)(T).indirect(ap(off)(T)), ap(b)(T), op)]
-    def mm(out, terms): return lambda q, T: [q.matmul(ap(out)(T), ap(a)(T), ap(b)(T), i == 0, i == len(terms) - 1) for i, (a, b) in enumerate(terms)]
+    def scan(out, a, b, o0, o1, step):
+        V(vh(wid(out)) if two(out, a, b) else v1(wid(out)), [a, b], [out], lambda q, T: [q.tensor_tensor_scan(ap(out)(T), ap(a)(T), ap(b)(T), 0.0, o0, o1)], step)
 
-    def either(key, nv, ns, reads, writes, fv, fs, name):
-        if side(key) == "v":
-            V(nv, reads, writes, fv, name)
+    def ts(out, in0, s1, o1, s2=None, o2=None, step=None):
+        V(cost1(out, in0), names(in0, s1, s2), [out],
+          lambda q, T: [q.tensor_scalar(ap(out)(T), ap(in0)(T), ap(s1)(T), None, o1) if o2 is None else q.tensor_scalar(ap(out)(T), ap(in0)(T), ap(s1)(T), ap(s2)(T), o1, o2)], step)
+
+    def act(out, in_, f, step=None, **kw):
+        S(v1(wid(out)), names(in_, *kw.values()), [out], lambda q, T: [q.activation(ap(out)(T), ap(in_)(T), f, **dict((k, ap(x)(T)) for k, x in kw.items()))], step)
+
+    def mm(terms, step=None, start=True, stop=True, more=(), whole=None):
+        cyc_n = sum(max(min(64, wid(a)), wid(b)) * (4 if SCRATCH[rng(a)[0]][2] == F32 else 1) for (o, a, b) in terms)
+        outs = [whole] if whole else [o for (o, a, b) in terms]
+        add("t", cyc_n * pec, [x for (o, a, b) in terms for x in (a, b)] + list(more) + ([] if start else outs), outs,
+            lambda q, T: [q.matmul(ap(o)(T), ap(a)(T), ap(b)(T), start and i == 0, stop and i == len(terms) - 1) for i, (o, a, b) in enumerate(terms)], step, k=len(terms))
+
+    def on_v(step): return step[0] in ON_V or step[0][:-1] in ON_V
+
+    def gather(out, win, off, step):
+        if on_v(step):
+            V(vg(wid(out)), [win, off], [out], lambda q, T: [q.tensor_copy(ap(out)(T), ap(win)(T).indirect(ap(off)(T)))], step)
         else:
-            S(ns, reads, writes, fs, name)
+            S(sg(wid(out)), [win, off], [out], lambda q, T: [q.activation(ap(out)(T), ap(win)(T).indirect(ap(off)(T)), AF.Copy)], step)
 
-    def dma(eng, cost, reads, writes, sem, fn, k=1): add(eng, cost, reads, writes, fn, sem, sem=sem, n=k)
-    dma("y", 2.0, [], [r("TI")], "ldt", lambda q, T: [q.dma_start(T.TI[:], T.tube[:])])
-    dma("y", 2.0, [], [r("wi")], "ldw", lambda q, T: [q.dma_start(T.wi[:], T.wt[:])])
-    dma("y", 2.0, [], [r("ki")], "ldk", lambda q, T: [q.dma_start(T.ki[:], T.kn[:])])
-    dma("y", 2.0, [], [r("li")], "ldl", lambda q, T: [q.dma_start(T.li[:, 0:5], T.lim[:])])
-    dma("y", 9.0, [], [r("X", 0, 4096)], "ldx", lambda q, T: [q.dma_start(T.X[:, 0:4096], T.field[:, 0:4096])])
-    dma("s", 9.0, [], [r("X", 4096, 8192)], "ldy", lambda q, T: [q.dma_start(T.X[:, 4096:8192], T.field[:, 4096:8192])])
-    def G(cost, reads, writes, fn): add("g", cost, reads, writes, fn)
-    V(v1(64), [], [r("ones")], fill("ones", 1.0))
-    G(0.4, [], [r("pI")], lambda q, T: [q.iota(T.pI[:], [[0, 1]], 0, 1)])
-    G(0.4, [], [r("v1i")], lambda q, T: [q.iota(T.v1i[:], [[256, 8]], 0, 0)])
-    G(0.4, [], [r("v2i")], lambda q, T: [q.iota(T.v2i[:], [[0, 2], [16, 8]], -128, 0)])
-    G(0.4, [], [r("v3i")], lambda q, T: [q.iota(T.v3i[:], [[512, 16]], 0, 0)])
-    G(0.6, [], [r("irow")], lambda q, T: [q.iota(T.irow[:], [[0, 8], [1, 16]], 0, 0, allow_small_or_imprecise_dtypes=True)])
-    G(0.6, [], [r("grow")], lambda q, T: [q.iota(T.grow[:], [[16384, 8], [0, 16]], 0, 0, allow_small_or_imprecise_dtypes=True)])
-    V(tiny, [r("grow")], [r("grow")], lambda q, T: [q.tensor_scalar(T.grow[:], T.grow[:], 16.0, None, O.mult)])
-    G(0.5, [r("ones")], [r("BO1")], lambda q, T: [q.affine_select(T.BO1[:], T.ones[:], [[-16, 8], [0, 16]], O.is_ge, 0.0, 0, 1)])
-    G(0.5, [r("BO1")], [r("BO")], lambda q, T: [q.affine_select(T.BO[:], T.BO1[:], [[16, 8], [0, 16]], O.is_ge, 0.0, 15, -1)])
-    G(0.5, [r("ones")], [r("IB")], lambda q, T: [q.affine_select(T.IB[:], T.ones[:], [[-1, 128]], O.is_equal, 0.0, 0, 1)])
-    V(v1(256), [r("TI")], [r("LU0")], copy("LU0", "TI"))
-    V(v1(1024), [], [r("RB")], fill("RB", 0.0))
-    V(v1(64), [r("RB")], [r("RB")], fill(("RB", 0, 1024, 16), 256.0))
-    V(tiny, [r("pI")], [r("iI")], ts("iI", "pI", 15, O.bitwise_and))
-    V(tiny, [r("iI")], [r("icol")], copy("icol", "iI"))
-    V(tiny, [r("wi")], [r("wc")], copy("wc", "wi"))
-    V(tiny, [r("ki")], [r("kc")], copy("kc", "ki"))
-    V(tiny, [r("li")], [r("lf")], copy(("lf", 0, 5), ("li", 0, 5)))
-    V(tiny, [r("lf")], [r("nl")], ts(("nl", 0, 5), ("lf", 0, 5), -1.0, O.mult, 0.5, O.add))
-    V(tiny, [r("nl")], [r("nth", 0, 1)], copy(("nth", 0, 1), ("nl", 0, 1)))
-    V(tiny, [r("lf")], [r("thv", 0, 1)], copy(("thv", 0, 1), ("lf", 0, 1)))
-    V(tiny, [r("icol")], [r("ige1")], ts("ige1", "icol", 1.0, O.is_ge))
-    V(tiny, [r("icol")], [r("e15")], ts("e15", "icol", 15.0, O.is_equal))
-    V(tiny, [r("ige1")], [r("pthr")], ts("pthr", "ige1", 102.0, O.mult, -101.0, O.add))
-    V(tiny, [r("ige1")], [r("pthv")], ts("pthv", "ige1", 109.5, O.mult, -101.0, O.add))
-    V(v1(1024), [], [r("sel")], fill("sel", 0.0))
-    for gg in range(8):
-        V(tiny, [r("BO")], [r("sel")], copy(("sel", 16 * gg, 16 * gg + 129 * 15 + 1, 129), ("BO", 16 * gg, 16 * gg + 16)))
-    V(tiny, [r("icol")], [r("i16")], ts("i16", "icol", 16.0, O.mult))
-    V(tiny, [r("i16"), r("v1i")], [r("VB")], ts("VB", "v1i", "i16", O.add))
-    V(v1(128), [r("BO")], [r("BOf")], copy("BOf", "BO"))
-    V(v1(128), [r("BO")], [r("BOf256")], ts("BOf256", "BO", 256.0, O.mult))
-    G(0.5, [r("BO")], [r("BOd")], lambda q, T: [q.affine_select(T.BOd[:], T.BO[:], [[-1, 128]], O.is_equal, 0.0, -1, 1)])
-    V(v1(256), [r("IB"), r("BOd")], [r("OHm")], tt("OHm", "IB", "BOd", O.subtract))
-    V(tiny, [], [r("c64", 0, 1)], lambda q, T: [q.memset(T.c64[0:32, :], -64.0)])
-    V(tiny, [], [r("c64", 1, 2)], lambda q, T: [q.memset(T.c64[32:64, :], 1.0 / 64)])
-    V(v1(128), [r("IB")], [r("IF")], copy("IF", "IB"))
-    V(tiny, [r("kc")], [r("k2")], ts("k2", "kc", -256.0, O.add))
-    V(tiny, [r("k2")], [r("sqb")], ts("sqb", "k2", 2.0, O.mult, 511.875, O.add))
-    V(tiny, [r("k2")], [r("k3")], ts("k3", "k2", "k2", O.mult, -4.0, O.mult))
-    V(tiny, [r("k3")], [r("k4")], ts("k4", "k3", -128.25, O.add))
-    V(v1(2048), [], [r("ZS")], fill("ZS", 0.0))
-    V(v1(512), [], [r("R01")], fill("R01", 1.0))
-    V(v1(64), [r("R01")], [r("R01")], fill(("R01", 0, 1024, 16), 0.0))
-    V(vh(2048), [r("sel")], [r("sel128")], ts("sel128", "sel", 128.0, O.mult))
-    V(tiny, [r("icol"), r("v2i")], [r("VW")], ts("VW", "v2i", "icol", O.add))
-    V(tiny, [r("BO")], [r("blk32")], ts("blk32", ("BO", 0, 128, 16), 32.0, O.mult))
-    V(tiny, [r("BO")], [r("blkn")], ts("blkn", ("BO", 0, 128, 16), -16.0, O.mult))
-    V(v1(64), [], [r("RK")], fill("RK", 0.0))
-    V(tiny, [r("RK")], [r("RK")], fill(("RK", 0, 128, 16), 8388608.0))
-    for c in range(2):
-        V(tiny, [], [r("KM%d" % c, 128, 144)], fill(("KM%d" % c, 128, 144), 8388608.0))
-    V(vh(128), [r("IB"), r("ige1")], [r("pIm")], ts("pIm", "IB", "ige1", O.mult))
-    V(vh(128), [r("pIm")], [r("nIm")], ts("nIm", "pIm", -1.0, O.mult))
-    V(v1(128), [r("sel")], [r("Sel0")], copy("Sel0", ("sel", 0, 128)))
-    V(vh(2048), [r("sel"), r("icol")], [r("isel")], ts("isel", "sel", "icol", O.mult))
-    V(vh(2048), [r("sel"), r("wc")], [r("wsel")], ts("wsel", "sel", "wc", O.mult))
-    V(tiny, [r("icol")], [r("i32c")], ts("i32c", "icol", 32.0, O.mult))
-    V(tiny, [r("v3i"), r("i32c")], [r("SOp")], ts("SOp", "v3i", "i32c", O.add))
-    V(v1(64), [], [r("half")], fill("half", 0.5))
-    V(vh(128), [r("ones"), r("e15")], [r("S15")], ts("S15", "ones", "e15", O.mult))
-    for c in range(2):
-        S(v1(2048), [r("ZS")], [r("W", 2048 * c, 2048 * c + 2048)], act(("W", 2048 * c, 2048 * c + 2048), ("ZS", 2048 * c, 2048 * c + 2048), AF.Copy))
+    def gadd(out, win, off, b, step): V(vg(wid(out)), [win, off, b], [out], lambda q, T: [q.tensor_tensor(ap(out)(T), ap(win)(T).indirect(ap(off)(T)), ap(b)(T), O.add)], step)
+    def move(out, in_, step): (copy(out, in_, step) if on_v(step) else act(out, in_, AF.Copy, step))
+    row = ("ones", 0, 128, 1, 0, 1)
 
-    C35 = 1.5 * 2.0 ** 35
+    dma("y", P["ldx"], [], [("X", 0, 4096)], "ldx", lambda q, T: [q.dma_start(T.X[:, 0:4096], T.field[:, 0:4096])])
+    dma("s", P["ldx"], [], [("X", 4096, 8192)], "ldy", lambda q, T: [q.dma_start(T.X[:, 4096:8192], T.field[:, 4096:8192])])
+    dma("y", 2.0, [], ["TI"], "ldt", lambda q, T: [q.dma_start(T.TI[:], T.tube[:])])
+    dma("y", 2.0, [], ["pri"], "ldp", lambda q, T: [q.dma_start(T.pri[:, 0:1], T.wt[:]), q.dma_start(T.pri[:, 1:2], T.kn[:]), q.dma_start(T.pri[:, 2:7], T.lim[:])], 3)
+    fill("ones", 1.0)
+    G(0.2, [], ["pI"], lambda q, T: [q.iota(T.pI[:], [[0, 1]], 0, 1)])
+    G(0.45, ["ones"], ["IB"], lambda q, T: [q.affine_select(T.IB[:], T.ones[:], [[-1, 128]], O.is_equal, 0.0, 0, 1)])
+    G(0.45, ["ones"], ["BO1"], lambda q, T: [q.affine_select(T.BO1[:], T.ones[:], [[-16, 8], [0, 16]], O.is_ge, 0.0, 0, 1)])
+    G(0.2, [], ["vbi"], lambda q, T: [q.iota(T.vbi[:], [[16, 16]], 0, 0)])
+    G(0.45, ["BO1"], ["BO"], lambda q, T: [q.affine_select(T.BO[:], T.BO1[:], [[16, 8], [0, 16]], O.is_ge, 0.0, 15, -1)])
+    G(0.4, [], ["grow"], lambda q, T: [q.iota(T.grow[:], [[16384, 8], [0, 16]], 4096, 0, allow_small_or_imprecise_dtypes=True)])
+    G(0.45, ["BO"], ["BOd"], lambda q, T: [q.affine_select(T.BOd[:], T.BO[:], [[-1, 128]], O.is_equal, 0.0, -1, 1)])
+    G(0.4, [], ["irow"], lambda q, T: [q.iota(T.irow[:], [[0, 8], [1, 16]], 0, 0, allow_small_or_imprecise_dtypes=True)])
+    for c in range(NC):
+        G(3.9, [], [("W", 2048 * c, 2048 * c + 2048)], lambda q, T, c=c: [q.iota(T.W[:, 2048 * c:2048 * c + 2048], [[0, 2048]], 0, 0, allow_small_or_imprecise_dtypes=True)])
+    rb = 16 * max(GP[0] + GP[1])
+    fill("sel", 0.0)
+    fill(("RB", 0, rb), 0.0)
+    fill("RK", 0.0)
+    fill("VW", 0.0)
+    ts("iI", "pI", 15, O.bitwise_and)
+    fill(("RB", 0, rb, 16), 256.0)
+    fill(("RK", 0, 128, 16), 8388608.0)
+    copy("icol", "iI")
+    fill("mh", -0.5)
+    fill("half", 0.5)
+    for c in range(NC):
+        fill(("KM%d" % c, 128, 144), 8388608.0)
+    if 0 in AU:
+        add("s", 16 * v1(128), ["IB"], ["Rep"], lambda q, T: [q.activation(T.Rep[:, i:2048:16], T.IB[:], AF.Copy, scale=-1.0) for i in range(16)], k=16)
+    act("IF", "IB", AF.Copy)
+    ts("ige1", "icol", 1.0, O.is_ge)
+    ts("e15", "icol", 15.0, O.is_equal, 128.0, O.mult)
+    ts("VS", "vbi", "icol", O.add)
+    add("v", 8 * tiny, ["BO", "sel"], ["sel"], lambda q, T: [q.tensor_copy(T.sel[:, 16 * h:16 * h + 129 * 15 + 1:129], T.BO[:, 16 * h:16 * h + 16]) for h in range(8)], k=8)
+    copy(("prm", 0, 7), ("pri", 0, 7))
+    copy("LU0", "TI")
+    ts("wq", ("prm", 0, 1), 1.0 / 4096, O.mult)
+    ts("k3", ("prm", 1, 2), ("prm", 1, 2), O.mult, -4.0, O.mult)
+    copy(("thv", 0, 1), ("prm", 2, 3))
+    ts("sqb", ("prm", 1, 2), 2.0, O.mult, 512.0, O.add)
+    act("wsel", "sel", AF.Copy, scale="wq")
+    act("Sel0", ("sel", 0, 128), AF.Copy)
+    ts("k4", "k3", -0.25, O.add)
+    ts("pth", "ige1", 109.5, O.mult, -101.0, O.add)
+    ts("pIm", "IB", "ige1", O.mult)
+    ts("S15", "ones", "e15", O.mult)
+    ts("VB", ("VS", 0, 8), 16.0, O.mult)
+    for c in range(NC):
+        ts(("VW", 16 * c, 16 * c + 8), ("VS", 0, 8), 16 - 1.0 / 128, O.mult)
+    ts("nIm", "pIm", -128.0, O.mult)
+    copy("BOh", "BO")
+    tt("BO1", "IB", "BOd", O.subtract)
+    ts("blk32", ("BO", 0, 128, 16), 32.0, O.mult)
+    ts("blk16", ("BO", 0, 128, 16), 16.0, O.mult)
+    ts("blkn", ("BO", 0, 128, 16), -16.0, O.mult)
+    ts("OHm", "BO1", 128.0, O.mult)
+    ts("grow", "grow", 16.0, O.mult)
+    ts("selh", "sel", 128.0, O.mult)
+
     C24 = 1.5 * 2.0 ** 24
-    nsel = [("sel", 128 * k, 128 * k + 128) for k in range(16)]
-    for t in range(RO):
-        last = t == RO - 1
-        LU, NU = "LU%d" % t, "NU%d" % t
+    def blocks(b): return [(b, 128 * k, 128 * k + 128) for k in range(16)]
+    def cuts(sizes): return [(sum(sizes[:p]), sum(sizes[:p + 1])) for p in range(len(sizes))]
+
+    def head(t, c):
+        LU, dl, pa, pb = "LU%d" % t, "DL%d" % c, "pa%d" % c, "pb%d" % c
+        a0, a1, c0, c1 = n * c, n * c + n, 16 * n * c, 16 * n * (c + 1)
+        def Q(x, lo=0, hi=n): return (x, a0 + lo, a0 + hi)
+        def Wd(x, lo=0, hi=n): return (x, c0 + 16 * lo, c0 + 16 * hi)
+        def st(x): return (x + "ab"[c], t)
         if t:
-            for c, (a0, n, pcs) in enumerate(CHUNKS):
-                add("x", P["hop"], [r("NU%d" % (t - 1), a0, a0 + n)], [r(LU, a0, a0 + n)], None, "arr", sem="arr%d%d" % (t, c))
-        for c, (a0, n, pcs) in enumerate(CHUNKS):
-            a1 = a0 + n
-            V(v1(n), [r(LU, a0, a1)], [r("L32", a0, a1)], copy(("L32", a0, a1), (LU, a0, a1)), "L32 c%d t%d" % (c, t))
-            S(v1(n), [r("L32", a0, a1), r("k4")], [r("LQ", a0, a1)], act(("LQ", a0, a1), ("L32", a0, a1), AF.Identity, bias="k4"), "LQ c%d t%d" % (c, t))
-            dl = "DL%d" % c
-            dma("y", 2.2, [r("L32", a0, a1)], [r(dl)], "dl%d" % c, lambda q, T, dl=dl, a0=a0, a1=a1: [q.dma_start(T[dl][:], T.L32[:, a0:a1])])
-            dma("y", P["wdma"], [r(dl)], [r("W", 16 * a0, 16 * a1)], "w%d" % c,
-                lambda q, T, dl=dl, a0=a0, a1=a1, n=n: [q.dma_start(T.W[j::16, 16 * a0 + n * j:16 * a1], T[dl][:, 1:17 - j, :]) for j in range(1, 16)], 15)
-        for c, (a0, n, pcs) in enumerate(CHUNKS):
-            c0, b0 = 16 * a0, "pb%d0" % (c % 2)
-            for p, (p0, pn) in enumerate(pcs):
-                lo, hi, m = c0 + 16 * p0, c0 + 16 * (p0 + pn), 16 * pn
-                u0, u1 = a0 + p0, a0 + p0 + pn
-                key = "c%d s%d" % (c, p)
-                pt = " %s t%d" % (key, t)
-                either("G " + key, vg(m), sg(m), [r("X"), r(LU, u0, u1)], [r("G", lo, hi)],
-                       gcopy(True, ("G", lo, hi), ("X", 0, 8192), (LU, u0, u1)), gcopy(False, ("G", lo, hi), ("X", 0, 8192), (LU, u0, u1)), "G" + pt)
-                V(vh(m), [r("G", lo, hi), r("RB")], [r("M", lo, hi)], scan(("M", lo, hi), ("RB", 0, m), ("G", lo, hi), O.max, O.min), "M" + pt)
-            for k in range(n // UNIT):
-                lo, hi, m = c0 + 16 * UNIT * k, c0 + 16 * UNIT * (k + 1), 16 * UNIT
-                u0, u1 = a0 + UNIT * k, a0 + UNIT * (k + 1)
-                key = "c%d u%d" % (c, k)
-                ut = " %s t%d" % (key, t)
-                if side("I " + key) == "s":
-                    S(v1(m), [r("M", lo, hi), r("nth", t, t + 1)], [r("H", lo, hi)], act(("H", lo, hi), ("M", lo, hi), AF.Sign, bias=("nth", t, t + 1)), "I" + ut)
-                    th = "pthr"
-                else:
-                    V(vh(m), [r("M", lo, hi), r("thv", t, t + 1)], [r("H", lo, hi)], ts(("H", lo, hi), ("M", lo, hi), ("thv", t, t + 1), O.is_ge), "I" + ut)
-                    th = "pthv"
-                sa = (b0, 256 + UNIT * k, 256 + UNIT * (k + 1))
-                PE(64 * 17, [r("G", lo, hi), r("wsel"), r("ones"), r("c64")], [r(*sa)],
-                   lambda q, T, sa=sa, lo=lo, hi=hi: [q.matmul(ap(sa)(T), T.ones[0:64, :], T.c64[:, 0:UNIT], True, False)] +
-                   [q.matmul(ap(sa)(T), T.wsel[:, 128 * j:128 * j + 128], T.G[:, lo + j:hi:16], False, j == 15) for j in range(16)], 17, "sa" + ut)
-                cn = (b0, UNIT * k, UNIT * (k + 1))
-                PE(64 * 16, [r("H", lo, hi), r("sel")], [r(*cn)], mm(cn, [(nsel[j], ("H", lo + j, hi, 16)) for j in range(16)]), 16, "cnt" + ut)
-                V(v1(UNIT), [r(*cn), r(th)], [r("pas", u0, u1)], ts(("pas", u0, u1), cn, th, O.is_ge), "pass" + ut)
-            sa, ca, cb = (b0, 256, 256 + n), a0, a0 + n
-            V(v1(n), [r(*sa)], [r("B4", ca, cb)], ts(("B4", ca, cb), sa, C35, O.add, -C35, O.add), "B4 c%d t%d" % (c, t))
-            V(v1(n), [r(*sa), r("B4", ca, cb)], [r("UA", ca, cb)], tt(("UA", ca, cb), sa, ("B4", ca, cb), O.subtract), "UA c%d t%d" % (c, t))
-        nwt = ("pk1", 384, 400)
-        PE(64 * 17, [r("pas"), r("sel128"), r("IB"), r("VW")], [r(*nwt)],
-           mm(nwt, [("IB", "VW")] + [(("sel128", 128 * k, 128 * k + 128), ("pas", k, 256, 16)) for k in range(16)]), 17, "nw t%d" % t)
-        V(tiny, [r(*nwt)], [r("OW")], copy("OW", nwt), "OW t%d" % t)
-        for k in range(2):
-            npk = ("pk0", 256 + 128 * k, 384 + 128 * k)
-            PE(256, [r("pas"), r("pIm"), r("nIm"), r("ones")], [r(*npk)], mm(npk, [("pIm", "ones"), ("nIm", ("pas", 128 * k, 128 * k + 128))]), 2, "np t%d" % t)
-        for c, (a0, n, pcs) in enumerate(CHUNKS):
-            a1, c0, c1, h0, h1 = a0 + n, 16 * a0, 16 * (a0 + n), a0 // 16, (a0 + n) // 16
-            b = c % 2
-            b0, b1, pk = "pb%d0" % b, "pb%d1" % b, "pk%d" % b
-            tag = " c%d t%d" % (c, t)
-            R = lambda x, a0=a0, a1=a1: r(x, a0, a1)
-            Q = lambda x, a0=a0, a1=a1: (x, a0, a1)
-            W = lambda x, c0=c0, c1=c1: r(x, c0, c1)
-            nbt = (b0, 128, 128 + n // 16)
-            PE(64 * 17, [R("pas"), r("sel"), r("IB"), r("VB")], [r(*nbt)],
-               mm(nbt, [("IB", ("VB", 0, n // 16))] + [(nsel[k], ("pas", a0 + k, a1, 16)) for k in range(16)]), 17, "nb" + tag)
-            V(tiny, [r(*nbt)], [r("OM", h0, h1)], ts(("OM", h0, h1), nbt, -1.0, O.add), "OM" + tag)
-            if not last:
-                either("XL c%d" % c, vg(n), sg(n), [W("G"), r("OM", h0, h1)], [R("XL")],
-                       gcopy(True, Q("XL"), ("G", c0, c1), ("OM", h0, h1)), gcopy(False, Q("XL"), ("G", c0, c1), ("OM", h0, h1)), "XL" + tag)
-            zs = ("ZS", c0, c1, 16)
-            either("Z c%d" % c, vg(n), sg(n), [W("M"), r("OM", h0, h1)], [W("ZS")],
-                   gcopy(True, zs, ("M", c0, c1), ("OM", h0, h1)), gcopy(False, zs, ("M", c0, c1), ("OM", h0, h1)), "Z" + tag)
-            f_, u_, q_ = (b1, 384, 384 + n), (b1, 0, n), (b1, 256, 256 + n)
-            PE(n, [R("pas"), r("OHm")], [r(*f_)], mm(f_, [("OHm", Q("pas"))]), 1, "oneh" + tag)
-            V(v1(n), [r(*f_), R("UA")], [R("UO")], tt(Q("UO"), f_, Q("UA"), O.mult), "UO" + tag)
-            PE(4 * n, [R("UO"), r("BOf")], [r(*u_)], mm(u_, [("BOf", Q("UO"))]), 1, "u" + tag)
-            S(v1(n), [r(*u_), r("sqb")], [R("SQ")], act(Q("SQ"), u_, AF.Square, bias="sqb", scale=0.25), "SQ" + tag)
-            PE(8 * n, [R("UO"), r("BOf256"), r("IF"), R("LQ")], [r(*q_)], mm(q_, [("IF", Q("LQ")), ("BOf256", Q("UO"))]), 2, "q" + tag)
-            V(v1(n), [r(*q_), R("SQ")], [R("xI")], tt(Q("xI"), q_, Q("SQ"), O.add), "x" + tag)
-            V(v1(n), [R("xI")], [R("cI")], ts(Q("cI"), Q("xI"), 8191, O.bitwise_and), "and" + tag)
-            V(v1(n), [R("cI")], [R("CU")], copy(Q("CU"), Q("cI")), "CU" + tag)
-            first = []
-            for p, (p0, pn) in enumerate(pcs):
-                lo, hi, m = c0 + 16 * p0, c0 + 16 * (p0 + pn), 16 * pn
-                u0, u1 = a0 + p0, a0 + p0 + pn
-                key = "c%d s%d" % (c, p)
-                pt = " %s t%d" % (key, t)
-                D, A, z16, d16, sv = ("D", lo, hi), ("A", lo, hi), ("ZS", lo, hi, 16), ("D", lo, hi, 16), ("sv", u0, u1)
-                if not last:
-                    f = 2.0 if side("C " + key) == "v" else 1.0
-                    either("Z2 " + key, v1(pn), v1(pn), [r("ZS", lo, hi)], [r("Z2", u0, u1)],
-                           ts(("Z2", u0, u1), z16, f, O.mult, -0.5, O.add), act(("Z2", u0, u1), z16, AF.Copy, bias=-0.5, scale=f), "Z2" + pt)
-                V(vh(m), [r("ZS", lo, hi), r("R01")], [r("Zx", lo, hi)], scan(("Zx", lo, hi), ("R01", 0, m), ("ZS", lo, hi), O.mult, O.add), "Zx" + pt)
-                D0 = r("D0", lo, hi)
-                if side("C " + key) == "v":
-                    V(vg(m), [r("X"), r("CU", u0, u1), r("Zx", lo, hi)], [r(*D), D0], gtt(D, ("X", 0, 8192), ("CU", u0, u1), ("Zx", lo, hi), O.subtract), "D" + pt)
-                    first.append((p0, pn, d16, D0))
-                    either("A " + key, vh(m), v1(m), [r(*D), D0], [r(*A)], ts(A, D, 0.0, O.max), act(A, D, AF.Relu), "A" + pt)
-                else:
-                    S(sg(m), [r("X"), r("CU", u0, u1)], [r(*D), D0], gcopy(False, D, ("X", 0, 8192), ("CU", u0, u1)), "D" + pt)
-                    S(v1(pn), [D0], [r(*sv)], act(sv, d16, AF.Copy), "sv" + pt)
-                    first.append((p0, pn, sv, r(*sv)))
-                    V(v1(2 * pn), [r("ZS", lo, hi), r(*sv)], [D0], tt(d16, sv, z16, O.max), "fx" + pt)
-                    V(vh(m), [r(*D), D0, r("Zx", lo, hi)], [r(*A)], scan(A, ("Zx", lo, hi), D, O.min, O.max), "A" + pt)
-                    S(v1(pn), [r(*sv), r(*A)], [D0], act(d16, sv, AF.Copy), "rs" + pt)
+            add("x", P["hop"], [Q("NU%d" % (t - 1))], [Q(LU)], None, st("arr"), sem="arr%d%d" % (t, c))
+        def s1(x): return st(x) if t else None
+        copy(Q("L32"), Q(LU), s1("L32"))
+        act(Q("LQ"), Q("L32"), AF.Identity, s1("LQ"), bias="k4")
+        dma("y", 2.2, [Q("L32")], [dl], "dl%d" % c, lambda q, T: [q.dma_start(T[dl][:], T.L32[:, a0:a1])], 1, s1("dl"))
+        dma("y", P["wdma"], [dl], [Wd("W")], "w%d" % c,
+            lambda q, T: [q.dma_start(T.W[j::16, c0 + n * j:c1], T[dl][:, 1:17 - j, :]) for j in range(1, 16)], 15, s1("w"))
+        for p, (lo, hi) in enumerate(cuts(GP[c])):
+            gather(Wd("G", lo, hi), "X", Q(LU, lo, hi), st("Gp%d" % p))
+            scan(Wd("M", lo, hi), ("RB", 0, 16 * (hi - lo)), Wd("G", lo, hi), O.max, O.min, st("Mp%d" % p))
+        for k, (lo, hi) in enumerate(cuts([UNIT] * (n // UNIT))):
+            ends = [lo] + [y for (x, y) in cuts(GP[c]) if lo < y < hi and HP[c][k]] + [hi]
+            for p, (l, h) in enumerate(zip(ends, ends[1:])):
+                ts(Wd("H", l, h), Wd("M", l, h), ("thv", t, t + 1), O.is_ge, step=st("Hp%du%d" % (p, k)))
+            sa, cn, g0, g1 = (pa, 128 + lo, 128 + hi), (pa, lo, hi), c0 + 16 * lo, c0 + 16 * hi
+            mm([(sa, row, ("mh", 0, UNIT))] + [(sa, w, ("G", g0 + j, g1, 16)) for j, w in enumerate(blocks("wsel"))], st("sau%d" % k), more=[("G", g0, g1)])
+            mm([(cn, w, ("H", g0 + j, g1, 16)) for j, w in enumerate(blocks("sel"))], st("cntu%d" % k))
+            ts(("PU", 2 * a0 + lo, 2 * a0 + hi), cn, "pth", O.is_ge, 1.0 / 128, O.mult, st("passu%d" % k))
+        for k, (lo, hi) in enumerate(cuts([HU[c]] * (n // HU[c]))):
+            sa, f_, u_, q_ = (pa, 128 + lo, 128 + hi), (pb, lo, hi), (pb, 128 + lo, 128 + hi), (pb, 256 + lo, 256 + hi)
+            pas, uo = ("PU", 2 * a0 + lo, 2 * a0 + hi), ("PU", 2 * a0 + n + lo, 2 * a0 + n + hi)
+            ts(Q("KQ", lo, hi), sa, 1.0 / 8192, O.add, step=st("KQu%d" % k))
+            tt(Q("UA", lo, hi), sa, Q("KQ", lo, hi), O.subtract, st("UAu%d" % k))
+            mm([(f_, "OHm", pas)], st("onehu%d" % k))
+            tt(uo, f_, Q("UA", lo, hi), O.mult, st("UOu%d" % k))
+            mm([(u_, "BOh", uo)], st("uu%d" % k))
+            act(q_, u_, AF.Square, st("SQu%d" % k), bias="sqb", scale=1024.0)
+            tt(Q("xI", lo, hi), q_, Q("LQ", lo, hi), O.add, st("xu%d" % k))
+            ts(Q("cI", lo, hi), Q("xI", lo, hi), 8191, O.bitwise_and, step=st("andu%d" % k))
+            copy(Q("CU", lo, hi), Q("cI", lo, hi), st("CUu%d" % k))
+        both, nbt = ("pc0", 256 + 16 * c, 272 + 16 * c), ("pc0", 256 + 16 * c, 264 + 16 * c)
+        mm([(both, w, ("PU", 2 * a0 + k, 2 * a1, 16)) for k, w in enumerate(blocks("selh"))] + [(nbt, "IB", "VB")], st("nb"))
+        ts(("OM", 8 * c, 8 * c + 8), nbt, -1.0, O.add, step=st("OM"))
+        gather(Q("Zb"), Wd("M"), ("OM", 8 * c, 8 * c + 8), st("Z"))
+        zt = ("pc%d" % c, 288, 288 + n)
+        if AU[c]:
+            mm([((pb, 0, n), "IB", Q("Zb"))], st("Zp"))
+        else:
+            mm([(zt, Q("Zb"), "IB")], st("Zp"))
+            move(Q("ZT"), zt, st("ZT"))
+        mm([(("pc%d" % c, 0, n), "pIm", "ones"), (("pc%d" % c, 0, n), "nIm", ("PU", 2 * a0, 2 * a0 + n))], st("np"))
 
-            def key0(q, T, c0=c0, c1=c1, n=n, pk=pk, first=first):
-                o = [q.matmul(T[pk][0:n, 0:128], T.ones[0:1, 0:n], T.irow[:], True, False), q.matmul(T[pk][0:n, 0:128], T.ones[0:1, 0:n], T.grow[:], False, False)]
-                o += [q.matmul(T[pk][0:n, i:128:16], T.D[:, c0 + i:c1:16], T.blkn[:], False, False) for i in range(1, 16)]
-                return o + [q.matmul(T[pk][p0:p0 + pn, 0:128:16], ap(x)(T), T.blkn[:], False, False) for (p0, pn, x, _) in first]
+    def middle(t):
+        nb = ("pc0", 256, 288)
+        tt("nw", nb, "VW", O.subtract, ("nwb", t))
+        ts("OW", "nw", 128.0, O.mult, -128.0, O.add, ("OWb", t))
+        if t < RO - 1:
+            ts("k2", nb, -31.0 / 64, O.add, step=("k2b", t))
+            tt("rr", nb, "k2", O.subtract, ("rrb", t))
 
-            def key1(q, T, c0=c0, c1=c1, n=n, pk=pk):
-                return [q.matmul(T[pk][0:n, i:128:16], T.A[:, c0 + i:c1:16], T.blk32[:], False, i == 15) for i in range(16)]
-            PE(64 * 17 + 256, [W("D"), r("blkn"), r("irow"), r("grow"), r("ones")] + [f[3] for f in first], [r(pk, 0, 128)], key0, 17 + len(first), "key0" + tag)
-            PE(64 * 16, [W("A"), r("blk32"), r(pk, 0, 128)], [r(pk, 0, 128)], key1, 16, "key1" + tag)
-            KM, KB, OH = "KM%d" % b, "KB%d" % b, "OH%d" % b
-
-            def rows(x, lo=0, hi=128, st=1, n=n): return lambda T: T[x][0:n, lo:hi:st] if st > 1 else T[x][0:n, lo:hi]
-            V(v1(128), [r(pk, 0, 128), r("RK")], [r(KM, 0, 128)], lambda q, T, n=n, KM=KM, pk=pk: [q.tensor_tensor_scan(T[KM][0:n, 0:128], T.RK[0:n, :], T[pk][0:n, 0:128], 0.0, O.max, O.min)], "KM" + tag)
-            V(v1(128), [r(KM), r("RK")], [r(KB)], lambda q, T, n=n, KM=KM, KB=KB: [q.tensor_tensor_scan(T[KB][0:n, :], T.RK[0:n, :], T[KM][0:n, 15:143], 0.0, O.max, O.min)], "KB" + tag)
-            V(v1(128), [r(pk, 0, 128), r(KB)], [r(OH)], lambda q, T, n=n, KB=KB, pk=pk, OH=OH: [q.tensor_tensor(T[OH][0:n, :], T[pk][0:n, 0:128], T[KB][0:n, :], O.is_equal)], "OH" + tag)
-            oh = (b0, 384, 384 + n)
-            PE(n, [r(OH), r("IB")], [r(*oh)], lambda q, T, n=n, OH=OH, oh=oh: [q.matmul(ap(oh)(T), T[OH][0:n, :], T.IB[0:n, 0:n], True, True)], 1, "OHA" + tag)
-            if not last:
-                either("OHA c%d" % c, v1(n), v1(n), [r(*oh)], [R("OHA")], copy(Q("OHA"), oh), act(Q("OHA"), oh, AF.Copy), "OHAe" + tag)
-                tot = (b1, 128, 128 + n // 16)
-                PE(64 * 17, [R("OHA"), r("isel"), r("IB"), r("VB")], [r(*tot)],
-                   mm(tot, [("IB", ("VB", 0, n // 16))] + [(("isel", 128 * k, 128 * k + 128), ("OHA", a0 + k, a1, 16)) for k in range(16)]), 17, "to" + tag)
-                V(tiny, [r(*tot)], [r("OT", h0, h1)], copy(("OT", h0, h1), tot), "OT" + tag)
-                V(vg(n), [W("D"), W("D0"), r("OT", h0, h1), R("Z2")], [R("tt")], gtt(Q("tt"), ("D", c0, c1), ("OT", h0, h1), Q("Z2"), O.add), "tt" + tag)
-                V(v1(n), [R("tt")], [R("Y2")], ts(Q("Y2"), Q("tt"), C24, O.add, -C24, O.add), "Y2" + tag)
-            np_, nl_ = ("pk0", 256 + a0, 256 + a1), ("pb%d2" % b, 0, n)
-            V(vg(n), [W("W"), r("OW", h0, h1), R("pas")], [R("R1")], gtt(Q("R1"), ("W", c0, c1), ("OW", h0, h1), Q("pas"), O.mult), "R1" + tag)
-            V(v1(n), [r(*np_), R("cI")], [R("C1")], tt(Q("C1"), np_, Q("cI"), O.mult), "C1" + tag)
-            V(v1(n), [r(*oh), R("cI")], [R("OC")], tt(Q("OC"), oh, Q("cI"), O.mult), "OC" + tag)
-            PE(8 * n, [R("R1"), R("C1"), r("IF")], [r(*nl_)],
-               lambda q, T, x=Q("R1"), y=Q("C1"), o=nl_: [q.matmul(ap(o)(T), T.IF[:], ap(x)(T), True, False), q.matmul(ap(o)(T), T.IF[:], ap(y)(T), False, False)], 2, "nl0" + tag)
-            PE(4 * n, [R("OC"), r("Sel0"), r(*nl_)], [r(*nl_)], lambda q, T, x=Q("OC"), o=nl_: [q.matmul(ap(o)(T), T.Sel0[:], ap(x)(T), False, True)], 1, "nl1" + tag)
-            if not last:
-                V(v1(n), [r(*nl_)], [R(NU)], copy(Q(NU), nl_), "NU" + tag)
-                add("g", 0.5, [R(NU)], [], ("send", t, c), "send" + tag, sem="sent")
+    def tail(t, c):
+        last = t == RO - 1
+        NU, pc, pk = "NU%d" % t, "pc%d" % c, "pk%d" % c
+        a0, a1, c0, c1, h0, h1 = n * c, n * c + n, 16 * n * c, 16 * n * (c + 1), 8 * c, 8 * c + 8
+        def Q(x, lo=0, hi=n): return (x, a0 + lo, a0 + hi)
+        def Wd(x, lo=0, hi=n): return (x, c0 + 16 * lo, c0 + 16 * hi)
+        def st(x): return (x + "ab"[c], t)
+        key = (pk, 0, 128)
+        mm([(key, row, "irow"), (key, row, "grow")], st("keyc"), stop=False, whole=(pk, 0, 512))
+        for p, (lo, hi) in enumerate(cuts(DP[c])):
+            gather(Wd("D", lo, hi), "X", Q("CU", lo, hi), st("Dp%d" % p))
+        if AU[c]:
+            for k, (lo, hi) in enumerate(cuts([AU[c]] * (n // AU[c]))):
+                for i0 in range(0, 16, KG):
+                    zk = ("pb%d" % c, lo, hi)
+                    io = [(("A", c0 + n * i + lo, c0 + n * i + hi), ("D", c0 + 16 * lo + i, c0 + 16 * hi, 16)) for i in range(i0, i0 + KG)]
+                    add("v", KG * v1(hi - lo), [Wd("D", lo, hi), zk], [o for (o, d) in io],
+                        lambda q, T, io=io, zk=zk: [q.tensor_tensor(ap(o)(T), ap(d)(T), ap(zk)(T), O.max) for (o, d) in io], st("Au%di%d" % (k, i0)), k=KG)
+            mm([((pk, i, 128, 16), ("D", c0 + i, c1, 16), "blkn") for i in range(16)], st("kl"), False, False, [Wd("D")], key)
+            for i0 in range(0, 16, KG):
+                mm([((pk, i, 128, 16), ("A", c0 + n * i, c0 + n * i + n), "blk32") for i in range(i0, i0 + KG)], st("key%d" % i0), False, i0 + KG == 16, [], key)
+        for p, (lo, hi) in enumerate(cuts(DP[c]) if not AU[c] else []):
+            df = (DB[c][p % len(DB[c])], 0, 16 * (hi - lo))
+            mm([(df, Q("ZT"), ("Rep", 16 * lo, 16 * hi))], st("dz%d" % p), stop=False, whole=(df[0], 0, 512))
+            mm([(df, "IB", Wd("D", lo, hi))], st("dx%d" % p), start=False)
+            if on_v(st("A%d" % p)):
+                ts(Wd("A", lo, hi), df, 0.0, O.max, 2.0, O.mult, st("A%d" % p))
+                mm([((pk, i, 128, 16, lo, hi), ("D", c0 + 16 * lo + i, c0 + 16 * hi, 16), "blkn") for i in range(16)], st("kl%d" % p), False, False, [Wd("D", lo, hi)], key)
             else:
-                S(v1(n), [r(*nl_)], [R("yls")], act(Q("yls"), nl_, AF.Copy), "yls" + tag)
-                dma("y", 2.0, [R("yls")], [], "ol%d" % c, lambda q, T, x=Q("yl"), y=Q("yls"): [q.dma_start(ap(x)(T), ap(y)(T))])
-                S(v1(n), [W("ZS")], [R("yzs")], act(Q("yzs"), zs, AF.Copy), "yzs" + tag)
-                dma("y", 2.0, [R("yzs")], [], "oz%d" % c, lambda q, T, x=Q("yz"), y=Q("yzs"): [q.dma_start(ap(x)(T), ap(y)(T))])
+                act(Wd("A", lo, hi), df, AF.Abs, st("A%d" % p))
+        for p, (lo, hi) in enumerate(cuts(KP[c]) if not AU[c] else []):
+            mm([((pk, i, 128, 16, lo, hi), ("A", c0 + 16 * lo + i, c0 + 16 * hi, 16), "blk16") for i in range(16)], st("key%d" % p), False, True, [Wd("A", lo, hi)], key)
+        KM, KB, OH = "KM%d" % c, "KB%d" % c, "OH%d" % c
+        scan((KM, 0, 128), "RK", key, O.max, O.min, st("KM"))
+        scan(KB, "RK", (KM, 15, 143), O.max, O.min, st("KB"))
+        tt(OH, key, KB, O.is_equal, st("OH"))
+        oh, np_, nl_ = (pk, 128, 128 + n), (pc, 0, n), (pc, 128, 128 + n)
+        mm([(oh, OH, "IB")], st("oh"))
         if not last:
-            tag = " t%d" % t
-            sb = ("pb11", 144, 160)
-            PE(64 * 16, [r("XL"), r("wsel")], [r(*sb)], mm(sb, [(("wsel", 128 * k, 128 * k + 128), ("XL", k, 256, 16)) for k in range(16)]), 16, "sb" + tag)
-            V(tiny, [r(*sb)], [r("soA")], copy("soA", sb), "soA" + tag)
-            V(tiny, [r("soA")], [r("soB")], ts("soB", "soA", 31, O.bitwise_and), "soB" + tag)
-            V(tiny, [r("soB"), r("SOp")], [r("soC")], tt("soC", "soB", "SOp", O.add), "soC" + tag)
-            V(tiny, [r("soC")], [r("SO")], copy("SO", "soC"), "SO" + tag)
-            eb = ("pb11", 192, 256)
-            PE(64 * 4, [r("pas"), r("S15")], [r(*eb)], mm(eb, [("S15", ("pas", 64 * k, 64 * k + 64)) for k in range(4)]), 4, "E" + tag)
-            V(tiny, [r(*eb)], [r("er")], lambda q, T: [q.tensor_reduce(T.er[:], T.pb11[:, 192:256], AxisListType.X, O.add, negate=True)], "er" + tag)
-            V(tiny, [r("er")], [r("eI")], copy("eI", "er"), "eI" + tag)
-            V(tiny, [r("eI")], [r("eJ")], ts("eJ", "eI", 7, O.bitwise_and), "eJ" + tag)
-            n1 = (t + 1, t + 2)
-            who = [side("I c%d u%d" % (c, k)) for c, (a0, n, pcs) in enumerate(CHUNKS) for k in range(n // UNIT)]
-            if "s" in who:
-                V(tiny, [r("eJ"), r("nl")], [r("nth", *n1)], tt(("nth",) + n1, ("nl",) + n1, "eJ", O.subtract), "nth" + tag)
-            if "v" in who:
-                V(tiny, [r("eJ"), r("lf")], [r("thv", *n1)], tt(("thv",) + n1, ("lf",) + n1, "eJ", O.add), "thv" + tag)
-            for c, (a0, n, pcs) in enumerate(CHUNKS):
-                h0, h1 = a0 // 16, (a0 + n) // 16
-                V(0.055 + 3.5 * n * cyc, [r("Y2", a0, a0 + n), r("half"), r("SO")], [r("X")],
-                  lambda q, T, y=("Y2", a0, a0 + n), h=("half", 0, n), o=("SO", h0, h1): [q.tensor_tensor(T.X[:, 0:8192].indirect(ap(o)(T)), ap(y)(T), ap(h)(T), O.mult)], "scat c%d" % c + tag)
+            if on_v(st("OHA")):
+                ts(Q("OHA"), oh, "icol", O.mult, step=st("OHA"))
+            else:
+                act(Q("OHA"), oh, AF.Copy, st("OHA"), scale="icol")
+            tot, ot = (pk, 256, 264), ("OT", h0, h1)
+            mm([(tot, "IB", "VB")] + [(tot, w, ("OHA", a0 + k, a1, 16)) for k, w in enumerate(blocks("sel"))], st("to"))
+            copy(ot, tot, st("OT"))
+            if on_v(st("tt")):
+                act(Q("Z2"), Q("Zb"), AF.Copy, st("Z2"), bias=-0.5)
+                gadd(Q("tt"), Wd("D"), ot, Q("Z2"), st("tt"))
+                yp = Q("tt")
+            else:
+                yp = (pk, 264, 264 + n)
+                gather(Q("XB"), Wd("D"), ot, st("tt"))
+                mm([(yp, row, "mh"), (yp, "IB", Q("Zb")), (yp, "IB", Q("XB"))], st("yp"))
+            ts(Q("Y2"), yp, C24, O.add, -C24, O.add, st("Y2"))
+        tt(Q("C1"), np_, Q("cI"), O.mult, st("C1"))
+        tt(Q("OC"), oh, Q("cI"), O.mult, st("OC"))
+        ow = ("OW", 16 * c, 16 * c + 8)
+        if on_v(st("RC")):
+            gadd(Q("RC"), Wd("W"), ow, Q("C1"), st("RC"))
+            mm([(nl_, "IF", Q("RC"))], st("nl0"), stop=False, more=[(pc, 256, 512)])
+        else:
+            gather(Q("RC"), Wd("W"), ow, st("RC"))
+            mm([(nl_, "IF", Q("C1")), (nl_, "IF", Q("RC"))], st("nl0"), stop=False, more=[(pc, 256, 512)])
+        mm([(nl_, "Sel0", Q("OC"))], st("nl1"), start=False, more=[(pc, 256, 512)])
+        if not last:
+            copy(Q(NU), nl_, st("NU"))
+            add("g", 0.5, [Q(NU)], [], ("send", t, c), st("send"), sem="sent")
+        else:
+            act(Q("yls"), nl_, AF.Copy, st("yls"))
+            dma("y", 2.0, [Q("yls")], [], "ol%d" % c, lambda q, T: [q.dma_start(T.yl[:, a0:a1], T.yls[:, a0:a1])], 1, st("ol"))
+            act(Q("yzs"), Q("Zb"), AF.Copy, st("yzs"))
+            dma("y", 2.0, [Q("yzs")], [], "oz%d" % c, lambda q, T: [q.dma_start(T.yz[:, a0:a1], T.yzs[:, a0:a1])], 1, st("oz"))
+
+    def close(t):
+        so, eb = (SB, 416, 432), (SB, 448, 512)
+        mm([(so, "IB", "VS")] + [((SB, 416 + 8 * c, 424 + 8 * c), "IB", ("rr", 16 * c + 8, 16 * c + 16)) for c in range(NC)], ("sob", t), whole=so)
+        ts("SO", so, 32.0, O.mult, step=("SOb", t))
+        mm([(eb, "S15", ("PU", 2 * n * c + k, 2 * n * c + k + 64)) for c in range(NC) for k in (0, 64)], ("Eb", t))
+        V(tiny, [eb], ["er"], lambda q, T: [q.tensor_reduce(T.er[:], ap(eb)(T), AxisListType.X, O.add, negate=True)], ("erb", t))
+        copy("eI", "er", ("eIb", t))
+        ts("eJ", "eI", 7, O.bitwise_and, step=("eJb", t))
+        tt(("thv", t + 1, t + 2), ("prm", 3 + t, 4 + t), "eJ", O.add, ("thvb", t))
+
+    def scatter(t, c):
+        V(0.055 + P["sc"] * n * cyc, [("Y2", n * c, n * c + n), "half", ("SO", 8 * c, 8 * c + 8)], ["X"],
+          lambda q, T: [q.tensor_tensor(T.X[:].indirect(T.SO[:, 8 * c:8 * c + 8]), T.Y2[:, n * c:n * c + n], T.half[:], O.mult)], ("scat" + "ab"[c], t))
+
+    for t in range(RO):
+        for c in range(NC):
+            head(t, c)
+        middle(t)
+        if t < RO - 1:
+            close(t)
+        for c in range(NC):
+            tail(t, c)
+        for c in range(NC if t < RO - 1 else 0):
+            scatter(t, c)
     return ops
 
 
@@ -366,91 +379,44 @@ def deps_of(ops):
         for (b, lo, hi) in o["reads"]:
             acc.setdefault(b, []).append((o["id"], lo, hi, False))
         o["deps"] = sorted((p, k) for (p, k) in d if p != o["id"])
-        o["banks"] = sorted(set(b for (b, lo, hi) in o["reads"] + o["writes"] if b.startswith("pb") or b.startswith("pk")))
+        o["banks"] = sorted(set(b for (b, lo, hi) in o["reads"] + o["writes"] if b in BANKS))
     return ops
 
 
-def schedule(ops):
+def step_of(o):
+    return o["step"]
+
+
+def order_of(ops, place, period):
     n = len(ops)
-    wake = P["wake"]
-    succ = [[] for _ in range(n)]
-    left = [0] * n
+    succ, left = [[] for _ in ops], [0] * n
     for o in ops:
         ps = set(p for (p, k) in o["deps"])
         left[o["id"]] = len(ps)
         for p in ps:
             succ[p].append(o["id"])
-    prio = [0.0] * n
-    for o in reversed(ops):
-        prio[o["id"]] = o["cost"] + max([prio[s] + wake for s in succ[o["id"]]], default=0.0) + PRI.get(o["name"].rsplit(" t", 1)[0], 0.0)
-    fin = [0.0] * n
-    start = [0.0] * n
-    avail = [0.0] * n
-    free = {"x": 0.0}
-    bank = {}
-    ready = [o["id"] for o in ops if left[o["id"]] == 0]
-    order = []
-    while ready:
-        cand = []
-        first = 1e9
-        for i in ready:
-            o = ops[i]
-            e = o["eng"]
-            st = max(avail[i], free.get(e, 0.0))
-            for b in o["banks"]:
-                for e2, f2 in bank.get(b, {}).items():
-                    if e2 != e and f2 + wake > st:
-                        st = f2 + wake
-            cand.append((st, -prio[i], i))
-            if st < first:
-                first = st
-        pr, st, i = min((p, s, j) for (s, p, j) in cand if s <= first + 0.03)
-        o = ops[i]
-        e = o["eng"]
-        start[i] = st
-        fin[i] = st + o["cost"]
-        if o["sem"] and e in ("y", "s"):
-            free[e] = st + 0.06 * o["n"]
-        elif e != "x":
-            free[e] = fin[i]
-        for b in o["banks"]:
-            bank.setdefault(b, {})[e] = fin[i]
-        order.append(i)
-        ready.remove(i)
-        for s in succ[i]:
-            left[s] -= 1
-            if left[s] == 0:
-                ready.append(s)
-                a = 0.0
-                for (p, k) in ops[s]["deps"]:
-                    if not (k == "war" and ops[p]["eng"] == ops[s]["eng"]):
-                        a = max(a, fin[p] + wake)
-                avail[s] = a
-    return order, start, fin
+    key = [place[o["step"][0]] + o["step"][1] * period if o["step"] else o["id"] - 10000 for o in ops]
+    order, held = [], {}
+    for i in sorted(range(n), key=lambda j: (key[j], j)):
+        stack = [i]
+        if left[i]:
+            held[i] = True
+            continue
+        while stack:
+            j = stack.pop()
+            order.append(j)
+            free = []
+            for s in succ[j]:
+                left[s] -= 1
+                if left[s] == 0 and s in held:
+                    free.append(s)
+            stack += sorted(free, key=lambda x: -key[x])
+    return order
 
 
-def free_steps():
-    out = []
-    for c, (a0, n, pcs) in enumerate(CHUNKS):
-        for p in range(len(pcs)):
-            out += ["%s c%d s%d" % (x, c, p) for x in ("G", "C", "A", "Z2")]
-        out += ["I c%d u%d" % (c, k) for k in range(n // UNIT)] + ["%s c%d" % (x, c) for x in ("Z", "XL", "OHA")]
-    return out
-
-
-def step_names():
-    keep, names = dict(PLACE), set()
-    for e in "sv":
-        for k in free_steps():
-            PLACE[k] = e
-        names |= set(o["name"].rsplit(" t", 1)[0] for o in build() if " t" in o["name"])
-    PLACE.clear()
-    PLACE.update(keep)
-    return sorted(names)
-
-
-PLACE.update(zip(free_steps(), SIDES))
-PRI.update((k, int(x) / 10) for k, x in zip(step_names(), RANKS.split()))
+def places():
+    w = CYCLE.split()
+    return {x.lstrip("+-"): (k / len(w) + {"+": 1, "-": -1}.get(x[0], 0)) * PERIOD for k, x in enumerate(w)}
 
 
 def rank_program(g, core, T, topo):
@@ -464,7 +430,7 @@ def rank_program(g, core, T, topo):
     ne = len(topo.engines(core, dst))
     ni = len(topo.engines(cores[(rank - 1) % len(cores)], core))
     ops = deps_of(build())
-    order = schedule(ops)[0]
+    order = order_of(ops, places(), PERIOD)
     queues = {"v": g.vector, "s": g.scalar, "t": g.tensor, "g": g, "y": g.sync}
     csem = {"v": "cv", "s": "cs", "t": "ct", "g": "cg"}
     total = {}
@@ -506,9 +472,9 @@ def rank_program(g, core, T, topo):
                     know[e][s2] = v2
         after[i] = dict(know[e])
         if isinstance(o["fn"], tuple):
-            _, t, c = o["fn"]
-            a0, n, _ = CHUNKS[c]
-            g.remote_dma(T["LU%d" % (t + 1)][:, a0:a0 + n], T["NU%d" % t][:, a0:a0 + n], T.sem["arr%d%d" % (t + 1, c)], T.sem["sent"], pid, rid, mask)
+            t, c = o["fn"][1:]
+            there, here = send_sides(o["fn"], T)
+            g.remote_dma(there, here, T.sem["arr%d%d" % (t + 1, c)], T.sem["sent"], pid, rid, mask)
             total["sent"] = total.get("sent", 0) + ne
             token[i] = ("sent", total["sent"])
         else:

@@ -1,8 +1,10 @@
 from concourse.mybir import AluOpType, AxisListType, ActivationFunctionType
 
 RO = 5
+TWO = 0
 NC, NT = 2, 128
-UNIT = 64
+UN = [64, 64]
+LAST = 0
 GP = [[32, 32, 32, 32], [32, 32, 32, 32]]
 DP = [[32, 32, 32, 32], [32, 32, 32, 32]]
 HP = [[1, 1], [1, 1]]
@@ -11,23 +13,28 @@ AU, KG = [64, 0], 4
 KP = [[128], [96, 32]]
 DB = [["pa0", "pb0"], ["pa1", "pb1", "pa0", "pb1"]]
 SB = "pc1"
+SAB, OB, NBS = "pa", "pb", [0, 0]
+OH2 = ["", ""]
+SP = [64, 64]
+WP = [15]
 
 BF, F32, I32, U16, F16 = "bfloat16", "float32", "int32", "uint16", "float16"
-SCRATCH = {"irow": ("sbuf", [1, 128], BF), "grow": ("sbuf", [1, 128], BF), "mh": ("sbuf", [1, 128], BF)}
+SCRATCH = {"irow": ("sbuf", [1, 128], BF), "grow": ("sbuf", [1, 128], BF), "mh": ("sbuf", [1, 256], BF)}
 for _n, _w, _d in (
-        ("X", 8192, BF), ("TI", 256, I32), ("pri", 8, I32), ("prm", 8, F32), ("wq", 1, F32), ("sqb", 1, F32), ("k3", 1, F32), ("k4", 1, F32),
+        ("X", 8192, BF), ("TI", 256, I32), ("pri", 8, I32), ("prb", 8, BF), ("prm", 16, F32), ("wq", 2, F32), ("sqb", 2, F32), ("k3", 2, F32), ("k4", 2, F32),
+        ("X1", 8192, BF), ("SW", 128, BF), ("e128", 1, F32), ("v0", 8, BF), ("z2", 2, F32),
         ("pI", 1, I32), ("iI", 1, I32), ("icol", 1, F32), ("pth", 1, F32), ("ige1", 1, F32), ("e15", 1, F32),
         ("ones", 128, BF), ("BO1", 128, BF), ("BO", 128, BF), ("BOh", 128, F16), ("IB", 128, BF), ("IF", 128, F32),
         ("pIm", 128, BF), ("nIm", 128, F16), ("BOd", 128, BF), ("OHm", 128, F16), ("S15", 128, F16), ("Sel0", 128, F32),
-        ("sel", 2048, BF), ("wsel", 2048, BF), ("selh", 2048, F16), ("Rep", 2048, BF), ("blk16", 8, BF), ("blk32", 8, BF), ("blkn", 8, BF),
+        ("sel", 2048, BF), ("wsel", 4096, BF), ("selh", 2048, F16), ("Rep", 2048, BF), ("blk16", 8, BF), ("blk32", 8, BF), ("blkn", 8, BF),
         ("vbi", 16, I32), ("VB", 8, BF), ("VW", 32, F32), ("VS", 16, BF),
-        ("RB", 1024, BF), ("RK", 128, BF), ("half", 128, BF), ("W", 4096, F32),
-        ("er", 1, F32), ("eI", 1, I32), ("eJ", 1, I32), ("thv", 8, F32),
-        ("G", 4096, BF), ("M", 4096, BF), ("H", 4096, BF), ("D", 4096, BF), ("A", 4096, BF),
-        ("PU", 512, F16), ("OM", 16, U16), ("nw", 32, F32), ("OW", 32, U16), ("OT", 16, U16), ("SO", 16, U16), ("k2", 32, I32), ("rr", 32, BF),
+        ("RB", 1024, BF), ("RK", 128, BF), ("half", 256, BF), ("W", 4096, F32),
+        ("er", 1, F32), ("eI", 2, I32), ("eJ", 2, I32), ("thv", 16, F32),
+        ("G", 4096, BF), ("M", 4096, BF), ("H", 4096, BF), ("D", 4096, BF), ("A", 4096, BF), ("ZS", 2048, BF), ("Zx", 2048, BF), ("R01", 1024, BF), ("sv", 256, BF),
+        ("PU", 512, F16), ("OM", 16, U16), ("nw", 32, F32), ("OW", 32, U16), ("OT", 16, U16), ("SO", 32, U16), ("k2", 32, I32), ("rr", 32, BF),
         ("KQ", 256, I32), ("UA", 256, F16), ("LQ", 256, F32), ("Zb", 256, BF), ("ZT", 256, BF), ("XB", 256, BF),
         ("xI", 256, I32), ("cI", 256, I32), ("CU", 256, U16), ("L32", 256, F32), ("OHA", 256, BF),
-        ("OC", 256, F32), ("C1", 256, F32), ("RC", 256, F32), ("Y2", 256, BF), ("Z2", 256, F32), ("tt", 256, F32), ("yls", 256, F32), ("yzs", 256, F32)):
+        ("OC", 256, F32), ("C1", 256, F32), ("RC", 256, F32), ("Y2", 512, BF), ("Z2", 256, F32), ("tt", 256, I32), ("hIB", 128, BF), ("yls", 256, F32), ("yzs", 256, F32)):
     SCRATCH[_n] = ("sbuf", [128, _w], _d)
 for _c in range(NC):
     SCRATCH["DL%d" % _c] = ("dram", [8, 16, 128], F32)
@@ -42,14 +49,43 @@ for _t in range(RO):
         SCRATCH["NU%d" % _t] = ("sbuf", [128, 256], U16)
 BANKS = [_n for _n in SCRATCH if SCRATCH[_n][0] == "psum"]
 
-SEMAPHORES = ["cv", "cs", "ct", "cg", "sent", "ldp", "ldt", "ldx", "ldy"] + \
-    ["%s%d" % (a, c) for a in ("oz", "ol", "dl", "w") for c in range(NC)] + ["arr%d%d" % (t, c) for t in range(1, RO) for c in range(NC)]
+SEMAPHORES = ["cv", "cs", "ct", "cg", "sent", "ldp", "ldt", "ldx", "ldy", "ldz"] + \
+    ["%s%d" % (a, c) for a in ("oz", "ol", "dl") for c in range(NC)] + ["w%d%d" % (c, p) for c in range(NC) for p in range(4)] + ["arr%d%d" % (t, c) for t in range(1, RO) for c in range(NC)]
 
 P = {"cyc": 0.87e-3, "ga": 1.56, "sc": 3.8, "pec": 0.45e-3, "wake": 0.18, "hop": 3.5, "wdma": 6.0, "ldx": 8.0}
 ON_V = {"A3b", "RCa", "Gp1a", "Gp3a", "ttb", "Dp3b", "ZTb"}
 PERIOD = 20
 CYCLE = """
 Gp0a Gp1a L32a Gp2a sau0a Mp0a dla Mp1a Hp0u0a keycb Hp1u0a KQu0a Mp2a Gp1b cntu0a Gp3a Gp0b Hp0u1a passu0a UAu0a wa Mp3a onehu0a Gp2b sau1a Mp1b UOu0a Hp1u1a uu0a sau0b Mp0b LQa KQu1a SQu0a Hp1u0b Gp3b cntu1a Hp0u0b KQu0b xu0a L32b cntu0b andu0a passu1a LQb dlb UAu1a CUu0a Mp2b onehu1a sau1b Dp0a UOu1a Mp3b Hp0u1b uu1a npa nba UAu0b SQu1a KQu1b Dp1a passu0b Hp1u1b onehu0b xu1a OMa cntu1b UOu0b andu1a Za CUu1a C1a wb uu0b passu1b Zpa SQu0b UAu1b Dp2a Au0i4a onehu1b Eb npb UOu1b xu0b Au0i0a Dp3a nbb andu0b Au0i12a uu1b OMb SQu1b CUu0b Au1i0a Zb Dp1b xu1b Au1i8a Zpb kla andu1b ZTb key0a nwb Dp0b CUu1b Au1i4a dz1b dx1b Au0i8a dz2b yzsa Dp2b Au1i12a dz0b oza key4a Dp3b dx0b key8a A1b key12a dx2b k2b A0b OWb KMa kl3b RCa dz3b A2b KBa rrb dx3b OHa sob Z2b nl0a yzsb A3b oha key0b ozb erb OCa SOb key1b C1b OHAa eIb nl1a RCb eJb toa KMb ylsa NUa thvb KBb ola -arra senda nl0b OTa OHb tta ohb OCb ypa OHAb nl1b Y2a ylsb tob NUb olb scata sendb -arrb -keyca OTb ttb Y2b scatb
+"""
+ON_V = {"RCa", "RCb", "Gp1a", "Gp3a", "ttb", "Dp3b", "Dp1b"}
+AU, HU, DP, DB = [-1, 0], [64, 128], [[32, 32, 32, 32], [36, 24, 36, 32]], [["pa0", "pb0"], ["pa1", "pb1", "pa0", "pb0"]]
+CYCLE = """
+Gp0a Gp1a dla LQa Gp2a Mp0a sau0a Mp1a Hp0u0a Hp1u0a KQu0a Gp3a cntu0a wa Gp0b Mp2a Mp3a passu0a Gp1b UAu0a Hp0u1a onehu0a sau1a Hp1u1a L32b Mp0b Gp2b cntu1a dlb UOu0a Mp1b Hp0u0b uu0a sau0b Hp1u0b SQu0a Gp3b KQu1a xu0a cntu0b passu1a UAu1a andu0a Mp2b onehu1a CUu0a LQb sau1b Mp3b Dp0a UOu1a Hp0u1b wb npa Hp1u1b uu1a nba passu0b KQu0b SQu1a Dp1a xu1a cntu1b OMa andu1a CUu1a Za C1a passu1b sv0a Dp3a UAu0b fx0a onehu0b npb Eb UOu0b Zx1a uu0b nbb SQu0b Zx0a Dp2a xu0b OMb A0a yzsa Zb sv1a andu0b oza Zpb rs0a fx1a Z2b kl0a yzsb CUu0b ZTb A1a ozb Dp2b dz0b Dp1b dz1b key0a Dp0b Dp3b dx1b dz2b dx2b KMa A1b nwb dx0b KBa A2b OWb k2b dz3b OHa RCa A0b oha C1b dx3b OCa nl0a RCb A3b nl1a erb key0b eIb NUa OHAa ylsa rrb rs1a eJb key1b senda -arra ola thvb toa KMb KBb sob nl0b OTa OHb tta SOb ohb OCb ypa OHAb nl1b Y2a tob NUb ylsb scata -arrb sendb -keyca olb OTb ttb -keycb Y2b scatb -L32a
+"""
+ON_V = {"RCa", "RCb", "Gp1a", "Gp3a", "ttb", "Dp3b", "Dp1b", "OHAb"}
+GP, DP = [[36, 28, 36, 28], [32, 32, 32, 32]], [[32, 32, 32, 32], [32, 32, 32, 32]]
+CYCLE = """
+Gp0a Gp1a dla Mp1a Gp2a sau0a Mp0a Hp1u0a Hp0u0a LQa KQu0a Gp3a cntu0a wa Gp0b Mp2a UAu0a passu0a Mp3a sau1a Hp0u1a Gp1b Hp1u1a Mp0b onehu0a cntu1a UOu0a Gp2b L32b Mp1b dlb uu0a sau0b Hp0u0b Hp1u0b SQu0a Gp3b xu0a cntu0b passu1a KQu1a andu0a Mp2b onehu1a npa CUu0a LQb UAu1a sau1b Mp3b Dp0a UOu1a Hp0u1b uu1a Hp1u1b nba wb KQu0b SQu1a Dp1a passu0b xu1a cntu1b OMa andu1a CUu1a C1a Za passu1b sv0a Dp3a UAu0b fx0a onehu0b Eb UOu0b Zx1a uu0b nbb SQu0b Zx0a Dp2a npb xu0b OMb A0a sv1a Zb andu0b fx1a yzsa rs0a CUu0b Zpb Z2b yzsb A1a kl0a oza ZTb ozb Dp0b Dp1b dz2b key0a Dp2b Dp3b dz1b dx1b dz0b A1b KMa dx0b nwb dx2b KBa OWb A0b dz3b OHa k2b RCa A2b oha dx3b erb OCa nl0a C1b A3b nl1a RCb key0b eIb rs1a NUa ylsa OHAa rrb eJb key1b senda -arra ola thvb toa KMb KBb sob nl0b OTa OHb tta SOb ohb OCb ypa OHAb nl1b Y2a tob ylsb NUb scata olb sendb -arrb -keyca OTb -keycb ttb Y2b scatb -L32a
+"""
+WP = [5, 5, 5]
+CYCLE = """
+Gp0a Gp1a dla Mp1a Gp2a sau0a Mp0a Hp1u0a Hp0u0a LQa KQu0a Gp3a cntu0a Gp0b w0a Mp2a UAu0a passu0a Mp3a sau1a Gp1b Hp0u1a Hp1u1a Mp0b onehu0a cntu1a UOu0a L32b Gp2b w1a Mp1b uu0a sau0b Hp0u0b Hp1u0b SQu0a passu1a Gp3b KQu1a cntu0b xu0a UAu1a andu0a Mp2b onehu1a CUu0a npa dlb LQb UOu1a Dp0a Mp3b sau1b w2a Hp0u1b Hp1u1b uu1a nba KQu0b SQu1a Dp1a passu0b xu1a cntu1b OMa andu1a CUu1a Za C1a passu1b UAu0b sv0a Dp3a w0b onehu0b npb fx0a Eb UOu0b Zx1a uu0b nbb SQu0b Zx0a Dp2a xu0b OMb A0a w1b yzsa sv1a Zb andu0b fx1a rs0a CUu0b Zpb yzsb Z2b A1a kl0a ZTb Dp0b Dp1b dz2b key0a w2b Dp2b Dp3b dz1b dx1b dz0b rs1a A1b KMa dx0b nwb k2b dx2b KBa oza OWb A0b rrb dz3b OHa ozb RCa -arra oha A2b dx3b C1b OCa nl0a erb A3b nl1a eIb eJb key0b NUa ylsa OHAa thvb senda ola key1b RCb toa KMb KBb sob nl0b OTa OHb tta SOb ohb OCb ypa OHAb nl1b Y2a tob ylsb NUb scata olb sendb -arrb -keyca OTb ttb -keycb Y2b scatb -L32a
+"""
+CYCLE = """
+Gp0a Gp1a dla Mp1a LQa Gp2a sau0a Mp0a Hp1u0a Hp0u0a KQu0a Gp3a cntu0a Gp0b w1a Mp2a Mp3a UAu0a passu0a Gp1b Hp0u1a onehu0a sau1a Hp1u1a Mp0b UOu0a cntu1a L32b Gp2b Mp1b dlb Hp0u0b uu0a sau0b w0a Hp1u0b SQu0a KQu1a Gp3b passu1a cntu0b xu0a UAu1a andu0a Mp2b onehu1a CUu0a npa LQb UOu1a Dp0a Mp3b sau1b Hp0u1b w2a Hp1u1b uu1a nba KQu0b SQu1a Dp1a passu0b xu1a cntu1b OMa andu1a CUu1a Za C1a passu1b UAu0b sv0a w2b Dp3a onehu0b Eb fx0a npb UOu0b Zx0a uu0b nbb SQu0b Zx1a Dp2a xu0b OMb w0b A0a sv1a Zb andu0b fx1a yzsa CUu0b Zpb Z2b yzsb A1a kl0a rs0a ZTb Dp0b Dp1b dz2b w1b key0a Dp2b Dp3b dz1b dx1b dz0b A1b KMa dx0b nwb oza dz3b KBa k2b rs1a A0b OWb dx2b ozb OHa RCa oha dx3b rrb A2b OCa nl0a C1b erb A3b nl1a -arra eIb key0b NUa ylsa OHAa eJb senda key1b thvb ola toa KMb RCb KBb sob nl0b OTa OHb tta ohb SOb OCb ypa OHAb nl1b Y2a tob ylsb NUb scata olb -arrb sendb OTb ttb -keycb -keyca Y2b scatb -L32a
+"""
+GP = [[28, 36, 28, 36], [32, 32, 32, 32]]
+CYCLE = """
+Gp0a Gp1a dla Gp2a Gp3a sau0a LQa Mp0a KQu0a Mp1a sau1a Hp0u0a Hp1u0a Mp2a w1a Mp3a cntu0a Hp0u1a Gp0b L32b passu0a UAu0a Hp1u1a Gp1b onehu0a UOu0a Mp0b Gp3b dlb uu0a cntu1a Mp1b w2a Hp0u0b SQu0a sau0b Gp2b Hp1u0b xu0a KQu1a cntu0b LQb andu0a passu1a CUu0a UAu1a onehu1a Mp2b sau1b Dp1a Mp3b w0a UOu1a Hp0u1b Hp1u1b uu1a nba passu0b SQu1a KQu0b Dp0a xu1a cntu1b andu1a OMa CUu1a Za npa w1b passu1b UAu0b Dp3a C1a onehu0b UOu0b Zx1a uu0b npb nbb Zx0a SQu0b sv0a Dp2a w2b xu0b Eb fx0a OMb andu0b A0a sv1a Zb CUu0b nwb yzsa fx1a Zpb rs0a yzsb kl0a Z2b ZTb A1a Dp2b w0b dz2b Dp3b dz1b Dp0b key0a Dp1b dz3b dx2b KMa dz0b ozb KBa OWb A2b dx0b oza OHa dx1b RCa A0b dx3b oha nl0a A1b OCa erb nl1a A3b eIb C1b key0b ylsa OHAa NUa rs1a k2b ola key1b senda rrb toa eJb -arra RCb KMb sob nl0b KBb OTa OHb tta SOb ohb ypa OCb OHAb Y2a nl1b thvb tob ylsb NUb scata olb sendb OTb -keyca -arrb ttb -keycb Y2b scatb -L32a
+"""
+ON_V = {"Dp3b", "Gp1a", "Gp3a", "OHAb", "RCa", "RCb", "ZTb", "Za", "Zb", "tta", "ttb"}
+AU, HU, GP, WP, SAB, NBS = [64, 0], [64, 64], [[32, 32, 32, 32], [32, 32, 32, 32]], [15], "pk", [0, 1]
+CYCLE = """
+Gp0a Gp1a dla Gp2a Mp1a sau0a Mp0a Hp1u0a LQa Gp1b Hp0u0a Gp3a cntu0a Gp0b w0a KQu0a Mp2a passu0a Mp3a Gp2b UAu0a onehu0a Hp0u1a Hp1u1a sau1a UOu0a Mp0b Mp1b uu0a cntu1a Hp0u0b SQu0a Gp3b Hp1u0b sau0b xu0a KQu1a L32b passu1a cntu0b andu0a UAu1a LQb dlb KQu0b CUu0a Mp2b onehu1a npa sau1b Dp0a UOu1a Mp3b passu0b uu1a Hp0u1b nba Hp1u1b SQu1a Dp1a UAu0b onehu0b keyca KQu1b xu1a cntu1b OMa UOu0b UAu1b andu1a Za uu0b keycb CUu1a passu1b SQu0b w0b Zpa Dp2a onehu1b nbb Au0i12a xu0b UOu1b npb Au0i4a Eb Dp3a andu0b uu1b OMb Au0i0a CUu0b uTb Zb SQu1b Au0i8a Dp0b Zpb xu1b kla Au1i0a andu1b ZTb Dp1b Au1i4a key0a CUu1b dz1b nwb Au1i8a dz0b C1a dx0b Dp2b Au1i12a dx1b OWb Dp3b key4a key8a key12a A0b dz2b dx2b KMa RCa A1b dz3b KBa dx3b C1b A2b erb nl0a OHa RCb A3b k2b oha eIb key0b rrb yzsa Z2a OCa yzsb Z2b eJb key1b oza OHAa thvb nl1a ozb KMb toa ylsa NUa KBb sob ola senda -arra OHb OTa SOb ohb tta nl0b OCb OHAb Y2a nl1b tob scata ylsb NUb olb OTb sendb -arrb ttb Y2b scatb -L32a
+"""
+CYCLE = """
+Gp0a L32a Gp2a Mp1a sau0a dla Mp0a Hp1u0a LQa Hp0u0a Gp0b Gp3a cntu0a Gp1b KQu0a Mp2a passu0a Mp3a UAu0a onehu0a Gp2b Hp0u1a w0a Hp1u1a sau1a UOu0a Mp0b Mp1b uu0a cntu1a Hp0u0b SQu0a Gp3b Hp1u0b sau0b xu0a KQu1a passu1a L32b cntu0b andu0a UAu1a KQu0b dlb LQb CUu0a Mp2b onehu1a npa sau1b Dp0a UOu1a Mp3b passu0b uu1a nba Hp0u1b Hp1u1b SQu1a Dp1a KQu1b onehu0b UAu0b xu1a cntu1b OMa UOu0b UAu1b andu1a Za keyca uu0b keycb CUu1a passu1b SQu0b w0b Zpa Dp3a onehu1b Au0i12a nbb xu0b UOu1b Au0i4a npb Dp2a Eb uu1b andu0b OMb Au0i0a uTb CUu0b Zb SQu1b Au0i8a Dp1b Zpb xu1b kla Au1i0a andu1b ZTb Dp0b Au1i4a key0a dz0b CUu1b nwb Au1i12a dz1b Dp2b dx1b Au1i8a dx0b C1a OWb key4a Dp3b key8a key12a A1b dz2b dx2b A0b KMa dz3b RCa dx3b KBa A2b nl0a OHa A3b erb C1b k2b oha key0b eIb yzsb Z2b rrb yzsa Z2a OCa eJb key1b RCb ozb oza OHAa nl1a KMb thvb toa ylsa NUa KBb ola sob senda -arra OHb OTa SOb ohb tta nl0b OCb OHAb scata nl1b tob ylsb NUb olb sendb -arrb OTb ttb scatb -Gp1a
 """
 
 
@@ -82,6 +118,8 @@ def build():
 
     def add(eng, cost, reads, writes, fn, step=None, sem=None, k=1):
         reads, writes = [rng(x) for x in reads], [rng(x) for x in writes]
+        if LAST and step and step[1] == RO - 1:
+            step = ("_" + step[0], step[1])
         ops.append({"eng": eng, "cost": cost + extra(eng, sem, k, reads + writes, cost), "reads": reads, "writes": writes, "fn": fn, "step": step, "sem": sem, "n": k, "id": len(ops)})
 
     def V(cost, reads, writes, fn, step=None): add("v", cost, reads, writes, fn, step)
@@ -113,7 +151,7 @@ def build():
         V(v1(f * wid(out)), [a, b], [out], lambda q, T: [q.tensor_tensor(ap(out)(T), ap(a)(T), ap(b)(T), op)], step)
 
     def scan(out, a, b, o0, o1, step):
-        V(vh(wid(out)) if two(out, a, b) else v1(wid(out)), [a, b], [out], lambda q, T: [q.tensor_tensor_scan(ap(out)(T), ap(a)(T), ap(b)(T), 0.0, o0, o1)], step)
+        V(vh(wid(out) * P.get("sf", 1)) if two(out, a, b) else v1(wid(out) * P.get("sf4", 1)), [a, b], [out], lambda q, T: [q.tensor_tensor_scan(ap(out)(T), ap(a)(T), ap(b)(T), 0.0, o0, o1)], step)
 
     def ts(out, in0, s1, o1, s2=None, o2=None, step=None):
         V(cost1(out, in0), names(in0, s1, s2), [out],
@@ -130,8 +168,12 @@ def build():
 
     def on_v(step): return step[0] in ON_V or step[0][:-1] in ON_V
 
-    def gather(out, win, off, step):
-        if on_v(step):
+    def gather(out, win, off, step, half=False):
+        if half and on_v(step):
+            V(vg(wid(out)), [win, off], [out], lambda q, T: [q.tensor_scalar(ap(out)(T), ap(win)(T).indirect(ap(off)(T)), 0.5, None, O.mult)], step)
+        elif half:
+            S(sg(wid(out)), [win, off], [out], lambda q, T: [q.activation(ap(out)(T), ap(win)(T).indirect(ap(off)(T)), AF.Copy, scale=0.5)], step)
+        elif on_v(step):
             V(vg(wid(out)), [win, off], [out], lambda q, T: [q.tensor_copy(ap(out)(T), ap(win)(T).indirect(ap(off)(T)))], step)
         else:
             S(sg(wid(out)), [win, off], [out], lambda q, T: [q.activation(ap(out)(T), ap(win)(T).indirect(ap(off)(T)), AF.Copy)], step)
@@ -140,9 +182,15 @@ def build():
     def move(out, in_, step): (copy(out, in_, step) if on_v(step) else act(out, in_, AF.Copy, step))
     row = ("ones", 0, 128, 1, 0, 1)
 
-    dma("y", P["ldx"], [], [("X", 0, 4096)], "ldx", lambda q, T: [q.dma_start(T.X[:, 0:4096], T.field[:, 0:4096])])
-    dma("s", P["ldx"], [], [("X", 4096, 8192)], "ldy", lambda q, T: [q.dma_start(T.X[:, 4096:8192], T.field[:, 4096:8192])])
-    dma("y", 2.0, [], ["TI"], "ldt", lambda q, T: [q.dma_start(T.TI[:], T.tube[:])])
+    if TWO:
+        dma("y", P["ldx"], [], [("X", 0, 4096)], "ldx", lambda q, T: [q.dma_start(T.X[0:64, :], T.field[0:64, :])])
+        dma("s", P["ldx"], [], [("X", 4096, 8192)], "ldy", lambda q, T: [q.dma_start(T.X[64:128, :], T.field[0:64, :])])
+        dma("y", 2.5, [], ["TI"], "ldt",
+            lambda q, T: [q.dma_start(T.TI[64 * e:64 * e + 64, n * c:n * c + n], T.tube[64 * c:64 * c + 64, n * e:n * e + n]) for c in range(NC) for e in range(2)], 4)
+    else:
+        dma("y", P["ldx"], [], [("X", 0, 4096)], "ldx", lambda q, T: [q.dma_start(T.X[:, 0:4096], T.field[:, 0:4096])])
+        dma("s", P["ldx"], [], [("X", 4096, 8192)], "ldy", lambda q, T: [q.dma_start(T.X[:, 4096:8192], T.field[:, 4096:8192])])
+        dma("y", 2.0, [], ["TI"], "ldt", lambda q, T: [q.dma_start(T.TI[:], T.tube[:])])
     dma("y", 2.0, [], ["pri"], "ldp", lambda q, T: [q.dma_start(T.pri[:, 0:1], T.wt[:]), q.dma_start(T.pri[:, 1:2], T.kn[:]), q.dma_start(T.pri[:, 2:7], T.lim[:])], 3)
     fill("ones", 1.0)
     G(0.2, [], ["pI"], lambda q, T: [q.iota(T.pI[:], [[0, 1]], 0, 1)])
@@ -155,7 +203,9 @@ def build():
     G(0.4, [], ["irow"], lambda q, T: [q.iota(T.irow[:], [[0, 8], [1, 16]], 0, 0, allow_small_or_imprecise_dtypes=True)])
     for c in range(NC):
         G(3.9, [], [("W", 2048 * c, 2048 * c + 2048)], lambda q, T, c=c: [q.iota(T.W[:, 2048 * c:2048 * c + 2048], [[0, 2048]], 0, 0, allow_small_or_imprecise_dtypes=True)])
-    rb = 16 * max(GP[0] + GP[1])
+        if AU[c] < 0:
+            G(3.9, [], ["ZS"], lambda q, T: [q.iota(T.ZS[:], [[0, 2048]], 256, 0, allow_small_or_imprecise_dtypes=True)])
+    rb = 16 * max(GP[0] + GP[1] + (SP if min(AU) < 0 else []))
     fill("sel", 0.0)
     fill(("RB", 0, rb), 0.0)
     fill("RK", 0.0)
@@ -165,44 +215,70 @@ def build():
     fill(("RK", 0, 128, 16), 8388608.0)
     copy("icol", "iI")
     fill("mh", -0.5)
-    fill("half", 0.5)
     for c in range(NC):
         fill(("KM%d" % c, 128, 144), 8388608.0)
     if 0 in AU:
-        add("s", 16 * v1(128), ["IB"], ["Rep"], lambda q, T: [q.activation(T.Rep[:, i:2048:16], T.IB[:], AF.Copy, scale=-1.0) for i in range(16)], k=16)
+        add("s", 16 * v1(128), ["IB"], ["Rep"], lambda q, T: [q.activation(T.Rep[:, i:2048:16], T.IB[:], AF.Copy, scale=-0.5) for i in range(16)], k=16)
     act("IF", "IB", AF.Copy)
     ts("ige1", "icol", 1.0, O.is_ge)
     ts("e15", "icol", 15.0, O.is_equal, 128.0, O.mult)
-    ts("VS", "vbi", "icol", O.add)
+    ts("v0", ("vbi", 0, 8), "icol", O.add)
+    if TWO:
+        ts("e128", "pI", 64.0, O.is_ge, 128.0, O.mult)
+        fill("z2", 0.0)
+        for e in range(2):
+            copy(("SW", 64 * e, 64 * e + 64), ("IB", 64 - 64 * e, 128 - 64 * e))
+        ts(("VS", 0, 8), "v0", "e128", O.add)
+        ts(("VS", 8, 16), "v0", "e128", O.subtract, 128.0, O.add)
+    else:
+        ts("VS", "vbi", "icol", O.add)
     add("v", 8 * tiny, ["BO", "sel"], ["sel"], lambda q, T: [q.tensor_copy(T.sel[:, 16 * h:16 * h + 129 * 15 + 1:129], T.BO[:, 16 * h:16 * h + 16]) for h in range(8)], k=8)
-    copy(("prm", 0, 7), ("pri", 0, 7))
+    if TWO:
+        copy(("prb", 0, 7), ("pri", 0, 7))
+        add("t", 256 * pec, ["prb", "IB"], [("pb1", 0, 16)],
+            lambda q, T: [q.matmul(T.pb1[64 * e:64 * e + 64, 8 * c:8 * c + 7], T.IB[:, 64 * c:64 * c + 64], T.prb[:, 0:7], True, True) for c in range(NC) for e in range(2)], k=4)
+        copy("L32", "TI")
+        for c in range(NC):
+            copy(("prm", 8 * c, 8 * c + 7), ("pb1", 8 * c, 8 * c + 7))
+    else:
+        copy("L32", "TI")
+        for c in range(NC):
+            copy(("prm", 8 * c, 8 * c + 7), ("pri", 0, 7))
     copy("LU0", "TI")
-    ts("wq", ("prm", 0, 1), 1.0 / 4096, O.mult)
-    ts("k3", ("prm", 1, 2), ("prm", 1, 2), O.mult, -4.0, O.mult)
-    copy(("thv", 0, 1), ("prm", 2, 3))
-    ts("sqb", ("prm", 1, 2), 2.0, O.mult, 512.0, O.add)
-    act("wsel", "sel", AF.Copy, scale="wq")
+    ts("wq", ("prm", 0, 16, 8), 1.0 / 4096, O.mult)
+    tt("k3", ("prm", 1, 16, 8), ("prm", 1, 16, 8), O.mult)
+    copy(("thv", 0, 16, 8), ("prm", 2, 16, 8))
+    ts("sqb", ("prm", 1, 16, 8), 2.0, O.mult, 512.0, O.add)
+    act(("wsel", 0, 2048), "sel", AF.Copy, scale=("wq", 0, 1))
     act("Sel0", ("sel", 0, 128), AF.Copy)
-    ts("k4", "k3", -0.25, O.add)
+    if TWO:
+        act(("wsel", 2048, 4096), "sel", AF.Copy, ("wselb", 0), scale=("wq", 1, 2))
+        dma("y", P["ldx"], ["X"], ["X1"], "ldz", lambda q, T: [q.dma_start(T.X1[64 * e:64 * e + 64, :], T.field[64:128, :]) for e in range(2)], 2, ("ldzb", 0))
+    ts("k4", "k3", -4.0, O.mult, -0.25, O.add)
     ts("pth", "ige1", 109.5, O.mult, -101.0, O.add)
     ts("pIm", "IB", "ige1", O.mult)
     ts("S15", "ones", "e15", O.mult)
-    ts("VB", ("VS", 0, 8), 16.0, O.mult)
+    ts("VB", "v0", 16.0, O.mult)
     for c in range(NC):
-        ts(("VW", 16 * c, 16 * c + 8), ("VS", 0, 8), 16 - 1.0 / 128, O.mult)
+        ts(("VW", 16 * c, 16 * c + 8), "v0", 16 - 1.0 / 128, O.mult)
     ts("nIm", "pIm", -128.0, O.mult)
     copy("BOh", "BO")
     tt("BO1", "IB", "BOd", O.subtract)
-    ts("blk32", ("BO", 0, 128, 16), 32.0, O.mult)
-    ts("blk16", ("BO", 0, 128, 16), 16.0, O.mult)
-    ts("blkn", ("BO", 0, 128, 16), -16.0, O.mult)
+    ts("blk32", ("BO", 0, 128, 16), 64.0, O.mult)
+    ts("blk16", ("BO", 0, 128, 16), 32.0, O.mult)
+    ts("blkn", ("BO", 0, 128, 16), -32.0, O.mult)
+    ts("hIB", "IB", 0.5, O.mult)
     ts("OHm", "BO1", 128.0, O.mult)
     ts("grow", "grow", 16.0, O.mult)
     ts("selh", "sel", 128.0, O.mult)
 
     C24 = 1.5 * 2.0 ** 24
-    def blocks(b): return [(b, 128 * k, 128 * k + 128) for k in range(16)]
+    def blocks(b, lo=0): return [(b, lo + 128 * k, lo + 128 * k + 128) for k in range(16)]
     def cuts(sizes): return [(sum(sizes[:p]), sum(sizes[:p + 1])) for p in range(len(sizes))]
+
+    def zof(c): return ("ZS", 16 * n * c, 16 * n * (c + 1), 16) if AU[c] < 0 else ("Zb", n * c, n * c + n)
+
+    def xof(c): return "X1" if TWO and c else "X"
 
     def head(t, c):
         LU, dl, pa, pb = "LU%d" % t, "DL%d" % c, "pa%d" % c, "pb%d" % c
@@ -213,47 +289,69 @@ def build():
         if t:
             add("x", P["hop"], [Q("NU%d" % (t - 1))], [Q(LU)], None, st("arr"), sem="arr%d%d" % (t, c))
         def s1(x): return st(x) if t else None
-        copy(Q("L32"), Q(LU), s1("L32"))
-        act(Q("LQ"), Q("L32"), AF.Identity, s1("LQ"), bias="k4")
+        if t:
+            copy(Q("L32"), Q(LU), st("L32"))
+        act(Q("LQ"), Q("L32"), AF.Identity, st("LQ"), bias=("k4", c, c + 1))
         dma("y", 2.2, [Q("L32")], [dl], "dl%d" % c, lambda q, T: [q.dma_start(T[dl][:], T.L32[:, a0:a1])], 1, s1("dl"))
-        dma("y", P["wdma"], [dl], [Wd("W")], "w%d" % c,
-            lambda q, T: [q.dma_start(T.W[j::16, c0 + n * j:c1], T[dl][:, 1:17 - j, :]) for j in range(1, 16)], 15, s1("w"))
+        for p, (lo, hi) in enumerate(cuts(WP)):
+            dma("y", P.get("lat", 2.0) + P.get("hold", 0.3) * (hi - lo), [dl], [("W", c0 + p, c0 + p + 1)], "w%d%d" % (c, p),
+                lambda q, T, lo=lo, hi=hi: [q.dma_start(T.W[j::16, c0 + n * j:c1], T[dl][:, 1:17 - j, :]) for j in range(lo + 1, hi + 1)], hi - lo, st("w%d" % p))
         for p, (lo, hi) in enumerate(cuts(GP[c])):
-            gather(Wd("G", lo, hi), "X", Q(LU, lo, hi), st("Gp%d" % p))
+            gather(Wd("G", lo, hi), xof(c), Q(LU, lo, hi), st("Gp%d" % p))
             scan(Wd("M", lo, hi), ("RB", 0, 16 * (hi - lo)), Wd("G", lo, hi), O.max, O.min, st("Mp%d" % p))
-        for k, (lo, hi) in enumerate(cuts([UNIT] * (n // UNIT))):
+        for k, (lo, hi) in enumerate(cuts([UN[c]] * (n // UN[c]))):
             ends = [lo] + [y for (x, y) in cuts(GP[c]) if lo < y < hi and HP[c][k]] + [hi]
             for p, (l, h) in enumerate(zip(ends, ends[1:])):
-                ts(Wd("H", l, h), Wd("M", l, h), ("thv", t, t + 1), O.is_ge, step=st("Hp%du%d" % (p, k)))
-            sa, cn, g0, g1 = (pa, 128 + lo, 128 + hi), (pa, lo, hi), c0 + 16 * lo, c0 + 16 * hi
-            mm([(sa, row, ("mh", 0, UNIT))] + [(sa, w, ("G", g0 + j, g1, 16)) for j, w in enumerate(blocks("wsel"))], st("sau%d" % k), more=[("G", g0, g1)])
+                ts(Wd("H", l, h), Wd("M", l, h), ("thv", 8 * c * TWO + t, 8 * c * TWO + t + 1), O.is_ge, step=st("Hp%du%d" % (p, k)))
+            sa, cn, g0, g1 = (SAB + "%d" % c, 128 + lo, 128 + hi), (pa, lo, hi), c0 + 16 * lo, c0 + 16 * hi
+            mm([(sa, row, ("mh", 0, hi - lo))] + [(sa, w, ("G", g0 + j, g1, 16)) for j, w in enumerate(blocks("wsel", 2048 * c * TWO))], st("sau%d" % k), more=[("G", g0, g1)])
             mm([(cn, w, ("H", g0 + j, g1, 16)) for j, w in enumerate(blocks("sel"))], st("cntu%d" % k))
             ts(("PU", 2 * a0 + lo, 2 * a0 + hi), cn, "pth", O.is_ge, 1.0 / 128, O.mult, st("passu%d" % k))
         for k, (lo, hi) in enumerate(cuts([HU[c]] * (n // HU[c]))):
-            sa, f_, u_, q_ = (pa, 128 + lo, 128 + hi), (pb, lo, hi), (pb, 128 + lo, 128 + hi), (pb, 256 + lo, 256 + hi)
+            sa, f_, u_, q_ = (SAB + "%d" % c, 128 + lo, 128 + hi), (OB + "%d" % c, 256 * (OB == "pa") + lo, 256 * (OB == "pa") + hi), (pb, 128 + lo, 128 + hi), (pb, 256 + lo, 256 + hi)
             pas, uo = ("PU", 2 * a0 + lo, 2 * a0 + hi), ("PU", 2 * a0 + n + lo, 2 * a0 + n + hi)
             ts(Q("KQ", lo, hi), sa, 1.0 / 8192, O.add, step=st("KQu%d" % k))
             tt(Q("UA", lo, hi), sa, Q("KQ", lo, hi), O.subtract, st("UAu%d" % k))
             mm([(f_, "OHm", pas)], st("onehu%d" % k))
             tt(uo, f_, Q("UA", lo, hi), O.mult, st("UOu%d" % k))
             mm([(u_, "BOh", uo)], st("uu%d" % k))
-            act(q_, u_, AF.Square, st("SQu%d" % k), bias="sqb", scale=1024.0)
+            act(q_, u_, AF.Square, st("SQu%d" % k), bias=("sqb", c, c + 1), scale=1024.0)
             tt(Q("xI", lo, hi), q_, Q("LQ", lo, hi), O.add, st("xu%d" % k))
             ts(Q("cI", lo, hi), Q("xI", lo, hi), 8191, O.bitwise_and, step=st("andu%d" % k))
             copy(Q("CU", lo, hi), Q("cI", lo, hi), st("CUu%d" % k))
-        both, nbt = ("pc0", 256 + 16 * c, 272 + 16 * c), ("pc0", 256 + 16 * c, 264 + 16 * c)
-        mm([(both, w, ("PU", 2 * a0 + k, 2 * a1, 16)) for k, w in enumerate(blocks("selh"))] + [(nbt, "IB", "VB")], st("nb"))
+        both, nbt = ("pc%d" % (c * TWO), 256 + 16 * c, 272 + 16 * c), ("pc%d" % (c * TWO), 256 + 16 * c, 264 + 16 * c)
+        if NBS[c]:
+            mm([(nbt, w, ("PU", 2 * a0 + k, 2 * a0 + n, 16)) for k, w in enumerate(blocks("selh"))] + [(nbt, "IB", "VB")], st("nb"))
+            if t < RO - 1:
+                mm([((both[0], both[1] + 8, both[2]), w, ("PU", 2 * a0 + n + k, 2 * a1, 16)) for k, w in enumerate(blocks("selh"))], st("uT"))
+        else:
+            mm([(both, w, ("PU", 2 * a0 + k, 2 * a1, 16)) for k, w in enumerate(blocks("selh"))] + [(nbt, "IB", "VB")], st("nb"))
         ts(("OM", 8 * c, 8 * c + 8), nbt, -1.0, O.add, step=st("OM"))
-        gather(Q("Zb"), Wd("M"), ("OM", 8 * c, 8 * c + 8), st("Z"))
+        gather(zof(c), Wd("M"), ("OM", 8 * c, 8 * c + 8), st("Z"))
         zt = ("pc%d" % c, 288, 288 + n)
-        if AU[c]:
-            mm([((pb, 0, n), "IB", Q("Zb"))], st("Zp"))
+        if AU[c] < 0:
+            pass
+        elif AU[c]:
+            mm([((pb, 0, n), "hIB", Q("Zb"))], st("Zp"))
         else:
             mm([(zt, Q("Zb"), "IB")], st("Zp"))
             move(Q("ZT"), zt, st("ZT"))
         mm([(("pc%d" % c, 0, n), "pIm", "ones"), (("pc%d" % c, 0, n), "nIm", ("PU", 2 * a0, 2 * a0 + n))], st("np"))
 
+    def middle2(t, c):
+        pc, lo, x = "pc%d" % c, 16 * c, "ab"[c]
+        tt(("nw", lo, lo + 8), (pc, 256 + lo, 264 + lo), ("VW", lo, lo + 8), O.subtract, ("nw" + x, t))
+        ts(("OW", lo, lo + 8), ("nw", lo, lo + 8), 128.0, O.mult, -128.0, O.add, ("OW" + x, t))
+        if t < RO - 1:
+            ut, k2, rr, so = (pc, 264 + lo, 272 + lo), ("k2", lo, lo + 8), ("rr", lo, lo + 8), (pc, 416, 432)
+            ts(k2, ut, -31.0 / 64, O.add, step=("k2" + x, t))
+            tt(rr, ut, k2, O.subtract, ("rr" + x, t))
+            mm([(so, "IB", "VS"), ((pc, 416, 424), "IB", rr), ((pc, 424, 432), "SW", rr)], ("so" + x, t), whole=so)
+            ts(("SO", lo, lo + 16), so, 32.0, O.mult, step=("SO" + x, t))
+
     def middle(t):
+        if TWO:
+            return [middle2(t, c) for c in range(NC)]
         nb = ("pc0", 256, 288)
         tt("nw", nb, "VW", O.subtract, ("nwb", t))
         ts("OW", "nw", 128.0, O.mult, -128.0, O.add, ("OWb", t))
@@ -271,8 +369,22 @@ def build():
         key = (pk, 0, 128)
         mm([(key, row, "irow"), (key, row, "grow")], st("keyc"), stop=False, whole=(pk, 0, 512))
         for p, (lo, hi) in enumerate(cuts(DP[c])):
-            gather(Wd("D", lo, hi), "X", Q("CU", lo, hi), st("Dp%d" % p))
-        if AU[c]:
+            gather(Wd("D", lo, hi), xof(c), Q("CU", lo, hi), st("Dp%d" % p), True)
+        if AU[c] < 0:
+            for k, (lo, hi) in enumerate(cuts(SP)):
+                d16, z16, sv = Wd("D", lo, hi) + (16,), Wd("ZS", lo, hi) + (16,), Q("sv", lo, hi)
+                scan(Wd("Zx", lo, hi), ("RB", 0, 16 * (hi - lo)), Wd("ZS", lo, hi), O.max, O.min, st("Zx%d" % k))
+                act(sv, d16, AF.Copy, st("sv%d" % k))
+                tt(d16, sv, z16, O.max, st("fx%d" % k))
+                scan(Wd("A", lo, hi), Wd("Zx", lo, hi), Wd("D", lo, hi), O.min, O.max, st("A%d" % k))
+                act(d16, sv, AF.Copy, st("rs%d" % k))
+            for p, (lo, hi) in enumerate(cuts(KP[c])):
+                add("t", 16 * max(8, min(64, hi - lo)) * pec, [Q("sv", lo, hi), "blkn", key], [key],
+                    lambda q, T, lo=lo, hi=hi: [q.matmul(T[pk][lo:hi, i:128:16], T.D[:, c0 + 16 * lo + i:c0 + 16 * hi:16] if i else T.sv[:, a0 + lo:a0 + hi], T.blkn[:], False, False) for i in range(16)],
+                    st("kl%d" % p), k=16)
+            for p, (lo, hi) in enumerate(cuts(KP[c])):
+                mm([((pk, i, 128, 16, lo, hi), ("A", c0 + 16 * lo + i, c0 + 16 * hi, 16), "blk32") for i in range(16)], st("key%d" % p), False, True, [Wd("A", lo, hi)], key)
+        elif AU[c]:
             for k, (lo, hi) in enumerate(cuts([AU[c]] * (n // AU[c]))):
                 for i0 in range(0, 16, KG):
                     zk = ("pb%d" % c, lo, hi)
@@ -300,22 +412,32 @@ def build():
         oh, np_, nl_ = (pk, 128, 128 + n), (pc, 0, n), (pc, 128, 128 + n)
         mm([(oh, OH, "IB")], st("oh"))
         if not last:
+            o2, tot, ot = oh, (pk, 256, 264), ("OT", h0, h1)
+            if OH2[c]:
+                o2, tot = (OH2[c], 0, n), (OH2[c], 128, 136)
+                mm([(o2, OH, "IB")], st("o2"))
             if on_v(st("OHA")):
-                ts(Q("OHA"), oh, "icol", O.mult, step=st("OHA"))
+                ts(Q("OHA"), o2, "icol", O.mult, step=st("OHA"))
             else:
-                act(Q("OHA"), oh, AF.Copy, st("OHA"), scale="icol")
-            tot, ot = (pk, 256, 264), ("OT", h0, h1)
+                act(Q("OHA"), o2, AF.Copy, st("OHA"), scale="icol")
             mm([(tot, "IB", "VB")] + [(tot, w, ("OHA", a0 + k, a1, 16)) for k, w in enumerate(blocks("sel"))], st("to"))
             copy(ot, tot, st("OT"))
-            if on_v(st("tt")):
-                act(Q("Z2"), Q("Zb"), AF.Copy, st("Z2"), bias=-0.5)
+            if TWO:
+                yb = "pa%d" % c
+                yp, own, oth = (yb, 256, 512), (yb, 256, 384), (yb, 384, 512)
+                mm([(yp, row, "mh"), (own, "IB", zof(c)), (oth, "SW", zof(c))], st("yp0"), stop=False, more=[(yb, 0, 256)], whole=yp)
+                gather(Q("XB"), Wd("D"), ot, st("tt"))
+                mm([(own, "IB", Q("XB")), (oth, "SW", Q("XB"))], st("yp1"), start=False, whole=yp)
+                ts(("Y2", 2 * a0, 2 * a1), yp, C24, O.add, -C24, O.add, st("Y2"))
+            elif on_v(st("tt")):
+                act(Q("Z2"), zof(c), AF.Copy, st("Z2"), bias=-0.25, scale=0.5)
                 gadd(Q("tt"), Wd("D"), ot, Q("Z2"), st("tt"))
                 yp = Q("tt")
             else:
                 yp = (pk, 264, 264 + n)
                 gather(Q("XB"), Wd("D"), ot, st("tt"))
-                mm([(yp, row, "mh"), (yp, "IB", Q("Zb")), (yp, "IB", Q("XB"))], st("yp"))
-            ts(Q("Y2"), yp, C24, O.add, -C24, O.add, st("Y2"))
+                mm([(yp, row, ("mh", 0, n)), (yp, "IB", zof(c)), (yp, "IB", Q("XB"))], st("yp"))
+
         tt(Q("C1"), np_, Q("cI"), O.mult, st("C1"))
         tt(Q("OC"), oh, Q("cI"), O.mult, st("OC"))
         ow = ("OW", 16 * c, 16 * c + 8)
@@ -331,23 +453,34 @@ def build():
             add("g", 0.5, [Q(NU)], [], ("send", t, c), st("send"), sem="sent")
         else:
             act(Q("yls"), nl_, AF.Copy, st("yls"))
-            dma("y", 2.0, [Q("yls")], [], "ol%d" % c, lambda q, T: [q.dma_start(T.yl[:, a0:a1], T.yls[:, a0:a1])], 1, st("ol"))
-            act(Q("yzs"), Q("Zb"), AF.Copy, st("yzs"))
-            dma("y", 2.0, [Q("yzs")], [], "oz%d" % c, lambda q, T: [q.dma_start(T.yz[:, a0:a1], T.yzs[:, a0:a1])], 1, st("oz"))
+            def out(y, s): return lambda q, T: ([q.dma_start(T[y][64 * c:64 * c + 64, n * e:n * e + n], T[s][64 * e:64 * e + 64, a0:a1]) for e in range(2)] if TWO else
+                                                [q.dma_start(T[y][:, a0:a1], T[s][:, a0:a1])])
+            dma("y", 2.0, [Q("yls")], [], "ol%d" % c, out("yl", "yls"), 1 + TWO, st("ol"))
+            act(Q("yzs"), zof(c), AF.Copy, st("yzs"))
+            dma("y", 2.0, [Q("yzs")], [], "oz%d" % c, out("yz", "yzs"), 1 + TWO, st("oz"))
 
     def close(t):
         so, eb = (SB, 416, 432), (SB, 448, 512)
-        mm([(so, "IB", "VS")] + [((SB, 416 + 8 * c, 424 + 8 * c), "IB", ("rr", 16 * c + 8, 16 * c + 16)) for c in range(NC)], ("sob", t), whole=so)
-        ts("SO", so, 32.0, O.mult, step=("SOb", t))
+        if not TWO:
+            mm([(so, "IB", "VS")] + [((SB, 416 + 8 * c, 424 + 8 * c), "IB", ("rr", 16 * c + 8, 16 * c + 16)) for c in range(NC)], ("sob", t), whole=so)
+            ts(("SO", 0, 16), so, 32.0, O.mult, step=("SOb", t))
         mm([(eb, "S15", ("PU", 2 * n * c + k, 2 * n * c + k + 64)) for c in range(NC) for k in (0, 64)], ("Eb", t))
         V(tiny, [eb], ["er"], lambda q, T: [q.tensor_reduce(T.er[:], ap(eb)(T), AxisListType.X, O.add, negate=True)], ("erb", t))
-        copy("eI", "er", ("eIb", t))
-        ts("eJ", "eI", 7, O.bitwise_and, step=("eJb", t))
-        tt(("thv", t + 1, t + 2), ("prm", 3 + t, 4 + t), "eJ", O.add, ("thvb", t))
+        if TWO:
+            ts("eI", "z2", "er", O.add, step=("eIb", t))
+            ts("eJ", "eI", 7, O.bitwise_and, step=("eJb", t))
+            V(tiny, ["eJ", "prm"], [("thv", t + 1, t + 2), ("thv", t + 9, t + 10)],
+              lambda q, T: [q.tensor_tensor(T.thv[:, t + 1:16:8], T.prm[:, t + 3:16:8], T.eJ[:], O.add)], ("thvb", t))
+            return
+        copy(("eI", 0, 1), "er", ("eIb", t))
+        ts(("eJ", 0, 1), ("eI", 0, 1), 7, O.bitwise_and, step=("eJb", t))
+        tt(("thv", t + 1, t + 2), ("prm", 3 + t, 4 + t), ("eJ", 0, 1), O.add, ("thvb", t))
 
     def scatter(t, c):
-        V(0.055 + P["sc"] * n * cyc, [("Y2", n * c, n * c + n), "half", ("SO", 8 * c, 8 * c + 8)], ["X"],
-          lambda q, T: [q.tensor_tensor(T.X[:].indirect(T.SO[:, 8 * c:8 * c + 8]), T.Y2[:, n * c:n * c + n], T.half[:], O.mult)], ("scat" + "ab"[c], t))
+        m = n * (1 + TWO)
+        y2, so = ("tt", m * c, m * c + m), ("SO", m // 16 * c, m // 16 * (c + 1))
+        V(0.055 + P["sc"] * m * cyc, [y2, so], [xof(c)],
+          lambda q, T: [q.tensor_copy(T[xof(c)][:].indirect(ap(so)(T)), ap(y2)(T))], ("scat" + "ab"[c], t))
 
     for t in range(RO):
         for c in range(NC):

from concourse.mybir import AluOpType, AxisListType, ActivationFunctionType

RO = 5
TWO = 0
NC, NT = 2, 128
UN = [64, 64]
LAST = 0
GP = [[32, 32, 32, 32], [32, 32, 32, 32]]
DP = [[32, 32, 32, 32], [32, 32, 32, 32]]
HP = [[1, 1], [1, 1]]
HU = [64, 64]
AU, KG = [64, 0], 4
KP = [[128], [96, 32]]
DB = [["pa0", "pb0"], ["pa1", "pb1", "pa0", "pb1"]]
SB = "pc1"
SAB, OB, NBS = "pa", "pb", [0, 0]
OH2 = ["", ""]
SP = [64, 64]
WP = [15]

BF, F32, I32, U16, F16 = "bfloat16", "float32", "int32", "uint16", "float16"
SCRATCH = {"irow": ("sbuf", [1, 128], BF), "grow": ("sbuf", [1, 128], BF), "mh": ("sbuf", [1, 256], BF)}
for _n, _w, _d in (
        ("X", 8192, BF), ("TI", 256, I32), ("pri", 8, I32), ("prb", 8, BF), ("prm", 16, F32), ("wq", 2, F32), ("sqb", 2, F32), ("k3", 2, F32), ("k4", 2, F32),
        ("X1", 8192, BF), ("SW", 128, BF), ("e128", 1, F32), ("v0", 8, BF), ("z2", 2, F32),
        ("pI", 1, I32), ("iI", 1, I32), ("icol", 1, F32), ("pth", 1, F32), ("ige1", 1, F32), ("e15", 1, F32),
        ("ones", 128, BF), ("BO1", 128, BF), ("BO", 128, BF), ("BOh", 128, F16), ("IB", 128, BF), ("IF", 128, F32),
        ("pIm", 128, BF), ("nIm", 128, F16), ("BOd", 128, BF), ("OHm", 128, F16), ("S15", 128, F16), ("Sel0", 128, F32),
        ("sel", 2048, BF), ("wsel", 4096, BF), ("selh", 2048, F16), ("Rep", 2048, BF), ("blk16", 8, BF), ("blk32", 8, BF), ("blkn", 8, BF),
        ("vbi", 16, I32), ("VB", 8, BF), ("VW", 32, F32), ("VS", 16, BF),
        ("RB", 1024, BF), ("RK", 128, BF), ("half", 256, BF), ("W", 4096, F32),
        ("er", 1, F32), ("eI", 2, I32), ("eJ", 2, I32), ("thv", 16, F32),
        ("G", 4096, BF), ("M", 4096, BF), ("H", 4096, BF), ("D", 4096, BF), ("A", 4096, BF), ("ZS", 2048, BF), ("Zx", 2048, BF), ("R01", 1024, BF), ("sv", 256, BF),
        ("PU", 512, F16), ("OM", 16, U16), ("nw", 32, F32), ("OW", 32, U16), ("OT", 16, U16), ("SO", 32, U16), ("k2", 32, I32), ("rr", 32, BF),
        ("KQ", 256, I32), ("UA", 256, F16), ("LQ", 256, F32), ("Zb", 256, BF), ("ZT", 256, BF), ("XB", 256, BF),
        ("xI", 256, I32), ("cI", 256, I32), ("CU", 256, U16), ("L32", 256, F32), ("OHA", 256, BF),
        ("OC", 256, F32), ("C1", 256, F32), ("RC", 256, F32), ("Y2", 512, BF), ("Z2", 256, F32), ("tt", 256, I32), ("hIB", 128, BF), ("yls", 256, F32), ("yzs", 256, F32)):
    SCRATCH[_n] = ("sbuf", [128, _w], _d)
for _c in range(NC):
    SCRATCH["DL%d" % _c] = ("dram", [8, 16, 128], F32)
    SCRATCH["KM%d" % _c] = ("sbuf", [128, 144], F32)
    SCRATCH["KB%d" % _c] = ("sbuf", [128, 128], F32)
    SCRATCH["OH%d" % _c] = ("sbuf", [128, 128], BF)
    for _b in ("pa%d", "pb%d", "pc%d", "pk%d"):
        SCRATCH[_b % _c] = ("psum", [128, 512], F32)
for _t in range(RO):
    SCRATCH["LU%d" % _t] = ("sbuf", [128, 256], U16)
    if _t < RO - 1:
        SCRATCH["NU%d" % _t] = ("sbuf", [128, 256], U16)
BANKS = [_n for _n in SCRATCH if SCRATCH[_n][0] == "psum"]

SEMAPHORES = ["cv", "cs", "ct", "cg", "sent", "ldp", "ldt", "ldx", "ldy", "ldz"] + \
    ["%s%d" % (a, c) for a in ("oz", "ol", "dl") for c in range(NC)] + ["w%d%d" % (c, p) for c in range(NC) for p in range(4)] + ["arr%d%d" % (t, c) for t in range(1, RO) for c in range(NC)]

P = {"cyc": 0.87e-3, "ga": 1.56, "sc": 3.8, "pec": 0.45e-3, "wake": 0.18, "hop": 3.5, "wdma": 6.0, "ldx": 8.0}
ON_V = {"A3b", "RCa", "Gp1a", "Gp3a", "ttb", "Dp3b", "ZTb"}
PERIOD = 20
CYCLE = """
Gp0a Gp1a L32a Gp2a sau0a Mp0a dla Mp1a Hp0u0a keycb Hp1u0a KQu0a Mp2a Gp1b cntu0a Gp3a Gp0b Hp0u1a passu0a UAu0a wa Mp3a onehu0a Gp2b sau1a Mp1b UOu0a Hp1u1a uu0a sau0b Mp0b LQa KQu1a SQu0a Hp1u0b Gp3b cntu1a Hp0u0b KQu0b xu0a L32b cntu0b andu0a passu1a LQb dlb UAu1a CUu0a Mp2b onehu1a sau1b Dp0a UOu1a Mp3b Hp0u1b uu1a npa nba UAu0b SQu1a KQu1b Dp1a passu0b Hp1u1b onehu0b xu1a OMa cntu1b UOu0b andu1a Za CUu1a C1a wb uu0b passu1b Zpa SQu0b UAu1b Dp2a Au0i4a onehu1b Eb npb UOu1b xu0b Au0i0a Dp3a nbb andu0b Au0i12a uu1b OMb SQu1b CUu0b Au1i0a Zb Dp1b xu1b Au1i8a Zpb kla andu1b ZTb key0a nwb Dp0b CUu1b Au1i4a dz1b dx1b Au0i8a dz2b yzsa Dp2b Au1i12a dz0b oza key4a Dp3b dx0b key8a A1b key12a dx2b k2b A0b OWb KMa kl3b RCa dz3b A2b KBa rrb dx3b OHa sob Z2b nl0a yzsb A3b oha key0b ozb erb OCa SOb key1b C1b OHAa eIb nl1a RCb eJb toa KMb ylsa NUa thvb KBb ola -arra senda nl0b OTa OHb tta ohb OCb ypa OHAb nl1b Y2a ylsb tob NUb olb scata sendb -arrb -keyca OTb ttb Y2b scatb
"""
ON_V = {"RCa", "RCb", "Gp1a", "Gp3a", "ttb", "Dp3b", "Dp1b"}
AU, HU, DP, DB = [-1, 0], [64, 128], [[32, 32, 32, 32], [36, 24, 36, 32]], [["pa0", "pb0"], ["pa1", "pb1", "pa0", "pb0"]]
CYCLE = """
Gp0a Gp1a dla LQa Gp2a Mp0a sau0a Mp1a Hp0u0a Hp1u0a KQu0a Gp3a cntu0a wa Gp0b Mp2a Mp3a passu0a Gp1b UAu0a Hp0u1a onehu0a sau1a Hp1u1a L32b Mp0b Gp2b cntu1a dlb UOu0a Mp1b Hp0u0b uu0a sau0b Hp1u0b SQu0a Gp3b KQu1a xu0a cntu0b passu1a UAu1a andu0a Mp2b onehu1a CUu0a LQb sau1b Mp3b Dp0a UOu1a Hp0u1b wb npa Hp1u1b uu1a nba passu0b KQu0b SQu1a Dp1a xu1a cntu1b OMa andu1a CUu1a Za C1a passu1b sv0a Dp3a UAu0b fx0a onehu0b npb Eb UOu0b Zx1a uu0b nbb SQu0b Zx0a Dp2a xu0b OMb A0a yzsa Zb sv1a andu0b oza Zpb rs0a fx1a Z2b kl0a yzsb CUu0b ZTb A1a ozb Dp2b dz0b Dp1b dz1b key0a Dp0b Dp3b dx1b dz2b dx2b KMa A1b nwb dx0b KBa A2b OWb k2b dz3b OHa RCa A0b oha C1b dx3b OCa nl0a RCb A3b nl1a erb key0b eIb NUa OHAa ylsa rrb rs1a eJb key1b senda -arra ola thvb toa KMb KBb sob nl0b OTa OHb tta SOb ohb OCb ypa OHAb nl1b Y2a tob NUb ylsb scata -arrb sendb -keyca olb OTb ttb -keycb Y2b scatb -L32a
"""
ON_V = {"RCa", "RCb", "Gp1a", "Gp3a", "ttb", "Dp3b", "Dp1b", "OHAb"}
GP, DP = [[36, 28, 36, 28], [32, 32, 32, 32]], [[32, 32, 32, 32], [32, 32, 32, 32]]
CYCLE = """
Gp0a Gp1a dla Mp1a Gp2a sau0a Mp0a Hp1u0a Hp0u0a LQa KQu0a Gp3a cntu0a wa Gp0b Mp2a UAu0a passu0a Mp3a sau1a Hp0u1a Gp1b Hp1u1a Mp0b onehu0a cntu1a UOu0a Gp2b L32b Mp1b dlb uu0a sau0b Hp0u0b Hp1u0b SQu0a Gp3b xu0a cntu0b passu1a KQu1a andu0a Mp2b onehu1a npa CUu0a LQb UAu1a sau1b Mp3b Dp0a UOu1a Hp0u1b uu1a Hp1u1b nba wb KQu0b SQu1a Dp1a passu0b xu1a cntu1b OMa andu1a CUu1a C1a Za passu1b sv0a Dp3a UAu0b fx0a onehu0b Eb UOu0b Zx1a uu0b nbb SQu0b Zx0a Dp2a npb xu0b OMb A0a sv1a Zb andu0b fx1a yzsa rs0a CUu0b Zpb Z2b yzsb A1a kl0a oza ZTb ozb Dp0b Dp1b dz2b key0a Dp2b Dp3b dz1b dx1b dz0b A1b KMa dx0b nwb dx2b KBa OWb A0b dz3b OHa k2b RCa A2b oha dx3b erb OCa nl0a C1b A3b nl1a RCb key0b eIb rs1a NUa ylsa OHAa rrb eJb key1b senda -arra ola thvb toa KMb KBb sob nl0b OTa OHb tta SOb ohb OCb ypa OHAb nl1b Y2a tob ylsb NUb scata olb sendb -arrb -keyca OTb -keycb ttb Y2b scatb -L32a
"""
WP = [5, 5, 5]
CYCLE = """
Gp0a Gp1a dla Mp1a Gp2a sau0a Mp0a Hp1u0a Hp0u0a LQa KQu0a Gp3a cntu0a Gp0b w0a Mp2a UAu0a passu0a Mp3a sau1a Gp1b Hp0u1a Hp1u1a Mp0b onehu0a cntu1a UOu0a L32b Gp2b w1a Mp1b uu0a sau0b Hp0u0b Hp1u0b SQu0a passu1a Gp3b KQu1a cntu0b xu0a UAu1a andu0a Mp2b onehu1a CUu0a npa dlb LQb UOu1a Dp0a Mp3b sau1b w2a Hp0u1b Hp1u1b uu1a nba KQu0b SQu1a Dp1a passu0b xu1a cntu1b OMa andu1a CUu1a Za C1a passu1b UAu0b sv0a Dp3a w0b onehu0b npb fx0a Eb UOu0b Zx1a uu0b nbb SQu0b Zx0a Dp2a xu0b OMb A0a w1b yzsa sv1a Zb andu0b fx1a rs0a CUu0b Zpb yzsb Z2b A1a kl0a ZTb Dp0b Dp1b dz2b key0a w2b Dp2b Dp3b dz1b dx1b dz0b rs1a A1b KMa dx0b nwb k2b dx2b KBa oza OWb A0b rrb dz3b OHa ozb RCa -arra oha A2b dx3b C1b OCa nl0a erb A3b nl1a eIb eJb key0b NUa ylsa OHAa thvb senda ola key1b RCb toa KMb KBb sob nl0b OTa OHb tta SOb ohb OCb ypa OHAb nl1b Y2a tob ylsb NUb scata olb sendb -arrb -keyca OTb ttb -keycb Y2b scatb -L32a
"""
CYCLE = """
Gp0a Gp1a dla Mp1a LQa Gp2a sau0a Mp0a Hp1u0a Hp0u0a KQu0a Gp3a cntu0a Gp0b w1a Mp2a Mp3a UAu0a passu0a Gp1b Hp0u1a onehu0a sau1a Hp1u1a Mp0b UOu0a cntu1a L32b Gp2b Mp1b dlb Hp0u0b uu0a sau0b w0a Hp1u0b SQu0a KQu1a Gp3b passu1a cntu0b xu0a UAu1a andu0a Mp2b onehu1a CUu0a npa LQb UOu1a Dp0a Mp3b sau1b Hp0u1b w2a Hp1u1b uu1a nba KQu0b SQu1a Dp1a passu0b xu1a cntu1b OMa andu1a CUu1a Za C1a passu1b UAu0b sv0a w2b Dp3a onehu0b Eb fx0a npb UOu0b Zx0a uu0b nbb SQu0b Zx1a Dp2a xu0b OMb w0b A0a sv1a Zb andu0b fx1a yzsa CUu0b Zpb Z2b yzsb A1a kl0a rs0a ZTb Dp0b Dp1b dz2b w1b key0a Dp2b Dp3b dz1b dx1b dz0b A1b KMa dx0b nwb oza dz3b KBa k2b rs1a A0b OWb dx2b ozb OHa RCa oha dx3b rrb A2b OCa nl0a C1b erb A3b nl1a -arra eIb key0b NUa ylsa OHAa eJb senda key1b thvb ola toa KMb RCb KBb sob nl0b OTa OHb tta ohb SOb OCb ypa OHAb nl1b Y2a tob ylsb NUb scata olb -arrb sendb OTb ttb -keycb -keyca Y2b scatb -L32a
"""
GP = [[28, 36, 28, 36], [32, 32, 32, 32]]
CYCLE = """
Gp0a Gp1a dla Gp2a Gp3a sau0a LQa Mp0a KQu0a Mp1a sau1a Hp0u0a Hp1u0a Mp2a w1a Mp3a cntu0a Hp0u1a Gp0b L32b passu0a UAu0a Hp1u1a Gp1b onehu0a UOu0a Mp0b Gp3b dlb uu0a cntu1a Mp1b w2a Hp0u0b SQu0a sau0b Gp2b Hp1u0b xu0a KQu1a cntu0b LQb andu0a passu1a CUu0a UAu1a onehu1a Mp2b sau1b Dp1a Mp3b w0a UOu1a Hp0u1b Hp1u1b uu1a nba passu0b SQu1a KQu0b Dp0a xu1a cntu1b andu1a OMa CUu1a Za npa w1b passu1b UAu0b Dp3a C1a onehu0b UOu0b Zx1a uu0b npb nbb Zx0a SQu0b sv0a Dp2a w2b xu0b Eb fx0a OMb andu0b A0a sv1a Zb CUu0b nwb yzsa fx1a Zpb rs0a yzsb kl0a Z2b ZTb A1a Dp2b w0b dz2b Dp3b dz1b Dp0b key0a Dp1b dz3b dx2b KMa dz0b ozb KBa OWb A2b dx0b oza OHa dx1b RCa A0b dx3b oha nl0a A1b OCa erb nl1a A3b eIb C1b key0b ylsa OHAa NUa rs1a k2b ola key1b senda rrb toa eJb -arra RCb KMb sob nl0b KBb OTa OHb tta SOb ohb ypa OCb OHAb Y2a nl1b thvb tob ylsb NUb scata olb sendb OTb -keyca -arrb ttb -keycb Y2b scatb -L32a
"""
ON_V = {"Dp3b", "Gp1a", "Gp3a", "OHAb", "RCa", "RCb", "ZTb", "Za", "Zb", "tta", "ttb"}
AU, HU, GP, WP, SAB, NBS = [64, 0], [64, 64], [[32, 32, 32, 32], [32, 32, 32, 32]], [15], "pk", [0, 1]
CYCLE = """
Gp0a Gp1a dla Gp2a Mp1a sau0a Mp0a Hp1u0a LQa Gp1b Hp0u0a Gp3a cntu0a Gp0b w0a KQu0a Mp2a passu0a Mp3a Gp2b UAu0a onehu0a Hp0u1a Hp1u1a sau1a UOu0a Mp0b Mp1b uu0a cntu1a Hp0u0b SQu0a Gp3b Hp1u0b sau0b xu0a KQu1a L32b passu1a cntu0b andu0a UAu1a LQb dlb KQu0b CUu0a Mp2b onehu1a npa sau1b Dp0a UOu1a Mp3b passu0b uu1a Hp0u1b nba Hp1u1b SQu1a Dp1a UAu0b onehu0b keyca KQu1b xu1a cntu1b OMa UOu0b UAu1b andu1a Za uu0b keycb CUu1a passu1b SQu0b w0b Zpa Dp2a onehu1b nbb Au0i12a xu0b UOu1b npb Au0i4a Eb Dp3a andu0b uu1b OMb Au0i0a CUu0b uTb Zb SQu1b Au0i8a Dp0b Zpb xu1b kla Au1i0a andu1b ZTb Dp1b Au1i4a key0a CUu1b dz1b nwb Au1i8a dz0b C1a dx0b Dp2b Au1i12a dx1b OWb Dp3b key4a key8a key12a A0b dz2b dx2b KMa RCa A1b dz3b KBa dx3b C1b A2b erb nl0a OHa RCb A3b k2b oha eIb key0b rrb yzsa Z2a OCa yzsb Z2b eJb key1b oza OHAa thvb nl1a ozb KMb toa ylsa NUa KBb sob ola senda -arra OHb OTa SOb ohb tta nl0b OCb OHAb Y2a nl1b tob scata ylsb NUb olb OTb sendb -arrb ttb Y2b scatb -L32a
"""
CYCLE = """
Gp0a L32a Gp2a Mp1a sau0a dla Mp0a Hp1u0a LQa Hp0u0a Gp0b Gp3a cntu0a Gp1b KQu0a Mp2a passu0a Mp3a UAu0a onehu0a Gp2b Hp0u1a w0a Hp1u1a sau1a UOu0a Mp0b Mp1b uu0a cntu1a Hp0u0b SQu0a Gp3b Hp1u0b sau0b xu0a KQu1a passu1a L32b cntu0b andu0a UAu1a KQu0b dlb LQb CUu0a Mp2b onehu1a npa sau1b Dp0a UOu1a Mp3b passu0b uu1a nba Hp0u1b Hp1u1b SQu1a Dp1a KQu1b onehu0b UAu0b xu1a cntu1b OMa UOu0b UAu1b andu1a Za keyca uu0b keycb CUu1a passu1b SQu0b w0b Zpa Dp3a onehu1b Au0i12a nbb xu0b UOu1b Au0i4a npb Dp2a Eb uu1b andu0b OMb Au0i0a uTb CUu0b Zb SQu1b Au0i8a Dp1b Zpb xu1b kla Au1i0a andu1b ZTb Dp0b Au1i4a key0a dz0b CUu1b nwb Au1i12a dz1b Dp2b dx1b Au1i8a dx0b C1a OWb key4a Dp3b key8a key12a A1b dz2b dx2b A0b KMa dz3b RCa dx3b KBa A2b nl0a OHa A3b erb C1b k2b oha key0b eIb yzsb Z2b rrb yzsa Z2a OCa eJb key1b RCb ozb oza OHAa nl1a KMb thvb toa ylsa NUa KBb ola sob senda -arra OHb OTa SOb ohb tta nl0b OCb OHAb scata nl1b tob ylsb NUb olb sendb -arrb OTb ttb scatb -Gp1a
"""


def extra(eng, sem, n, sides, cost=0.0):
    if sem or eng not in "vs":
        return 0.0
    if P.get("pm") and any(x[0] in BANKS for x in sides):
        return max(0.0, n * P["pm"] * P["cyc"] - cost)
    return n * (P.get("ov", 0.0) + (P.get("op", 0.0) if any(x[0] in BANKS for x in sides) else 0.0))


def send_sides(fn, T):
    _, t, c = fn
    return T["LU%d" % (t + 1)][:, NT * c:NT * c + NT], T["NU%d" % t][:, NT * c:NT * c + NT]


def build():
    O, AF = AluOpType, ActivationFunctionType
    ops = []
    cyc, pec = P["cyc"], P["pec"]
    n = NT

    def v1(m): return max(64, m) * cyc
    def vh(m): return max(64, m / 2) * cyc
    def vg(m): return 0.055 + m * P["ga"] * cyc
    def sg(m): return 0.07 + m * P["ga"] * cyc
    tiny = v1(1)

    def rng(x): return (x, 0, 100000) if isinstance(x, str) else x[:3]

    def add(eng, cost, reads, writes, fn, step=None, sem=None, k=1):
        reads, writes = [rng(x) for x in reads], [rng(x) for x in writes]
        if LAST and step and step[1] == RO - 1:
            step = ("_" + step[0], step[1])
        ops.append({"eng": eng, "cost": cost + extra(eng, sem, k, reads + writes, cost), "reads": reads, "writes": writes, "fn": fn, "step": step, "sem": sem, "n": k, "id": len(ops)})

    def V(cost, reads, writes, fn, step=None): add("v", cost, reads, writes, fn, step)
    def S(cost, reads, writes, fn, step=None): add("s", cost, reads, writes, fn, step)
    def G(cost, reads, writes, fn): add("g", cost, reads, writes, fn)
    def dma(eng, cost, reads, writes, sem, fn, k=1, step=None): add(eng, cost, reads, writes, fn, step, sem=sem, k=k)

    def ap(a):
        if isinstance(a, (int, float)):
            return lambda T: a
        if isinstance(a, str):
            return lambda T: T[a][:]
        if len(a) == 3:
            return lambda T: T[a[0]][:, a[1]:a[2]]
        if len(a) == 4:
            return lambda T: T[a[0]][:, a[1]:a[2]:a[3]]
        return lambda T: T[a[0]][a[4]:a[5], a[1]:a[2]:a[3]]

    def names(*xs): return [x for x in xs if not isinstance(x, (int, float)) and x is not None]
    def wid(a): return SCRATCH[a][1][1] if isinstance(a, str) else len(range(*a[1:4]))
    def two(*xs): return all(SCRATCH[rng(x)[0]][2] in (BF, F16, U16) for x in xs)
    def cost1(out, in_): return vh(wid(out)) if two(out, in_) else v1(wid(out))

    def copy(out, in_, step=None): V(cost1(out, in_), [in_], [out], lambda q, T: [q.tensor_copy(ap(out)(T), ap(in_)(T))], step)
    def fill(out, x): V(cost1(out, out), [], [out], lambda q, T: [q.memset(ap(out)(T), x)])

    def tt(out, a, b, op, step=None):
        f = 1 if rng(a)[0] in BANKS or rng(b)[0] in BANKS else 2
        V(v1(f * wid(out)), [a, b], [out], lambda q, T: [q.tensor_tensor(ap(out)(T), ap(a)(T), ap(b)(T), op)], step)

    def scan(out, a, b, o0, o1, step):
        V(vh(wid(out) * P.get("sf", 1)) if two(out, a, b) else v1(wid(out) * P.get("sf4", 1)), [a, b], [out], lambda q, T: [q.tensor_tensor_scan(ap(out)(T), ap(a)(T), ap(b)(T), 0.0, o0, o1)], step)

    def ts(out, in0, s1, o1, s2=None, o2=None, step=None):
        V(cost1(out, in0), names(in0, s1, s2), [out],
          lambda q, T: [q.tensor_scalar(ap(out)(T), ap(in0)(T), ap(s1)(T), None, o1) if o2 is None else q.tensor_scalar(ap(out)(T), ap(in0)(T), ap(s1)(T), ap(s2)(T), o1, o2)], step)

    def act(out, in_, f, step=None, **kw):
        S(v1(wid(out)), names(in_, *kw.values()), [out], lambda q, T: [q.activation(ap(out)(T), ap(in_)(T), f, **dict((k, ap(x)(T)) for k, x in kw.items()))], step)

    def mm(terms, step=None, start=True, stop=True, more=(), whole=None):
        cyc_n = sum(max(min(64, wid(a)), wid(b)) * (4 if SCRATCH[rng(a)[0]][2] == F32 else 1) for (o, a, b) in terms)
        outs = [whole] if whole else [o for (o, a, b) in terms]
        add("t", cyc_n * pec, [x for (o, a, b) in terms for x in (a, b)] + list(more) + ([] if start else outs), outs,
            lambda q, T: [q.matmul(ap(o)(T), ap(a)(T), ap(b)(T), start and i == 0, stop and i == len(terms) - 1) for i, (o, a, b) in enumerate(terms)], step, k=len(terms))

    def on_v(step): return step[0] in ON_V or step[0][:-1] in ON_V

    def gather(out, win, off, step, half=False):
        if half and on_v(step):
            V(vg(wid(out)), [win, off], [out], lambda q, T: [q.tensor_scalar(ap(out)(T), ap(win)(T).indirect(ap(off)(T)), 0.5, None, O.mult)], step)
        elif half:
            S(sg(wid(out)), [win, off], [out], lambda q, T: [q.activation(ap(out)(T), ap(win)(T).indirect(ap(off)(T)), AF.Copy, scale=0.5)], step)
        elif on_v(step):
            V(vg(wid(out)), [win, off], [out], lambda q, T: [q.tensor_copy(ap(out)(T), ap(win)(T).indirect(ap(off)(T)))], step)
        else:
            S(sg(wid(out)), [win, off], [out], lambda q, T: [q.activation(ap(out)(T), ap(win)(T).indirect(ap(off)(T)), AF.Copy)], step)

    def gadd(out, win, off, b, step): V(vg(wid(out)), [win, off, b], [out], lambda q, T: [q.tensor_tensor(ap(out)(T), ap(win)(T).indirect(ap(off)(T)), ap(b)(T), O.add)], step)
    def move(out, in_, step): (copy(out, in_, step) if on_v(step) else act(out, in_, AF.Copy, step))
    row = ("ones", 0, 128, 1, 0, 1)

    if TWO:
        dma("y", P["ldx"], [], [("X", 0, 4096)], "ldx", lambda q, T: [q.dma_start(T.X[0:64, :], T.field[0:64, :])])
        dma("s", P["ldx"], [], [("X", 4096, 8192)], "ldy", lambda q, T: [q.dma_start(T.X[64:128, :], T.field[0:64, :])])
        dma("y", 2.5, [], ["TI"], "ldt",
            lambda q, T: [q.dma_start(T.TI[64 * e:64 * e + 64, n * c:n * c + n], T.tube[64 * c:64 * c + 64, n * e:n * e + n]) for c in range(NC) for e in range(2)], 4)
    else:
        dma("y", P["ldx"], [], [("X", 0, 4096)], "ldx", lambda q, T: [q.dma_start(T.X[:, 0:4096], T.field[:, 0:4096])])
        dma("s", P["ldx"], [], [("X", 4096, 8192)], "ldy", lambda q, T: [q.dma_start(T.X[:, 4096:8192], T.field[:, 4096:8192])])
        dma("y", 2.0, [], ["TI"], "ldt", lambda q, T: [q.dma_start(T.TI[:], T.tube[:])])
    dma("y", 2.0, [], ["pri"], "ldp", lambda q, T: [q.dma_start(T.pri[:, 0:1], T.wt[:]), q.dma_start(T.pri[:, 1:2], T.kn[:]), q.dma_start(T.pri[:, 2:7], T.lim[:])], 3)
    fill("ones", 1.0)
    G(0.2, [], ["pI"], lambda q, T: [q.iota(T.pI[:], [[0, 1]], 0, 1)])
    G(0.45, ["ones"], ["IB"], lambda q, T: [q.affine_select(T.IB[:], T.ones[:], [[-1, 128]], O.is_equal, 0.0, 0, 1)])
    G(0.45, ["ones"], ["BO1"], lambda q, T: [q.affine_select(T.BO1[:], T.ones[:], [[-16, 8], [0, 16]], O.is_ge, 0.0, 0, 1)])
    G(0.2, [], ["vbi"], lambda q, T: [q.iota(T.vbi[:], [[16, 16]], 0, 0)])
    G(0.45, ["BO1"], ["BO"], lambda q, T: [q.affine_select(T.BO[:], T.BO1[:], [[16, 8], [0, 16]], O.is_ge, 0.0, 15, -1)])
    G(0.4, [], ["grow"], lambda q, T: [q.iota(T.grow[:], [[16384, 8], [0, 16]], 4096, 0, allow_small_or_imprecise_dtypes=True)])
    G(0.45, ["BO"], ["BOd"], lambda q, T: [q.affine_select(T.BOd[:], T.BO[:], [[-1, 128]], O.is_equal, 0.0, -1, 1)])
    G(0.4, [], ["irow"], lambda q, T: [q.iota(T.irow[:], [[0, 8], [1, 16]], 0, 0, allow_small_or_imprecise_dtypes=True)])
    for c in range(NC):
        G(3.9, [], [("W", 2048 * c, 2048 * c + 2048)], lambda q, T, c=c: [q.iota(T.W[:, 2048 * c:2048 * c + 2048], [[0, 2048]], 0, 0, allow_small_or_imprecise_dtypes=True)])
        if AU[c] < 0:
            G(3.9, [], ["ZS"], lambda q, T: [q.iota(T.ZS[:], [[0, 2048]], 256, 0, allow_small_or_imprecise_dtypes=True)])
    rb = 16 * max(GP[0] + GP[1] + (SP if min(AU) < 0 else []))
    fill("sel", 0.0)
    fill(("RB", 0, rb), 0.0)
    fill("RK", 0.0)
    fill("VW", 0.0)
    ts("iI", "pI", 15, O.bitwise_and)
    fill(("RB", 0, rb, 16), 256.0)
    fill(("RK", 0, 128, 16), 8388608.0)
    copy("icol", "iI")
    fill("mh", -0.5)
    for c in range(NC):
        fill(("KM%d" % c, 128, 144), 8388608.0)
    if 0 in AU:
        add("s", 16 * v1(128), ["IB"], ["Rep"], lambda q, T: [q.activation(T.Rep[:, i:2048:16], T.IB[:], AF.Copy, scale=-0.5) for i in range(16)], k=16)
    act("IF", "IB", AF.Copy)
    ts("ige1", "icol", 1.0, O.is_ge)
    ts("e15", "icol", 15.0, O.is_equal, 128.0, O.mult)
    ts("v0", ("vbi", 0, 8), "icol", O.add)
    if TWO:
        ts("e128", "pI", 64.0, O.is_ge, 128.0, O.mult)
        fill("z2", 0.0)
        for e in range(2):
            copy(("SW", 64 * e, 64 * e + 64), ("IB", 64 - 64 * e, 128 - 64 * e))
        ts(("VS", 0, 8), "v0", "e128", O.add)
        ts(("VS", 8, 16), "v0", "e128", O.subtract, 128.0, O.add)
    else:
        ts("VS", "vbi", "icol", O.add)
    add("v", 8 * tiny, ["BO", "sel"], ["sel"], lambda q, T: [q.tensor_copy(T.sel[:, 16 * h:16 * h + 129 * 15 + 1:129], T.BO[:, 16 * h:16 * h + 16]) for h in range(8)], k=8)
    if TWO:
        copy(("prb", 0, 7), ("pri", 0, 7))
        add("t", 256 * pec, ["prb", "IB"], [("pb1", 0, 16)],
            lambda q, T: [q.matmul(T.pb1[64 * e:64 * e + 64, 8 * c:8 * c + 7], T.IB[:, 64 * c:64 * c + 64], T.prb[:, 0:7], True, True) for c in range(NC) for e in range(2)], k=4)
        copy("L32", "TI")
        for c in range(NC):
            copy(("prm", 8 * c, 8 * c + 7), ("pb1", 8 * c, 8 * c + 7))
    else:
        copy("L32", "TI")
        for c in range(NC):
            copy(("prm", 8 * c, 8 * c + 7), ("pri", 0, 7))
    copy("LU0", "TI")
    ts("wq", ("prm", 0, 16, 8), 1.0 / 4096, O.mult)
    tt("k3", ("prm", 1, 16, 8), ("prm", 1, 16, 8), O.mult)
    copy(("thv", 0, 16, 8), ("prm", 2, 16, 8))
    ts("sqb", ("prm", 1, 16, 8), 2.0, O.mult, 512.0, O.add)
    act(("wsel", 0, 2048), "sel", AF.Copy, scale=("wq", 0, 1))
    act("Sel0", ("sel", 0, 128), AF.Copy)
    if TWO:
        act(("wsel", 2048, 4096), "sel", AF.Copy, ("wselb", 0), scale=("wq", 1, 2))
        dma("y", P["ldx"], ["X"], ["X1"], "ldz", lambda q, T: [q.dma_start(T.X1[64 * e:64 * e + 64, :], T.field[64:128, :]) for e in range(2)], 2, ("ldzb", 0))
    ts("k4", "k3", -4.0, O.mult, -0.25, O.add)
    ts("pth", "ige1", 109.5, O.mult, -101.0, O.add)
    ts("pIm", "IB", "ige1", O.mult)
    ts("S15", "ones", "e15", O.mult)
    ts("VB", "v0", 16.0, O.mult)
    for c in range(NC):
        ts(("VW", 16 * c, 16 * c + 8), "v0", 16 - 1.0 / 128, O.mult)
    ts("nIm", "pIm", -128.0, O.mult)
    copy("BOh", "BO")
    tt("BO1", "IB", "BOd", O.subtract)
    ts("blk32", ("BO", 0, 128, 16), 64.0, O.mult)
    ts("blk16", ("BO", 0, 128, 16), 32.0, O.mult)
    ts("blkn", ("BO", 0, 128, 16), -32.0, O.mult)
    ts("hIB", "IB", 0.5, O.mult)
    ts("OHm", "BO1", 128.0, O.mult)
    ts("grow", "grow", 16.0, O.mult)
    ts("selh", "sel", 128.0, O.mult)

    C24 = 1.5 * 2.0 ** 24
    def blocks(b, lo=0): return [(b, lo + 128 * k, lo + 128 * k + 128) for k in range(16)]
    def cuts(sizes): return [(sum(sizes[:p]), sum(sizes[:p + 1])) for p in range(len(sizes))]

    def zof(c): return ("ZS", 16 * n * c, 16 * n * (c + 1), 16) if AU[c] < 0 else ("Zb", n * c, n * c + n)

    def xof(c): return "X1" if TWO and c else "X"

    def head(t, c):
        LU, dl, pa, pb = "LU%d" % t, "DL%d" % c, "pa%d" % c, "pb%d" % c
        a0, a1, c0, c1 = n * c, n * c + n, 16 * n * c, 16 * n * (c + 1)
        def Q(x, lo=0, hi=n): return (x, a0 + lo, a0 + hi)
        def Wd(x, lo=0, hi=n): return (x, c0 + 16 * lo, c0 + 16 * hi)
        def st(x): return (x + "ab"[c], t)
        if t:
            add("x", P["hop"], [Q("NU%d" % (t - 1))], [Q(LU)], None, st("arr"), sem="arr%d%d" % (t, c))
        def s1(x): return st(x) if t else None
        if t:
            copy(Q("L32"), Q(LU), st("L32"))
        act(Q("LQ"), Q("L32"), AF.Identity, st("LQ"), bias=("k4", c, c + 1))
        dma("y", 2.2, [Q("L32")], [dl], "dl%d" % c, lambda q, T: [q.dma_start(T[dl][:], T.L32[:, a0:a1])], 1, s1("dl"))
        for p, (lo, hi) in enumerate(cuts(WP)):
            dma("y", P.get("lat", 2.0) + P.get("hold", 0.3) * (hi - lo), [dl], [("W", c0 + p, c0 + p + 1)], "w%d%d" % (c, p),
                lambda q, T, lo=lo, hi=hi: [q.dma_start(T.W[j::16, c0 + n * j:c1], T[dl][:, 1:17 - j, :]) for j in range(lo + 1, hi + 1)], hi - lo, st("w%d" % p))
        for p, (lo, hi) in enumerate(cuts(GP[c])):
            gather(Wd("G", lo, hi), xof(c), Q(LU, lo, hi), st("Gp%d" % p))
            scan(Wd("M", lo, hi), ("RB", 0, 16 * (hi - lo)), Wd("G", lo, hi), O.max, O.min, st("Mp%d" % p))
        for k, (lo, hi) in enumerate(cuts([UN[c]] * (n // UN[c]))):
            ends = [lo] + [y for (x, y) in cuts(GP[c]) if lo < y < hi and HP[c][k]] + [hi]
            for p, (l, h) in enumerate(zip(ends, ends[1:])):
                ts(Wd("H", l, h), Wd("M", l, h), ("thv", 8 * c * TWO + t, 8 * c * TWO + t + 1), O.is_ge, step=st("Hp%du%d" % (p, k)))
            sa, cn, g0, g1 = (SAB + "%d" % c, 128 + lo, 128 + hi), (pa, lo, hi), c0 + 16 * lo, c0 + 16 * hi
            mm([(sa, row, ("mh", 0, hi - lo))] + [(sa, w, ("G", g0 + j, g1, 16)) for j, w in enumerate(blocks("wsel", 2048 * c * TWO))], st("sau%d" % k), more=[("G", g0, g1)])
            mm([(cn, w, ("H", g0 + j, g1, 16)) for j, w in enumerate(blocks("sel"))], st("cntu%d" % k))
            ts(("PU", 2 * a0 + lo, 2 * a0 + hi), cn, "pth", O.is_ge, 1.0 / 128, O.mult, st("passu%d" % k))
        for k, (lo, hi) in enumerate(cuts([HU[c]] * (n // HU[c]))):
            sa, f_, u_, q_ = (SAB + "%d" % c, 128 + lo, 128 + hi), (OB + "%d" % c, 256 * (OB == "pa") + lo, 256 * (OB == "pa") + hi), (pb, 128 + lo, 128 + hi), (pb, 256 + lo, 256 + hi)
            pas, uo = ("PU", 2 * a0 + lo, 2 * a0 + hi), ("PU", 2 * a0 + n + lo, 2 * a0 + n + hi)
            ts(Q("KQ", lo, hi), sa, 1.0 / 8192, O.add, step=st("KQu%d" % k))
            tt(Q("UA", lo, hi), sa, Q("KQ", lo, hi), O.subtract, st("UAu%d" % k))
            mm([(f_, "OHm", pas)], st("onehu%d" % k))
            tt(uo, f_, Q("UA", lo, hi), O.mult, st("UOu%d" % k))
            mm([(u_, "BOh", uo)], st("uu%d" % k))
            act(q_, u_, AF.Square, st("SQu%d" % k), bias=("sqb", c, c + 1), scale=1024.0)
            tt(Q("xI", lo, hi), q_, Q("LQ", lo, hi), O.add, st("xu%d" % k))
            ts(Q("cI", lo, hi), Q("xI", lo, hi), 8191, O.bitwise_and, step=st("andu%d" % k))
            copy(Q("CU", lo, hi), Q("cI", lo, hi), st("CUu%d" % k))
        both, nbt = ("pc%d" % (c * TWO), 256 + 16 * c, 272 + 16 * c), ("pc%d" % (c * TWO), 256 + 16 * c, 264 + 16 * c)
        if NBS[c]:
            mm([(nbt, w, ("PU", 2 * a0 + k, 2 * a0 + n, 16)) for k, w in enumerate(blocks("selh"))] + [(nbt, "IB", "VB")], st("nb"))
            if t < RO - 1:
                mm([((both[0], both[1] + 8, both[2]), w, ("PU", 2 * a0 + n + k, 2 * a1, 16)) for k, w in enumerate(blocks("selh"))], st("uT"))
        else:
            mm([(both, w, ("PU", 2 * a0 + k, 2 * a1, 16)) for k, w in enumerate(blocks("selh"))] + [(nbt, "IB", "VB")], st("nb"))
        ts(("OM", 8 * c, 8 * c + 8), nbt, -1.0, O.add, step=st("OM"))
        gather(zof(c), Wd("M"), ("OM", 8 * c, 8 * c + 8), st("Z"))
        zt = ("pc%d" % c, 288, 288 + n)
        if AU[c] < 0:
            pass
        elif AU[c]:
            mm([((pb, 0, n), "hIB", Q("Zb"))], st("Zp"))
        else:
            mm([(zt, Q("Zb"), "IB")], st("Zp"))
            move(Q("ZT"), zt, st("ZT"))
        mm([(("pc%d" % c, 0, n), "pIm", "ones"), (("pc%d" % c, 0, n), "nIm", ("PU", 2 * a0, 2 * a0 + n))], st("np"))

    def middle2(t, c):
        pc, lo, x = "pc%d" % c, 16 * c, "ab"[c]
        tt(("nw", lo, lo + 8), (pc, 256 + lo, 264 + lo), ("VW", lo, lo + 8), O.subtract, ("nw" + x, t))
        ts(("OW", lo, lo + 8), ("nw", lo, lo + 8), 128.0, O.mult, -128.0, O.add, ("OW" + x, t))
        if t < RO - 1:
            ut, k2, rr, so = (pc, 264 + lo, 272 + lo), ("k2", lo, lo + 8), ("rr", lo, lo + 8), (pc, 416, 432)
            ts(k2, ut, -31.0 / 64, O.add, step=("k2" + x, t))
            tt(rr, ut, k2, O.subtract, ("rr" + x, t))
            mm([(so, "IB", "VS"), ((pc, 416, 424), "IB", rr), ((pc, 424, 432), "SW", rr)], ("so" + x, t), whole=so)
            ts(("SO", lo, lo + 16), so, 32.0, O.mult, step=("SO" + x, t))

    def middle(t):
        if TWO:
            return [middle2(t, c) for c in range(NC)]
        nb = ("pc0", 256, 288)
        tt("nw", nb, "VW", O.subtract, ("nwb", t))
        ts("OW", "nw", 128.0, O.mult, -128.0, O.add, ("OWb", t))
        if t < RO - 1:
            ts("k2", nb, -31.0 / 64, O.add, step=("k2b", t))
            tt("rr", nb, "k2", O.subtract, ("rrb", t))

    def tail(t, c):
        last = t == RO - 1
        NU, pc, pk = "NU%d" % t, "pc%d" % c, "pk%d" % c
        a0, a1, c0, c1, h0, h1 = n * c, n * c + n, 16 * n * c, 16 * n * (c + 1), 8 * c, 8 * c + 8
        def Q(x, lo=0, hi=n): return (x, a0 + lo, a0 + hi)
        def Wd(x, lo=0, hi=n): return (x, c0 + 16 * lo, c0 + 16 * hi)
        def st(x): return (x + "ab"[c], t)
        key = (pk, 0, 128)
        mm([(key, row, "irow"), (key, row, "grow")], st("keyc"), stop=False, whole=(pk, 0, 512))
        for p, (lo, hi) in enumerate(cuts(DP[c])):
            gather(Wd("D", lo, hi), xof(c), Q("CU", lo, hi), st("Dp%d" % p), True)
        if AU[c] < 0:
            for k, (lo, hi) in enumerate(cuts(SP)):
                d16, z16, sv = Wd("D", lo, hi) + (16,), Wd("ZS", lo, hi) + (16,), Q("sv", lo, hi)
                scan(Wd("Zx", lo, hi), ("RB", 0, 16 * (hi - lo)), Wd("ZS", lo, hi), O.max, O.min, st("Zx%d" % k))
                act(sv, d16, AF.Copy, st("sv%d" % k))
                tt(d16, sv, z16, O.max, st("fx%d" % k))
                scan(Wd("A", lo, hi), Wd("Zx", lo, hi), Wd("D", lo, hi), O.min, O.max, st("A%d" % k))
                act(d16, sv, AF.Copy, st("rs%d" % k))
            for p, (lo, hi) in enumerate(cuts(KP[c])):
                add("t", 16 * max(8, min(64, hi - lo)) * pec, [Q("sv", lo, hi), "blkn", key], [key],
                    lambda q, T, lo=lo, hi=hi: [q.matmul(T[pk][lo:hi, i:128:16], T.D[:, c0 + 16 * lo + i:c0 + 16 * hi:16] if i else T.sv[:, a0 + lo:a0 + hi], T.blkn[:], False, False) for i in range(16)],
                    st("kl%d" % p), k=16)
            for p, (lo, hi) in enumerate(cuts(KP[c])):
                mm([((pk, i, 128, 16, lo, hi), ("A", c0 + 16 * lo + i, c0 + 16 * hi, 16), "blk32") for i in range(16)], st("key%d" % p), False, True, [Wd("A", lo, hi)], key)
        elif AU[c]:
            for k, (lo, hi) in enumerate(cuts([AU[c]] * (n // AU[c]))):
                for i0 in range(0, 16, KG):
                    zk = ("pb%d" % c, lo, hi)
                    io = [(("A", c0 + n * i + lo, c0 + n * i + hi), ("D", c0 + 16 * lo + i, c0 + 16 * hi, 16)) for i in range(i0, i0 + KG)]
                    add("v", KG * v1(hi - lo), [Wd("D", lo, hi), zk], [o for (o, d) in io],
                        lambda q, T, io=io, zk=zk: [q.tensor_tensor(ap(o)(T), ap(d)(T), ap(zk)(T), O.max) for (o, d) in io], st("Au%di%d" % (k, i0)), k=KG)
            mm([((pk, i, 128, 16), ("D", c0 + i, c1, 16), "blkn") for i in range(16)], st("kl"), False, False, [Wd("D")], key)
            for i0 in range(0, 16, KG):
                mm([((pk, i, 128, 16), ("A", c0 + n * i, c0 + n * i + n), "blk32") for i in range(i0, i0 + KG)], st("key%d" % i0), False, i0 + KG == 16, [], key)
        for p, (lo, hi) in enumerate(cuts(DP[c]) if not AU[c] else []):
            df = (DB[c][p % len(DB[c])], 0, 16 * (hi - lo))
            mm([(df, Q("ZT"), ("Rep", 16 * lo, 16 * hi))], st("dz%d" % p), stop=False, whole=(df[0], 0, 512))
            mm([(df, "IB", Wd("D", lo, hi))], st("dx%d" % p), start=False)
            if on_v(st("A%d" % p)):
                ts(Wd("A", lo, hi), df, 0.0, O.max, 2.0, O.mult, st("A%d" % p))
                mm([((pk, i, 128, 16, lo, hi), ("D", c0 + 16 * lo + i, c0 + 16 * hi, 16), "blkn") for i in range(16)], st("kl%d" % p), False, False, [Wd("D", lo, hi)], key)
            else:
                act(Wd("A", lo, hi), df, AF.Abs, st("A%d" % p))
        for p, (lo, hi) in enumerate(cuts(KP[c]) if not AU[c] else []):
            mm([((pk, i, 128, 16, lo, hi), ("A", c0 + 16 * lo + i, c0 + 16 * hi, 16), "blk16") for i in range(16)], st("key%d" % p), False, True, [Wd("A", lo, hi)], key)
        KM, KB, OH = "KM%d" % c, "KB%d" % c, "OH%d" % c
        scan((KM, 0, 128), "RK", key, O.max, O.min, st("KM"))
        scan(KB, "RK", (KM, 15, 143), O.max, O.min, st("KB"))
        tt(OH, key, KB, O.is_equal, st("OH"))
        oh, np_, nl_ = (pk, 128, 128 + n), (pc, 0, n), (pc, 128, 128 + n)
        mm([(oh, OH, "IB")], st("oh"))
        if not last:
            o2, tot, ot = oh, (pk, 256, 264), ("OT", h0, h1)
            if OH2[c]:
                o2, tot = (OH2[c], 0, n), (OH2[c], 128, 136)
                mm([(o2, OH, "IB")], st("o2"))
            if on_v(st("OHA")):
                ts(Q("OHA"), o2, "icol", O.mult, step=st("OHA"))
            else:
                act(Q("OHA"), o2, AF.Copy, st("OHA"), scale="icol")
            mm([(tot, "IB", "VB")] + [(tot, w, ("OHA", a0 + k, a1, 16)) for k, w in enumerate(blocks("sel"))], st("to"))
            copy(ot, tot, st("OT"))
            if TWO:
                yb = "pa%d" % c
                yp, own, oth = (yb, 256, 512), (yb, 256, 384), (yb, 384, 512)
                mm([(yp, row, "mh"), (own, "IB", zof(c)), (oth, "SW", zof(c))], st("yp0"), stop=False, more=[(yb, 0, 256)], whole=yp)
                gather(Q("XB"), Wd("D"), ot, st("tt"))
                mm([(own, "IB", Q("XB")), (oth, "SW", Q("XB"))], st("yp1"), start=False, whole=yp)
                ts(("Y2", 2 * a0, 2 * a1), yp, C24, O.add, -C24, O.add, st("Y2"))
            elif on_v(st("tt")):
                act(Q("Z2"), zof(c), AF.Copy, st("Z2"), bias=-0.25, scale=0.5)
                gadd(Q("tt"), Wd("D"), ot, Q("Z2"), st("tt"))
                yp = Q("tt")
            else:
                yp = (pk, 264, 264 + n)
                gather(Q("XB"), Wd("D"), ot, st("tt"))
                mm([(yp, row, ("mh", 0, n)), (yp, "IB", zof(c)), (yp, "IB", Q("XB"))], st("yp"))

        tt(Q("C1"), np_, Q("cI"), O.mult, st("C1"))
        tt(Q("OC"), oh, Q("cI"), O.mult, st("OC"))
        ow = ("OW", 16 * c, 16 * c + 8)
        if on_v(st("RC")):
            gadd(Q("RC"), Wd("W"), ow, Q("C1"), st("RC"))
            mm([(nl_, "IF", Q("RC"))], st("nl0"), stop=False, more=[(pc, 256, 512)])
        else:
            gather(Q("RC"), Wd("W"), ow, st("RC"))
            mm([(nl_, "IF", Q("C1")), (nl_, "IF", Q("RC"))], st("nl0"), stop=False, more=[(pc, 256, 512)])
        mm([(nl_, "Sel0", Q("OC"))], st("nl1"), start=False, more=[(pc, 256, 512)])
        if not last:
            copy(Q(NU), nl_, st("NU"))
            add("g", 0.5, [Q(NU)], [], ("send", t, c), st("send"), sem="sent")
        else:
            act(Q("yls"), nl_, AF.Copy, st("yls"))
            def out(y, s): return lambda q, T: ([q.dma_start(T[y][64 * c:64 * c + 64, n * e:n * e + n], T[s][64 * e:64 * e + 64, a0:a1]) for e in range(2)] if TWO else
                                                [q.dma_start(T[y][:, a0:a1], T[s][:, a0:a1])])
            dma("y", 2.0, [Q("yls")], [], "ol%d" % c, out("yl", "yls"), 1 + TWO, st("ol"))
            act(Q("yzs"), zof(c), AF.Copy, st("yzs"))
            dma("y", 2.0, [Q("yzs")], [], "oz%d" % c, out("yz", "yzs"), 1 + TWO, st("oz"))

    def close(t):
        so, eb = (SB, 416, 432), (SB, 448, 512)
        if not TWO:
            mm([(so, "IB", "VS")] + [((SB, 416 + 8 * c, 424 + 8 * c), "IB", ("rr", 16 * c + 8, 16 * c + 16)) for c in range(NC)], ("sob", t), whole=so)
            ts(("SO", 0, 16), so, 32.0, O.mult, step=("SOb", t))
        mm([(eb, "S15", ("PU", 2 * n * c + k, 2 * n * c + k + 64)) for c in range(NC) for k in (0, 64)], ("Eb", t))
        V(tiny, [eb], ["er"], lambda q, T: [q.tensor_reduce(T.er[:], ap(eb)(T), AxisListType.X, O.add, negate=True)], ("erb", t))
        if TWO:
            ts("eI", "z2", "er", O.add, step=("eIb", t))
            ts("eJ", "eI", 7, O.bitwise_and, step=("eJb", t))
            V(tiny, ["eJ", "prm"], [("thv", t + 1, t + 2), ("thv", t + 9, t + 10)],
              lambda q, T: [q.tensor_tensor(T.thv[:, t + 1:16:8], T.prm[:, t + 3:16:8], T.eJ[:], O.add)], ("thvb", t))
            return
        copy(("eI", 0, 1), "er", ("eIb", t))
        ts(("eJ", 0, 1), ("eI", 0, 1), 7, O.bitwise_and, step=("eJb", t))
        tt(("thv", t + 1, t + 2), ("prm", 3 + t, 4 + t), ("eJ", 0, 1), O.add, ("thvb", t))

    def scatter(t, c):
        m = n * (1 + TWO)
        y2, so = ("tt", m * c, m * c + m), ("SO", m // 16 * c, m // 16 * (c + 1))
        V(0.055 + P["sc"] * m * cyc, [y2, so], [xof(c)],
          lambda q, T: [q.tensor_copy(T[xof(c)][:].indirect(ap(so)(T)), ap(y2)(T))], ("scat" + "ab"[c], t))

    for t in range(RO):
        for c in range(NC):
            head(t, c)
        middle(t)
        if t < RO - 1:
            close(t)
        for c in range(NC):
            tail(t, c)
        for c in range(NC if t < RO - 1 else 0):
            scatter(t, c)
    return ops


def deps_of(ops):
    acc = {}
    for o in ops:
        d = set()
        for (b, lo, hi) in o["reads"]:
            for (p, l2, h2, w) in acc.get(b, []):
                if w and l2 < hi and lo < h2:
                    d.add((p, "raw"))
        for (b, lo, hi) in o["writes"]:
            for (p, l2, h2, w) in acc.get(b, []):
                if l2 < hi and lo < h2:
                    d.add((p, "waw" if w else "war"))
        for (b, lo, hi) in o["writes"]:
            acc[b] = [a for a in acc.get(b, []) if not (lo <= a[1] and a[2] <= hi)] + [(o["id"], lo, hi, True)]
        for (b, lo, hi) in o["reads"]:
            acc.setdefault(b, []).append((o["id"], lo, hi, False))
        o["deps"] = sorted((p, k) for (p, k) in d if p != o["id"])
        o["banks"] = sorted(set(b for (b, lo, hi) in o["reads"] + o["writes"] if b in BANKS))
    return ops


def step_of(o):
    return o["step"]


def order_of(ops, place, period):
    n = len(ops)
    succ, left = [[] for _ in ops], [0] * n
    for o in ops:
        ps = set(p for (p, k) in o["deps"])
        left[o["id"]] = len(ps)
        for p in ps:
            succ[p].append(o["id"])
    key = [place[o["step"][0]] + o["step"][1] * period if o["step"] else o["id"] - 10000 for o in ops]
    order, held = [], {}
    for i in sorted(range(n), key=lambda j: (key[j], j)):
        stack = [i]
        if left[i]:
            held[i] = True
            continue
        while stack:
            j = stack.pop()
            order.append(j)
            free = []
            for s in succ[j]:
                left[s] -= 1
                if left[s] == 0 and s in held:
                    free.append(s)
            stack += sorted(free, key=lambda x: -key[x])
    return order


def places():
    w = CYCLE.split()
    return {x.lstrip("+-"): (k / len(w) + {"+": 1, "-": -1}.get(x[0], 0)) * PERIOD for k, x in enumerate(w)}


def rank_program(g, core, T, topo):
    rank = T.rank_of(core)
    if rank is None:
        return
    cores = T.cores
    dst = cores[(rank + 1) % len(cores)]
    rid, pid, _ = topo.addr(dst)
    mask = topo.mask(core, dst)
    ne = len(topo.engines(core, dst))
    ni = len(topo.engines(cores[(rank - 1) % len(cores)], core))
    ops = deps_of(build())
    order = order_of(ops, places(), PERIOD)
    queues = {"v": g.vector, "s": g.scalar, "t": g.tensor, "g": g, "y": g.sync}
    csem = {"v": "cv", "s": "cs", "t": "ct", "g": "cg"}
    total = {}
    token = {}
    after = {}
    know = {e: {} for e in queues}
    lastbank = {}
    for i in order:
        o = ops[i]
        e = o["eng"]
        if e == "x":
            token[i] = (o["sem"], ni)
            total[o["sem"]] = ni
            after[i] = {}
            continue
        q = queues[e]
        need = {}
        ds = [p for (p, k) in o["deps"] if not (k == "war" and ops[p]["eng"] == e and token[p][0] == csem.get(e))]
        if e == "t":
            ds = [p for p in ds if ops[p]["eng"] != "t"]
        for b in o["banks"]:
            for e2, p in lastbank.get(b, {}).items():
                if e2 != e:
                    ds.append(p)
        inherit = []
        for p in ds:
            s, v = token[p]
            if know[e].get(s, 0) < v:
                need[s] = max(need.get(s, 0), v)
                inherit.append(p)
        for s in sorted(need):
            if any(after[p].get(s, 0) >= need[s] and token[p][0] != s for p in inherit):
                continue
            q.wait_ge(T.sem[s], int(need[s]))
        for p in inherit:
            s, v = token[p]
            for s2, v2 in list(after[p].items()) + [(s, v)]:
                if know[e].get(s2, 0) < v2:
                    know[e][s2] = v2
        after[i] = dict(know[e])
        if isinstance(o["fn"], tuple):
            t, c = o["fn"][1:]
            there, here = send_sides(o["fn"], T)
            g.remote_dma(there, here, T.sem["arr%d%d" % (t + 1, c)], T.sem["sent"], pid, rid, mask)
            total["sent"] = total.get("sent", 0) + ne
            token[i] = ("sent", total["sent"])
        else:
            ins = o["fn"](q, T)
            s, k = (o["sem"], 16) if o["sem"] else (csem[e], 1)
            for x in ins:
                x.then_inc(T.sem[s], k)
            total[s] = total.get(s, 0) + k * len(ins)
            token[i] = (s, total[s])
        for b in o["banks"]:
            lastbank.setdefault(b, {})[e] = i
    for s in sorted(total):
        g.wait_ge(T.sem[s], int(total[s]))
